import numpy as np
import ml_dtypes


def mxq(x, axis, fmt="e4m3"):
    dtype, down = {"e4m3": (ml_dtypes.float8_e4m3fn, 7), "e5m2": (ml_dtypes.float8_e5m2, 14)}[fmt]
    v = np.moveaxis(np.asarray(x, np.float32).astype(ml_dtypes.bfloat16).astype(np.float64), axis, -1)
    blocks = v.reshape(v.shape[:-1] + (-1, 32))
    amax = np.abs(blocks).max(-1, keepdims=True)
    byte = np.maximum(np.where(amax > 0, np.frexp(amax)[1] - 1 + 127, 0) - down, 1)
    scale = np.exp2(byte - 127.0)
    codes = (blocks / scale).astype(np.float32).astype(dtype).astype(np.float64)
    return np.moveaxis((codes * scale).reshape(v.shape), -1, axis)


WIDE = False


def mx_kscale(k):
    if not WIDE:
        return np.ones(k)
    levels = np.array([10, -10, 5, -5, 0])
    if k % 512:
        return np.exp2(np.random.permutation(np.resize(levels, k // 32))).repeat(32)
    a = np.empty((k // 512, 16))
    for p in range(k // 512):
        a[p, :8] = np.random.permutation(np.resize(levels, 8))
        for g in range(8):
            far = levels[np.abs(levels - a[p, g]) >= 10]
            a[p, g + 8] = far[np.random.randint(len(far))]
    return np.exp2(a.ravel()).repeat(32)


def f64(x):
    return np.asarray(x).astype(np.float64)


def striped(idx):
    return np.tile(idx.reshape(-1, 16).T, (8, 1)).astype(np.uint16)


def unstriped(offs):
    return offs[:16].T.reshape(-1).astype(np.int64)


E2M1 = np.array([0.0, 0.5, 1.0, 1.5, 2.0, 3.0, 4.0, 6.0, -0.0, -0.5, -1.0, -1.5, -2.0, -3.0, -4.0, -6.0])


def pack_weight(w, fmt):
    k, n = w.shape
    w = f64(np.asarray(w, np.float32).astype(ml_dtypes.bfloat16)).reshape(k // 32, 32, n)
    amax = np.abs(w).max(1)
    if fmt == "e4m3":
        byte = np.frexp(amax)[1] - 1 + 127 - 7
    else:
        mant, ex = np.frexp(amax / 6.0)
        byte = np.where(mant > 0.5, ex, ex - 1) + 127
    byte = np.clip(np.where(amax > 0, byte, 1), 1, 254)
    scaled = (w * np.exp2(127.0 - byte)[:, None, :]).reshape(k, n).astype(np.float32)
    by_word = np.ascontiguousarray(scaled.reshape(k // 512, 128, 4, n).transpose(0, 1, 3, 2))
    if fmt == "e4m3":
        words = by_word.astype(ml_dtypes.float8_e4m3fn).view(np.uint8)
    else:
        c = by_word.astype(ml_dtypes.float4_e2m1fn).view(np.uint8) & 0xF
        words = (c[..., 0::2] | (c[..., 1::2] << 4)).reshape(k // 512, 128, 2 * n)
    return np.ascontiguousarray(words), np.ascontiguousarray(byte.astype(np.uint8).reshape(k // 512, 16, n))


def unpack_weight(words, scales, fmt):
    g, _, n = scales.shape
    words = np.ascontiguousarray(words).reshape(g, 128, n, -1)
    if fmt == "e4m3":
        vals = words.view(ml_dtypes.float8_e4m3fn).astype(np.float64)
    else:
        nib = np.empty((g, 128, n, 4), np.uint8)
        nib[..., 0::2] = words & 0xF
        nib[..., 1::2] = words >> 4
        vals = E2M1[nib]
    vals = vals * np.repeat(np.exp2(scales.astype(np.float64) - 127.0), 8, axis=1)[..., None]
    return vals.transpose(0, 1, 3, 2).reshape(g * 512, n)


def gelu(v):
    return 0.5 * v * (1.0 + np.tanh(np.sqrt(2.0 / np.pi) * (v + 0.044715 * v**3)))


K, T, S, P, H, N = 1024, 2048, 1024, 512, 1024, 512

def setup_inputs():
    n = np.random.standard_normal
    s = mx_kscale(K)[:, None]
    u = mx_kscale(H)[:, None]
    tab_words, tab_scales = pack_weight(n((K, T)) * s, "e4m3")
    w2_words, w2_scales = pack_weight(1.2 * n((H, N)) / np.sqrt(H) / u, "e2m1")
    return {
        "tab_words": tab_words,
        "tab_scales": tab_scales,
        "offs": striped(np.random.permutation(T)[:S]),
        "pos1": striped(np.random.permutation(S)[:P]),
        "pos2": striped(np.random.permutation(S)[:P]),
        "w1": (n((K, H)) / np.sqrt(K) / s).astype(np.float32),
        "gain": (np.exp(0.3 * n(H)) * u[:, 0]).astype(np.float32),
        "w2_words": w2_words,
        "w2_scales": w2_scales,
    }

def reference(tab_words, tab_scales, offs, pos1, pos2, w1, gain, w2_words, w2_scales):
    v = unpack_weight(tab_words, tab_scales, "e4m3")[:, unstriped(offs)]
    w1q = mxq(f64(w1), 0, "e4m3")
    w2 = unpack_weight(w2_words, w2_scales, "e2m1")
    h = w1q.T @ v
    a = h[:, unstriped(pos1)]
    b = h[:, unstriped(pos2)]
    z = f64(gain)[:, None] * (a - 1.5 * b) / (1.0 + np.abs(b))
    zq = mxq(z, 0, "e4m3")
    return np.tanh(w2.T @ zq)

@@ -1,0 +1,279 @@
+from contextlib import ExitStack
+
+import concourse.mybir as mybir
+
+K, T, S, NP, H, N = 1024, 2048, 1024, 512, 1024, 512
+FLOPS = 2 * K * H * S + 2 * H * N * NP
+
+F32 = mybir.dt.float32
+BF16 = mybir.dt.bfloat16
+I32 = mybir.dt.int32
+U32 = mybir.dt.uint32
+U16 = mybir.dt.uint16
+U8 = mybir.dt.uint8
+FP8X4 = mybir.dt.float8_e4m3fn_x4
+FP4X4 = mybir.dt.float4_e2m1fn_x4
+ACT = mybir.ActivationFunctionType
+ALU = mybir.AluOpType
+
+P = 128
+CH = 128
+
+
+def tile_list_pair_spread_positions_kernel(
+    tc, tab_words, tab_scales, offs, pos1, pos2, w1, gain, w2_words, w2_scales, out
+):
+    nc = tc.nc
+    with ExitStack() as ctx:
+        keep = ctx.enter_context(tc.tile_pool(name="keep", bufs=1))
+        psum = ctx.enter_context(tc.psum_pool(name="psum", bufs=1))
+
+        def sb(name, shape, dtype, tag=""):
+            return keep.tile(shape, dtype, name=name, tag=tag or name, align_bytes=64)
+
+        def bank(i):
+            return psum.tile([P, 512], F32, name="bank%d" % i)
+
+        offs_t = keep.tile([P, S // 16], U16, name="offs_t")
+        pos1_t = keep.tile([P, NP // 16], U16, name="pos1_t")
+        pos2_t = keep.tile([P, NP // 16], U16, name="pos2_t")
+        tabw = [sb("tabw%d" % a, [P, T], I32) for a in range(2)]
+        tabs = sb("tabs", [P, T // 4], I32)
+        w2w = sb("w2w", [P, 2, N // 2], I32)
+        w2s = sb("w2s", [P, 2, N // 4], I32)
+        g = sb("g", [P, 2, 4], F32)
+        g15 = sb("g15", [P, 2, 4], F32)
+        ones = sb("ones", [P, NP], F32)
+        warm = sb("warm", [P, 1], F32)
+        raw = {(a, b): sb("raw%d%d" % (a, b), [P, 4, 512], F32) for a in range(2) for b in range(2)}
+
+        nc.vector.memset(tabs[:], 0)
+        nc.vector.memset(ones[:], 1.0)
+        nc.vector.memset(w2s[:], 0)
+        nc.scalar.activation(warm[:], ones[:, 0:1], ACT.Abs_reciprocal_sqrt)
+
+        def load_tab(a):
+            nc.sync.dma_start(tabw[a][:], tab_words[a].rearrange("p t i -> p (t i)").bitcast(I32))
+
+        def load_w1(a, b):
+            src = w1[512 * a : 512 * (a + 1), 512 * b : 512 * (b + 1)]
+            nc.sync.dma_start(raw[a, b][:], src.rearrange("(p j) c -> p j c", j=4))
+
+        nc.sync.dma_start(offs_t[:], offs)
+        for q in range(4):
+            nc.sync.dma_start(tabs[32 * q : 32 * q + 8, :], tab_scales[:, 4 * q : 4 * q + 4, :].bitcast(I32))
+        load_tab(0)
+        nc.sync.dma_start(g[:], gain.rearrange("(b p t) -> p b t", b=2, t=4))
+        load_w1(0, 0)
+        load_tab(1)
+        load_w1(1, 0)
+        nc.sync.dma_start(pos1_t[:], pos1)
+        nc.sync.dma_start(pos2_t[:], pos2)
+        load_w1(0, 1)
+        load_w1(1, 1)
+        nc.sync.dma_start(w2w[:], w2_words.rearrange("a p c -> p a c").bitcast(I32))
+        for q in range(4):
+            nc.sync.dma_start(
+                w2s[32 * q : 32 * q + 4, :, :],
+                w2_scales[:, 4 * q : 4 * q + 4, :].rearrange("a r n -> r a n").bitcast(I32),
+            )
+
+        gb = [sb("gb%d" % u, [P, NP], F32) for u in range(8)]
+        nc.vector.tensor_scalar(g15[:], g[:], -1.5, None, ALU.mult)
+
+        vw = [sb("vw%d" % a, [P, S], U32) for a in range(2)]
+        vs = sb("vs", [P, S], U8)
+        nc.vector.tensor_copy(vs[:], tabs[:].bitcast(U8).indirect(offs_t[:]))
+        nc.vector.tensor_copy(vw[0][:], tabw[0][:].bitcast(U32).indirect(offs_t[:]))
+
+        grp, wc, ws = {}, {}, {}
+
+        def cast(a, b, t0, nt, on_vector=False, reuse=""):
+            grp[a, b, t0] = sb("grp%d%d%d" % (a, b, t0), [P, nt, P, 4], BF16, reuse)
+            dst = grp[a, b, t0][:].rearrange("p t m j -> p m j t")
+            src = raw[a, b][:].rearrange("p j (m t) -> p m j t", t=4)[:, :, :, t0 : t0 + nt]
+            if on_vector:
+                nc.vector.tensor_copy(dst, src)
+            else:
+                nc.scalar.copy(dst, src)
+
+        def quant_w(a, b, t0, nt):
+            codes = sb("wc%d%d%d" % (a, b, t0), [P, nt * P], U32)
+            scales = sb("ws%d%d%d" % (a, b, t0), [P, nt * P], U8)
+            nc.vector.quantize_mx(
+                out=codes[:].bitcast(FP8X4),
+                scales=scales[:],
+                in_=grp[a, b, t0][:].rearrange("p t m j -> p (t m j)"),
+            )
+            for t in range(nt):
+                wc[a, b, t0 + t] = codes[:, P * t : P * (t + 1)]
+                ws[a, b, t0 + t] = scales[:, P * t : P * (t + 1)]
+
+        hps = {}
+
+        def mm1(u, a):
+            b, t = divmod(u, 4)
+            for half in range(2):
+                if a == 0:
+                    hps[u, half] = bank(2 * t + half)
+                span = slice(512 * half, 512 * (half + 1))
+                nc.tensor.matmul_mx(
+                    out=hps[u, half][:],
+                    lhsT=wc[a, b, t].bitcast(FP8X4),
+                    lhsT_scale=ws[a, b, t],
+                    rhs=vw[a][:, span].bitcast(FP8X4),
+                    rhs_scale=vs[4 * a :, span],
+                    start=(a == 0),
+                    stop=(a == 1),
+                )
+
+        h = [sb("h%d" % u, [P, S], F32) for u in range(8)]
+
+        def evac(u, shared=False):
+            nc.scalar.copy(h[u][:, 0:512], hps[u, 0][:])
+            if shared:
+                nc.vector.tensor_copy(h[u][:, 512:1024], hps[u, 1][:])
+            else:
+                nc.scalar.copy(h[u][:, 512:1024], hps[u, 1][:])
+
+        leg1 = {}
+        leg2 = [sb("leg2_%d" % u, [P, NP], F32) for u in range(8)]
+        num = [sb("num%d" % b, [P, 4, NP], F32) for b in range(2)]
+        rec = [sb("rec%d" % b, [P, 4, NP], F32) for b in range(2)]
+        tmp = ctx.enter_context(tc.tile_pool(name="tmp", bufs=2))
+
+        def picks(u):
+            nc.vector.tensor_copy(leg2[u][:], h[u][:].indirect(pos2_t[:]))
+            leg1[u] = tmp.tile([P, NP], F32, name="leg1", bufs=3)
+            nc.vector.tensor_tensor(leg1[u][:], h[u][:].indirect(pos1_t[:]), gb[u][:], ALU.mult)
+
+        def numer(u):
+            b, t = divmod(u, 4)
+            nc.vector.scalar_tensor_tensor(
+                num[b][:, t, :], leg2[u][:], g15[:, b, t : t + 1], leg1[u][:], ALU.mult, ALU.add
+            )
+
+        def recip(u):
+            b, t = divmod(u, 4)
+            mag = tmp.tile([P, NP], F32, name="mag")
+            root = tmp.tile([P, NP], F32, name="root")
+            nc.scalar.activation(mag[:], leg2[u][:], ACT.Abs)
+            nc.scalar.activation(root[:], mag[:], ACT.Abs_reciprocal_sqrt, bias=1.0)
+            nc.scalar.activation(rec[b][:, t, :], root[:], ACT.Square)
+
+        zb, zc, zs = {}, {}, {}
+
+        def make_z(b, c0, w):
+            zb[b, c0] = sb("zb%d_%d" % (b, c0), [P, w, 4], BF16)
+            nc.vector.tensor_tensor(
+                zb[b, c0][:].rearrange("p (c i) t -> p c t i", i=4),
+                num[b][:, :, c0 : c0 + w].rearrange("p t (c i) -> p c t i", i=4),
+                rec[b][:, :, c0 : c0 + w].rearrange("p t (c i) -> p c t i", i=4),
+                ALU.mult,
+            )
+
+        def quant_z(b, c0, w):
+            codes = sb("zc%d_%d" % (b, c0), [P, w], U32)
+            scales = sb("zs%d_%d" % (b, c0), [P, w], U8)
+            nc.vector.quantize_mx(
+                out=codes[:].bitcast(FP8X4), scales=scales[:], in_=zb[b, c0][:].rearrange("p c t -> p (c t)")
+            )
+            for c in range(c0, c0 + w, CH):
+                zc[b, c] = codes[:, c - c0 : c - c0 + CH]
+                zs[b, c] = scales[:, c - c0 : c - c0 + CH]
+
+        w2b = w2w[:].rearrange("p a c -> p (a c)").bitcast(U8)
+        w2sb = w2s[:].rearrange("p a c -> p (a c)").bitcast(U8)
+
+        def mm2(dst, nt, c, b):
+            nc.tensor.matmul_mx(
+                out=dst,
+                lhsT=w2b[:, 2 * N * b + 2 * P * nt : 2 * N * b + 2 * P * (nt + 1)].bitcast(FP4X4),
+                lhsT_scale=w2sb[:, N * b + P * nt : N * b + P * (nt + 1)],
+                rhs=zc[b, c].bitcast(FP8X4),
+                rhs_scale=zs[b, c],
+                start=(b == 0),
+                stop=(b == 1),
+            )
+
+        out_v = out.rearrange("(nt p) j -> p nt j", p=P)
+
+        def finish(c, first_bank):
+            acc = bank(first_bank)
+            for nt in range(4):
+                for b in range(2):
+                    mm2(acc[:, CH * nt : CH * (nt + 1)], nt, c, b)
+            res = sb("res%d" % c, [P, 4, CH], F32)
+            nc.scalar.activation(res[:].rearrange("p nt j -> p (nt j)"), acc[:], ACT.Tanh)
+            nc.sync.dma_start(out_v[:, :, c : c + CH], res[:])
+
+        def finish_last(c):
+            res = sb("res%d" % c, [P, 4, CH], F32)
+            accs = [bank(4 + nt) for nt in range(4)]
+            for nt in range(4):
+                mm2(accs[nt][:, 0:CH], nt, c, 0)
+            for nt in range(4):
+                mm2(accs[nt][:, 0:CH], nt, c, 1)
+                nc.scalar.activation(res[:, nt, :], accs[nt][:, 0:CH], ACT.Tanh)
+                if nt % 2 == 1:
+                    nc.sync.dma_start(out_v[:, nt - 1 : nt + 1, c : c + CH], res[:, nt - 1 : nt + 1, :])
+
+        cast(0, 0, 0, 2)
+        cast(0, 0, 2, 2)
+        quant_w(0, 0, 0, 2)
+        quant_w(0, 0, 2, 2)
+        for u in range(8):
+            nc.scalar.activation(gb[u][:], ones[:], ACT.Copy, scale=g[:, u // 4, u % 4 : u % 4 + 1])
+        nc.vector.tensor_copy(vw[1][:], tabw[1][:].bitcast(U32).indirect(offs_t[:]))
+        for u in range(4):
+            mm1(u, 0)
+        cast(1, 0, 0, 2, on_vector=True, reuse="grp002")
+        cast(1, 0, 2, 2)
+        quant_w(1, 0, 0, 2)
+        mm1(0, 1)
+        mm1(1, 1)
+        quant_w(1, 0, 2, 2)
+        mm1(2, 1)
+        mm1(3, 1)
+        evac(0, shared=True)
+        evac(1)
+        picks(0)
+        cast(0, 1, 0, 2, reuse="wc100")
+        cast(0, 1, 2, 2, reuse="wc102")
+        cast(1, 1, 0, 2, reuse="ws100")
+        evac(2)
+        picks(1)
+        numer(0)
+        quant_w(0, 1, 0, 2)
+        quant_w(0, 1, 2, 2)
+        quant_w(1, 1, 0, 2)
+        cast(1, 1, 2, 2, reuse="ws102")
+        evac(3)
+        for u in (4, 5):
+            mm1(u, 0)
+            mm1(u, 1)
+        picks(2)
+        quant_w(1, 1, 2, 2)
+        numer(1)
+        for u in (6, 7):
+            mm1(u, 0)
+            mm1(u, 1)
+        picks(3)
+        numer(2)
+        for u in range(4, 8):
+            recip(u - 4)
+            evac(u)
+            picks(u)
+            numer(u - 1)
+        for u in range(4, 8):
+            recip(u)
+        numer(7)
+        make_z(0, 0, NP)
+        make_z(1, 0, CH)
+        quant_z(0, 0, NP)
+        for c in range(0, NP - CH, CH):
+            make_z(1, c + CH, CH)
+            quant_z(1, c, CH)
+            finish(c, c // CH)
+        quant_z(1, NP - CH, CH)
+        finish_last(NP - CH)

@@ -43,13 +43,16 @@ def tile_list_pair_spread_positions_kernel(
         w2s = sb("w2s", [P, 2, N // 4], I32)
         g = sb("g", [P, 2, 4], F32)
         g15 = sb("g15", [P, 2, 4], F32)
-        ones = sb("ones", [P, NP], F32)
+        ones = sb("ones", [P, 256], F32)
         warm = sb("warm", [P, 1], F32)
         raw = {(a, b): sb("raw%d%d" % (a, b), [P, 4, 512], F32) for a in range(2) for b in range(2)}
 
         nc.vector.memset(tabs[:], 0)
         nc.vector.memset(ones[:], 1.0)
         nc.vector.memset(w2s[:], 0)
+        nc.scalar.dma_start(g[:], gain.rearrange("(b p t) -> p b t", b=2, t=4))
+        for q in range(4):
+            nc.scalar.dma_start(tabs[32 * q : 32 * q + 8, :], tab_scales[:, 4 * q : 4 * q + 4, :].bitcast(I32))
         nc.scalar.activation(warm[:], ones[:, 0:1], ACT.Abs_reciprocal_sqrt)
 
         def load_tab(a):
@@ -60,10 +63,7 @@ def tile_list_pair_spread_positions_kernel(
             nc.sync.dma_start(raw[a, b][:], src.rearrange("(p j) c -> p j c", j=4))
 
         nc.sync.dma_start(offs_t[:], offs)
-        for q in range(4):
-            nc.sync.dma_start(tabs[32 * q : 32 * q + 8, :], tab_scales[:, 4 * q : 4 * q + 4, :].bitcast(I32))
         load_tab(0)
-        nc.sync.dma_start(g[:], gain.rearrange("(b p t) -> p b t", b=2, t=4))
         load_w1(0, 0)
         load_tab(1)
         load_w1(1, 0)
@@ -78,7 +78,7 @@ def tile_list_pair_spread_positions_kernel(
                 w2_scales[:, 4 * q : 4 * q + 4, :].rearrange("a r n -> r a n").bitcast(I32),
             )
 
-        gb = [sb("gb%d" % u, [P, NP], F32) for u in range(8)]
+        gb = [sb("gb%d" % u, [P, 256], F32) for u in range(8)]
         nc.vector.tensor_scalar(g15[:], g[:], -1.5, None, ALU.mult)
 
         vw = [sb("vw%d" % a, [P, S], U32) for a in range(2)]
@@ -145,13 +145,19 @@ def tile_list_pair_spread_positions_kernel(
         def picks(u):
             nc.vector.tensor_copy(leg2[u][:], h[u][:].indirect(pos2_t[:]))
             leg1[u] = tmp.tile([P, NP], F32, name="leg1", bufs=3)
-            nc.vector.tensor_tensor(leg1[u][:], h[u][:].indirect(pos1_t[:]), gb[u][:], ALU.mult)
+            for half in range(2):
+                cols = slice(256 * half, 256 * (half + 1))
+                picked = h[u][:].indirect(pos1_t[:, 16 * half : 16 * (half + 1)])
+                nc.vector.tensor_tensor(leg1[u][:, cols], picked, gb[u][:, 0:256], ALU.mult)
+            numer(u)
 
         def numer(u):
             b, t = divmod(u, 4)
-            nc.vector.scalar_tensor_tensor(
-                num[b][:, t, :], leg2[u][:], g15[:, b, t : t + 1], leg1[u][:], ALU.mult, ALU.add
-            )
+            for half in range(2):
+                cols = slice(256 * half, 256 * (half + 1))
+                nc.vector.scalar_tensor_tensor(
+                    num[b][:, t, cols], leg2[u][:, cols], g15[:, b, t : t + 1], leg1[u][:, cols], ALU.mult, ALU.add
+                )
 
         def recip(u):
             b, t = divmod(u, 4)
@@ -163,8 +169,8 @@ def tile_list_pair_spread_positions_kernel(
 
         zb, zc, zs = {}, {}, {}
 
-        def make_z(b, c0, w):
-            zb[b, c0] = sb("zb%d_%d" % (b, c0), [P, w, 4], BF16)
+        def make_z(b, c0, w, reuse=""):
+            zb[b, c0] = sb("zb%d_%d" % (b, c0), [P, w, 4], BF16, reuse)
             nc.vector.tensor_tensor(
                 zb[b, c0][:].rearrange("p (c i) t -> p c t i", i=4),
                 num[b][:, :, c0 : c0 + w].rearrange("p t (c i) -> p c t i", i=4),
@@ -243,7 +249,6 @@ def tile_list_pair_spread_positions_kernel(
         cast(1, 1, 0, 2, reuse="ws100")
         evac(2)
         picks(1)
-        numer(0)
         quant_w(0, 1, 0, 2)
         quant_w(0, 1, 2, 2)
         quant_w(1, 1, 0, 2)
@@ -254,26 +259,27 @@ def tile_list_pair_spread_positions_kernel(
             mm1(u, 1)
         picks(2)
         quant_w(1, 1, 2, 2)
-        numer(1)
         for u in (6, 7):
             mm1(u, 0)
             mm1(u, 1)
         picks(3)
-        numer(2)
         for u in range(4, 8):
             recip(u - 4)
             evac(u)
             picks(u)
-            numer(u - 1)
         for u in range(4, 8):
             recip(u)
-        numer(7)
         make_z(0, 0, NP)
         make_z(1, 0, CH)
         quant_z(0, 0, NP)
-        for c in range(0, NP - CH, CH):
-            make_z(1, c + CH, CH)
-            quant_z(1, c, CH)
-            finish(c, c // CH)
-        quant_z(1, NP - CH, CH)
-        finish_last(NP - CH)
+        make_z(1, CH, CH)
+        quant_z(1, 0, CH)
+        finish(0, 0)
+        make_z(1, 2 * CH, CH)
+        quant_z(1, CH, CH)
+        finish(CH, 1)
+        quant_z(1, 2 * CH, CH)
+        finish(2 * CH, 2)
+        make_z(1, 3 * CH, CH, reuse="zb1_128")
+        quant_z(1, 3 * CH, CH)
+        finish_last(3 * CH)

@@ -39,13 +39,12 @@ def tile_list_pair_spread_positions_kernel(
         pos2_t = keep.tile([P, NP // 16], U16, name="pos2_t")
         tabw = [sb("tabw%d" % a, [P, T], I32) for a in range(2)]
         tabs = sb("tabs", [P, T // 4], I32)
-        w2w = sb("w2w", [P, 2, N // 2], I32)
         w2s = sb("w2s", [P, 2, N // 4], I32)
         g = sb("g", [P, 2, 4], F32)
         g15 = sb("g15", [P, 2, 4], F32)
         ones = sb("ones", [P, 256], F32)
         warm = sb("warm", [P, 1], F32)
-        raw = {(a, b): sb("raw%d%d" % (a, b), [P, 4, 512], F32) for a in range(2) for b in range(2)}
+        raw = {}
 
         nc.vector.memset(tabs[:], 0)
         nc.vector.memset(ones[:], 1.0)
@@ -58,22 +57,20 @@ def tile_list_pair_spread_positions_kernel(
         def load_tab(a):
             nc.sync.dma_start(tabw[a][:], tab_words[a].rearrange("p t i -> p (t i)").bitcast(I32))
 
-        def load_w1(a, b):
+        def load_w1(a, b, reuse=""):
+            raw[a, b] = sb("raw%d%d" % (a, b), [P, 4, 512], F32, reuse)
             src = w1[512 * a : 512 * (a + 1), 512 * b : 512 * (b + 1)]
             nc.sync.dma_start(raw[a, b][:], src.rearrange("(p j) c -> p j c", j=4))
 
         nc.sync.dma_start(offs_t[:], offs)
+        nc.sync.dma_start(pos1_t[:], pos1)
+        nc.sync.dma_start(pos2_t[:], pos2)
         load_tab(0)
         load_w1(0, 0)
         load_tab(1)
         load_w1(1, 0)
-        nc.sync.dma_start(pos1_t[:], pos1)
-        nc.sync.dma_start(pos2_t[:], pos2)
-        load_w1(0, 1)
-        load_w1(1, 1)
-        nc.sync.dma_start(w2w[:], w2_words.rearrange("a p c -> p a c").bitcast(I32))
         for q in range(4):
-            nc.sync.dma_start(
+            nc.gpsimd.dma_start(
                 w2s[32 * q : 32 * q + 4, :, :],
                 w2_scales[:, 4 * q : 4 * q + 4, :].rearrange("a r n -> r a n").bitcast(I32),
             )
@@ -82,9 +79,11 @@ def tile_list_pair_spread_positions_kernel(
         nc.vector.tensor_scalar(g15[:], g[:], -1.5, None, ALU.mult)
 
         vw = [sb("vw%d" % a, [P, S], U32) for a in range(2)]
-        vs = sb("vs", [P, S], U8)
-        nc.vector.tensor_copy(vs[:], tabs[:].bitcast(U8).indirect(offs_t[:]))
         nc.vector.tensor_copy(vw[0][:], tabw[0][:].bitcast(U32).indirect(offs_t[:]))
+        vs = sb("vs", [P, S], U8, "tabw0")
+
+        nc.vector.tensor_copy(vs[:], tabs[:].bitcast(U8).indirect(offs_t[:]))
+        load_w1(0, 1, reuse="tabs")
 
         grp, wc, ws = {}, {}, {}
 
@@ -97,8 +96,8 @@ def tile_list_pair_spread_positions_kernel(
             else:
                 nc.scalar.copy(dst, src)
 
-        def quant_w(a, b, t0, nt):
-            codes = sb("wc%d%d%d" % (a, b, t0), [P, nt * P], U32)
+        def quant_w(a, b, t0, nt, reuse=""):
+            codes = sb("wc%d%d%d" % (a, b, t0), [P, nt * P], U32, reuse)
             scales = sb("ws%d%d%d" % (a, b, t0), [P, nt * P], U8)
             nc.vector.quantize_mx(
                 out=codes[:].bitcast(FP8X4),
@@ -137,13 +136,14 @@ def tile_list_pair_spread_positions_kernel(
                 nc.scalar.copy(h[u][:, 512:1024], hps[u, 1][:])
 
         leg1 = {}
-        leg2 = [sb("leg2_%d" % u, [P, NP], F32) for u in range(8)]
+        leg2s = [sb("leg2_%d" % b, [P, 4, NP], F32) for b in range(2)]
+        leg2 = [leg2s[u // 4][:, u % 4, :] for u in range(8)]
         num = [sb("num%d" % b, [P, 4, NP], F32) for b in range(2)]
         rec = [sb("rec%d" % b, [P, 4, NP], F32) for b in range(2)]
         tmp = ctx.enter_context(tc.tile_pool(name="tmp", bufs=2))
 
         def picks(u):
-            nc.vector.tensor_copy(leg2[u][:], h[u][:].indirect(pos2_t[:]))
+            nc.vector.tensor_copy(leg2[u], h[u][:].indirect(pos2_t[:]))
             leg1[u] = tmp.tile([P, NP], F32, name="leg1", bufs=3)
             for half in range(2):
                 cols = slice(256 * half, 256 * (half + 1))
@@ -159,42 +159,47 @@ def tile_list_pair_spread_positions_kernel(
                     num[b][:, t, cols], leg2[u][:, cols], g15[:, b, t : t + 1], leg1[u][:, cols], ALU.mult, ALU.add
                 )
 
-        def recip(u):
+        def recip(u, n):
             b, t = divmod(u, 4)
-            mag = tmp.tile([P, NP], F32, name="mag")
-            root = tmp.tile([P, NP], F32, name="root")
-            nc.scalar.activation(mag[:], leg2[u][:], ACT.Abs)
+            mag = tmp.tile([P, n, NP], F32, name="mag")
+            root = tmp.tile([P, n, NP], F32, name="root")
+            nc.scalar.activation(mag[:], leg2s[b][:, t : t + n, :], ACT.Abs)
             nc.scalar.activation(root[:], mag[:], ACT.Abs_reciprocal_sqrt, bias=1.0)
-            nc.scalar.activation(rec[b][:, t, :], root[:], ACT.Square)
+            nc.scalar.activation(rec[b][:, t : t + n, :], root[:], ACT.Square)
 
         zb, zc, zs = {}, {}, {}
 
-        def make_z(b, c0, w, reuse=""):
-            zb[b, c0] = sb("zb%d_%d" % (b, c0), [P, w, 4], BF16, reuse)
+        def make_z(b, c, reuse=""):
+            if b == 0:
+                zb[c] = sb("zb%d" % c, [P, 2, CH, 4], BF16, reuse)
+            cols = slice(CH * c, CH * (c + 1))
             nc.vector.tensor_tensor(
-                zb[b, c0][:].rearrange("p (c i) t -> p c t i", i=4),
-                num[b][:, :, c0 : c0 + w].rearrange("p t (c i) -> p c t i", i=4),
-                rec[b][:, :, c0 : c0 + w].rearrange("p t (c i) -> p c t i", i=4),
+                zb[c][:, b].rearrange("p (c i) t -> p c t i", i=2),
+                num[b][:, :, cols].rearrange("p t (c i) -> p c t i", i=2),
+                rec[b][:, :, cols].rearrange("p t (c i) -> p c t i", i=2),
                 ALU.mult,
             )
 
-        def quant_z(b, c0, w):
-            codes = sb("zc%d_%d" % (b, c0), [P, w], U32)
-            scales = sb("zs%d_%d" % (b, c0), [P, w], U8)
+        def quant_z(c, b0, nb):
+            codes = sb("zc%d_%d" % (c, b0), [P, nb, CH], U32)
+            scales = sb("zs%d_%d" % (c, b0), [P, nb, CH], U8)
             nc.vector.quantize_mx(
-                out=codes[:].bitcast(FP8X4), scales=scales[:], in_=zb[b, c0][:].rearrange("p c t -> p (c t)")
+                out=codes[:].rearrange("p b c -> p (b c)").bitcast(FP8X4),
+                scales=scales[:].rearrange("p b c -> p (b c)"),
+                in_=zb[c][:, b0 : b0 + nb].rearrange("p b c t -> p (b c t)"),
             )
-            for c in range(c0, c0 + w, CH):
-                zc[b, c] = codes[:, c - c0 : c - c0 + CH]
-                zs[b, c] = scales[:, c - c0 : c - c0 + CH]
+            for b in range(nb):
+                zc[b0 + b, c] = codes[:, b, :]
+                zs[b0 + b, c] = scales[:, b, :]
 
-        w2b = w2w[:].rearrange("p a c -> p (a c)").bitcast(U8)
         w2sb = w2s[:].rearrange("p a c -> p (a c)").bitcast(U8)
+
+        late = {}
 
         def mm2(dst, nt, c, b):
             nc.tensor.matmul_mx(
                 out=dst,
-                lhsT=w2b[:, 2 * N * b + 2 * P * nt : 2 * N * b + 2 * P * (nt + 1)].bitcast(FP4X4),
+                lhsT=late["w2"][:, 2 * N * b + 2 * P * nt : 2 * N * b + 2 * P * (nt + 1)].bitcast(FP4X4),
                 lhsT_scale=w2sb[:, N * b + P * nt : N * b + P * (nt + 1)],
                 rhs=zc[b, c].bitcast(FP8X4),
                 rhs_scale=zs[b, c],
@@ -204,44 +209,50 @@ def tile_list_pair_spread_positions_kernel(
 
         out_v = out.rearrange("(nt p) j -> p nt j", p=P)
 
-        def finish(c, first_bank):
-            acc = bank(first_bank)
+        def finish(c):
+            acc = bank(c)
             for nt in range(4):
                 for b in range(2):
                     mm2(acc[:, CH * nt : CH * (nt + 1)], nt, c, b)
             res = sb("res%d" % c, [P, 4, CH], F32)
             nc.scalar.activation(res[:].rearrange("p nt j -> p (nt j)"), acc[:], ACT.Tanh)
-            nc.sync.dma_start(out_v[:, :, c : c + CH], res[:])
+            nc.sync.dma_start(out_v[:, :, CH * c : CH * (c + 1)], res[:])
 
-        def finish_last(c):
+        def finish_open(c, banks, store_tiles):
             res = sb("res%d" % c, [P, 4, CH], F32)
-            accs = [bank(4 + nt) for nt in range(4)]
+            accs = [bank(i) for i in banks]
             for nt in range(4):
                 mm2(accs[nt][:, 0:CH], nt, c, 0)
             for nt in range(4):
                 mm2(accs[nt][:, 0:CH], nt, c, 1)
                 nc.scalar.activation(res[:, nt, :], accs[nt][:, 0:CH], ACT.Tanh)
-                if nt % 2 == 1:
-                    nc.sync.dma_start(out_v[:, nt - 1 : nt + 1, c : c + CH], res[:, nt - 1 : nt + 1, :])
+                if (nt + 1) % store_tiles == 0:
+                    rows = slice(nt + 1 - store_tiles, nt + 1)
+                    nc.sync.dma_start(out_v[:, rows, CH * c : CH * (c + 1)], res[:, rows, :])
 
         cast(0, 0, 0, 2)
         cast(0, 0, 2, 2)
+        load_w1(1, 1, reuse="raw00")
         quant_w(0, 0, 0, 2)
-        quant_w(0, 0, 2, 2)
+        mm1(0, 0)
+        mm1(1, 0)
         for u in range(8):
             nc.scalar.activation(gb[u][:], ones[:], ACT.Copy, scale=g[:, u // 4, u % 4 : u % 4 + 1])
         nc.vector.tensor_copy(vw[1][:], tabw[1][:].bitcast(U32).indirect(offs_t[:]))
-        for u in range(4):
-            mm1(u, 0)
-        cast(1, 0, 0, 2, on_vector=True, reuse="grp002")
+        w2w = sb("w2w", [P, 2, N // 2], I32, "tabw1")
+        nc.sync.dma_start(w2w[:], w2_words.rearrange("a p c -> p a c").bitcast(I32))
+        late["w2"] = w2w[:].rearrange("p a c -> p (a c)").bitcast(U8)
+        cast(1, 0, 0, 2)
         cast(1, 0, 2, 2)
         quant_w(1, 0, 0, 2)
         mm1(0, 1)
         mm1(1, 1)
-        quant_w(1, 0, 2, 2)
-        mm1(2, 1)
-        mm1(3, 1)
         evac(0, shared=True)
+        quant_w(0, 0, 2, 2, reuse="grp100")
+        quant_w(1, 0, 2, 2)
+        for u in (2, 3):
+            mm1(u, 0)
+            mm1(u, 1)
         evac(1)
         picks(0)
         cast(0, 1, 0, 2, reuse="wc100")
@@ -263,23 +274,33 @@ def tile_list_pair_spread_positions_kernel(
             mm1(u, 0)
             mm1(u, 1)
         picks(3)
-        for u in range(4, 8):
-            recip(u - 4)
-            evac(u)
-            picks(u)
-        for u in range(4, 8):
-            recip(u)
-        make_z(0, 0, NP)
-        make_z(1, 0, CH)
-        quant_z(0, 0, NP)
-        make_z(1, CH, CH)
-        quant_z(1, 0, CH)
-        finish(0, 0)
-        make_z(1, 2 * CH, CH)
-        quant_z(1, CH, CH)
-        finish(CH, 1)
-        quant_z(1, 2 * CH, CH)
-        finish(2 * CH, 2)
-        make_z(1, 3 * CH, CH, reuse="zb1_128")
-        quant_z(1, 3 * CH, CH)
-        finish_last(3 * CH)
+        recip(0, 2)
+        evac(4)
+        evac(5)
+        picks(4)
+        recip(2, 2)
+        evac(6)
+        evac(7)
+        picks(5)
+        picks(6)
+        picks(7)
+        recip(4, 2)
+        recip(6, 1)
+        recip(7, 1)
+        make_z(0, 0, reuse="gb7")
+        make_z(1, 0)
+        make_z(0, 1, reuse="h7")
+        quant_z(0, 0, 2)
+        finish(0)
+        make_z(1, 1)
+        make_z(0, 2, reuse="gb7")
+        quant_z(1, 0, 2)
+        finish(1)
+        make_z(1, 2)
+        make_z(0, 3, reuse="h7")
+        quant_z(2, 0, 2)
+        finish(2)
+        quant_z(3, 0, 1)
+        make_z(1, 3)
+        quant_z(3, 1, 1)
+        finish_open(3, [4, 5, 6, 7], 2)

@@ -18,6 +18,8 @@ ALU = mybir.AluOpType
 
 P = 128
 CH = 128
+HALF = 256
+SQUARED = 4
 
 
 def tile_list_pair_spread_positions_kernel(
@@ -37,24 +39,26 @@ def tile_list_pair_spread_positions_kernel(
         offs_t = keep.tile([P, S // 16], U16, name="offs_t")
         pos1_t = keep.tile([P, NP // 16], U16, name="pos1_t")
         pos2_t = keep.tile([P, NP // 16], U16, name="pos2_t")
-        tabw = [sb("tabw%d" % a, [P, T], I32) for a in range(2)]
+        tabw = {}
         tabs = sb("tabs", [P, T // 4], I32)
         w2s = sb("w2s", [P, 2, N // 4], I32)
         g = sb("g", [P, 2, 4], F32)
-        g15 = sb("g15", [P, 2, 4], F32)
-        ones = sb("ones", [P, 256], F32)
-        warm = sb("warm", [P, 1], F32)
+        hedge = sb("hedge", [P, HALF], F32)
+        one = sb("one", [P, 1], F32, "tabw1")
+        warm = sb("warm", [P, 1], F32, "raw10")
+        zero = sb("zero", [P, 1], F32, "one2")
         raw = {}
 
         nc.vector.memset(tabs[:], 0)
-        nc.vector.memset(ones[:], 1.0)
-        nc.vector.memset(w2s[:], 0)
-        nc.scalar.dma_start(g[:], gain.rearrange("(b p t) -> p b t", b=2, t=4))
+        nc.vector.memset(one[:], 1.0)
+        nc.vector.memset(zero[:], 0.0)
+        nc.vector.memset(hedge[:], -1.5)
         for q in range(4):
             nc.scalar.dma_start(tabs[32 * q : 32 * q + 8, :], tab_scales[:, 4 * q : 4 * q + 4, :].bitcast(I32))
-        nc.scalar.activation(warm[:], ones[:, 0:1], ACT.Abs_reciprocal_sqrt)
+        nc.scalar.activation(warm[:], one[:], ACT.Abs_reciprocal_sqrt, bias=zero[:])
 
         def load_tab(a):
+            tabw[a] = sb("tabw%d" % a, [P, T], I32)
             nc.sync.dma_start(tabw[a][:], tab_words[a].rearrange("p t i -> p (t i)").bitcast(I32))
 
         def load_w1(a, b, reuse=""):
@@ -63,48 +67,58 @@ def tile_list_pair_spread_positions_kernel(
             nc.sync.dma_start(raw[a, b][:], src.rearrange("(p j) c -> p j c", j=4))
 
         nc.sync.dma_start(offs_t[:], offs)
-        nc.sync.dma_start(pos1_t[:], pos1)
-        nc.sync.dma_start(pos2_t[:], pos2)
         load_tab(0)
         load_w1(0, 0)
+        nc.sync.dma_start(pos2_t[:], pos2)
+        nc.sync.dma_start(pos1_t[:], pos1)
         load_tab(1)
-        load_w1(1, 0)
+        last = []
+        for half in range(2):
+            last.append(sb("last%d" % half, [P, 4, HALF], F32, "raw10" if half == 0 else "one2"))
+            src = w1[512:1024, HALF * half : HALF * (half + 1)]
+            nc.sync.dma_start(last[half][:], src.rearrange("(p j) c -> p j c", j=4))
+        nc.gpsimd.memset(w2s[:], 0)
+        nc.gpsimd.dma_start(g[:], gain.rearrange("(b p t) -> p b t", b=2, t=4))
         for q in range(4):
             nc.gpsimd.dma_start(
                 w2s[32 * q : 32 * q + 4, :, :],
                 w2_scales[:, 4 * q : 4 * q + 4, :].rearrange("a r n -> r a n").bitcast(I32),
             )
 
-        gb = [sb("gb%d" % u, [P, 256], F32) for u in range(8)]
-        nc.vector.tensor_scalar(g15[:], g[:], -1.5, None, ALU.mult)
-
-        vw = [sb("vw%d" % a, [P, S], U32) for a in range(2)]
-        nc.vector.tensor_copy(vw[0][:], tabw[0][:].bitcast(U32).indirect(offs_t[:]))
-        vs = sb("vs", [P, S], U8, "tabw0")
-
+        vs = sb("vs", [P, S], U8)
+        vw = [sb("vw0", [P, S], U32)]
         nc.vector.tensor_copy(vs[:], tabs[:].bitcast(U8).indirect(offs_t[:]))
+        nc.vector.tensor_copy(vw[0][:], tabw[0][:].bitcast(U32).indirect(offs_t[:]))
         load_w1(0, 1, reuse="tabs")
+        load_w1(1, 1, reuse="tabw0")
+        w2sb = w2s[:].rearrange("p a c -> p (a c)").bitcast(U8)
 
         grp, wc, ws = {}, {}, {}
 
-        def cast(a, b, t0, nt, on_vector=False, reuse=""):
-            grp[a, b, t0] = sb("grp%d%d%d" % (a, b, t0), [P, nt, P, 4], BF16, reuse)
+        def cast(a, b, t0, on_vector=False, reuse=""):
+            grp[a, b, t0] = sb("grp%d%d%d" % (a, b, t0), [P, 2, P, 4], BF16, reuse)
             dst = grp[a, b, t0][:].rearrange("p t m j -> p m j t")
-            src = raw[a, b][:].rearrange("p j (m t) -> p m j t", t=4)[:, :, :, t0 : t0 + nt]
+            src = raw[a, b][:].rearrange("p j (m t) -> p m j t", t=4)[:, :, :, t0 : t0 + 2]
             if on_vector:
                 nc.vector.tensor_copy(dst, src)
             else:
                 nc.scalar.copy(dst, src)
 
-        def quant_w(a, b, t0, nt, reuse=""):
-            codes = sb("wc%d%d%d" % (a, b, t0), [P, nt * P], U32, reuse)
-            scales = sb("ws%d%d%d" % (a, b, t0), [P, nt * P], U8)
+        def cast_last(t0, half):
+            if half == 0:
+                grp[1, 0, t0] = sb("grp10%d" % t0, [P, 2, P, 4], BF16)
+            dst = grp[1, 0, t0][:, :, 64 * half : 64 * (half + 1), :].rearrange("p t m j -> p m j t")
+            nc.scalar.copy(dst, last[half][:].rearrange("p j (m t) -> p m j t", t=4)[:, :, :, t0 : t0 + 2])
+
+        def quant_w(a, b, t0, reuse=""):
+            codes = sb("wc%d%d%d" % (a, b, t0), [P, 2 * P], U32, reuse)
+            scales = sb("ws%d%d%d" % (a, b, t0), [P, 2 * P], U8)
             nc.vector.quantize_mx(
                 out=codes[:].bitcast(FP8X4),
                 scales=scales[:],
                 in_=grp[a, b, t0][:].rearrange("p t m j -> p (t m j)"),
             )
-            for t in range(nt):
+            for t in range(2):
                 wc[a, b, t0 + t] = codes[:, P * t : P * (t + 1)]
                 ws[a, b, t0 + t] = scales[:, P * t : P * (t + 1)]
 
@@ -135,172 +149,188 @@ def tile_list_pair_spread_positions_kernel(
             else:
                 nc.scalar.copy(h[u][:, 512:1024], hps[u, 1][:])
 
-        leg1 = {}
-        leg2s = [sb("leg2_%d" % b, [P, 4, NP], F32) for b in range(2)]
-        leg2 = [leg2s[u // 4][:, u % 4, :] for u in range(8)]
-        num = [sb("num%d" % b, [P, 4, NP], F32) for b in range(2)]
-        rec = [sb("rec%d" % b, [P, 4, NP], F32) for b in range(2)]
+        leg2 = [sb("leg2_%d" % b, [P, 4, NP], F32) for b in range(2)]
+        left = [sb("left%d" % b, [P, 4, NP], F32) for b in range(2)]
+        right = [sb("right%d" % b, [P, 4, NP], F32) for b in range(2)]
+        spare = [sb("spare%d" % u, [P, NP], F32) for u in range(8)]
+        num = [left[u // 4][:, u % 4, :] if u < SQUARED else spare[u][:] for u in range(8)]
+        root = [spare[u][:] if u < SQUARED else left[u // 4][:, u % 4, :] for u in range(8)]
         tmp = ctx.enter_context(tc.tile_pool(name="tmp", bufs=2))
 
         def picks(u):
-            nc.vector.tensor_copy(leg2[u], h[u][:].indirect(pos2_t[:]))
-            leg1[u] = tmp.tile([P, NP], F32, name="leg1", bufs=3)
+            b, t = divmod(u, 4)
             for half in range(2):
-                cols = slice(256 * half, 256 * (half + 1))
+                cols = slice(HALF * half, HALF * (half + 1))
+                picked = h[u][:].indirect(pos2_t[:, 16 * half : 16 * (half + 1)])
+                nc.vector.tensor_tensor(leg2[b][:, t, cols], picked, hedge[:], ALU.mult)
+            for half in range(2):
+                cols = slice(HALF * half, HALF * (half + 1))
                 picked = h[u][:].indirect(pos1_t[:, 16 * half : 16 * (half + 1)])
-                nc.vector.tensor_tensor(leg1[u][:, cols], picked, gb[u][:, 0:256], ALU.mult)
-            numer(u)
+                nc.vector.tensor_tensor(num[u][:, cols], picked, leg2[b][:, t, cols], ALU.add)
 
-        def numer(u):
+        def inv_root(u):
             b, t = divmod(u, 4)
-            for half in range(2):
-                cols = slice(256 * half, 256 * (half + 1))
-                nc.vector.scalar_tensor_tensor(
-                    num[b][:, t, cols], leg2[u][:, cols], g15[:, b, t : t + 1], leg1[u][:, cols], ALU.mult, ALU.add
-                )
+            mag = tmp.tile([P, NP], F32, name="mag")
+            nc.scalar.activation(mag[:], leg2[b][:, t, :], ACT.Abs)
+            nc.scalar.activation(root[u], mag[:], ACT.Abs_reciprocal_sqrt, bias=1.0, scale=1.0 / 1.5)
 
-        def recip(u, n):
+        def square_then_gain(u):
             b, t = divmod(u, 4)
-            mag = tmp.tile([P, n, NP], F32, name="mag")
-            root = tmp.tile([P, n, NP], F32, name="root")
-            nc.scalar.activation(mag[:], leg2s[b][:, t : t + n, :], ACT.Abs)
-            nc.scalar.activation(root[:], mag[:], ACT.Abs_reciprocal_sqrt, bias=1.0)
-            nc.scalar.activation(rec[b][:, t : t + n, :], root[:], ACT.Square)
+            rec = tmp.tile([P, NP], F32, name="rec")
+            nc.scalar.activation(rec[:], root[u], ACT.Square)
+            nc.vector.tensor_scalar(right[b][:, t, :], rec[:], g[:, b, t : t + 1], None, ALU.mult)
 
-        zb, zc, zs = {}, {}, {}
+        def second_factor(u):
+            if u < SQUARED:
+                square_then_gain(u)
+            else:
+                gain_and_root(u)
 
-        def make_z(b, c, reuse=""):
-            if b == 0:
-                zb[c] = sb("zb%d" % c, [P, 2, CH, 4], BF16, reuse)
-            cols = slice(CH * c, CH * (c + 1))
+        def gain_and_root(u):
+            b, t = divmod(u, 4)
+            nc.vector.scalar_tensor_tensor(
+                right[b][:, t, :], num[u], g[:, b, t : t + 1], root[u], ALU.mult, ALU.mult
+            )
+
+        zb = [sb("zb%d" % b, [P, NP - CH, 4], BF16) for b in range(2)]
+        late = {}
+
+        def z_tile(b, cols):
+            return late[b][:] if cols.start == NP - CH else zb[b][:, cols, :]
+
+        zc = [sb("zc%d" % b, [P, NP], U32) for b in range(2)]
+        zs = [sb("zs%d" % b, [P, NP], U8) for b in range(2)]
+
+        def make_z(b, cols):
             nc.vector.tensor_tensor(
-                zb[c][:, b].rearrange("p (c i) t -> p c t i", i=2),
-                num[b][:, :, cols].rearrange("p t (c i) -> p c t i", i=2),
-                rec[b][:, :, cols].rearrange("p t (c i) -> p c t i", i=2),
+                z_tile(b, cols).rearrange("p (c i) t -> p c t i", i=2),
+                left[b][:, :, cols].rearrange("p t (c i) -> p c t i", i=2),
+                right[b][:, :, cols].rearrange("p t (c i) -> p c t i", i=2),
                 ALU.mult,
             )
 
-        def quant_z(c, b0, nb):
-            codes = sb("zc%d_%d" % (c, b0), [P, nb, CH], U32)
-            scales = sb("zs%d_%d" % (c, b0), [P, nb, CH], U8)
+        def quant_z(b, cols):
             nc.vector.quantize_mx(
-                out=codes[:].rearrange("p b c -> p (b c)").bitcast(FP8X4),
-                scales=scales[:].rearrange("p b c -> p (b c)"),
-                in_=zb[c][:, b0 : b0 + nb].rearrange("p b c t -> p (b c t)"),
+                out=zc[b][:, cols].bitcast(FP8X4),
+                scales=zs[b][:, cols],
+                in_=z_tile(b, cols).rearrange("p c t -> p (c t)"),
             )
-            for b in range(nb):
-                zc[b0 + b, c] = codes[:, b, :]
-                zs[b0 + b, c] = scales[:, b, :]
 
-        w2sb = w2s[:].rearrange("p a c -> p (a c)").bitcast(U8)
+        acc = {}
 
-        late = {}
-
-        def mm2(dst, nt, c, b):
+        def mm2(nt, c, b):
+            group, part = max(c - 1, 0), c % 2 if c < 2 else 0
+            if b == 0 and part == 0:
+                acc[group, nt] = bank(4 * (group % 2) + nt)
+            cols = slice(CH * c, CH * (c + 1))
             nc.tensor.matmul_mx(
-                out=dst,
-                lhsT=late["w2"][:, 2 * N * b + 2 * P * nt : 2 * N * b + 2 * P * (nt + 1)].bitcast(FP4X4),
+                out=acc[group, nt][:, CH * part : CH * (part + 1)],
+                lhsT=w2c[:, 2 * N * b + 2 * P * nt : 2 * N * b + 2 * P * (nt + 1)].bitcast(FP4X4),
                 lhsT_scale=w2sb[:, N * b + P * nt : N * b + P * (nt + 1)],
-                rhs=zc[b, c].bitcast(FP8X4),
-                rhs_scale=zs[b, c],
-                start=(b == 0),
-                stop=(b == 1),
+                rhs=zc[b][:, cols].bitcast(FP8X4),
+                rhs_scale=zs[b][:, cols],
+                start=(b == 0 and part == 0),
+                stop=(b == 1 and c > 0),
             )
 
         out_v = out.rearrange("(nt p) j -> p nt j", p=P)
 
-        def finish(c):
-            acc = bank(c)
+        def finish(group, store_tiles):
+            width = HALF if group == 0 else CH
+            first = 0 if group == 0 else CH * (group + 1)
+            res = sb("res%d" % group, [P, 4, width], F32)
             for nt in range(4):
-                for b in range(2):
-                    mm2(acc[:, CH * nt : CH * (nt + 1)], nt, c, b)
-            res = sb("res%d" % c, [P, 4, CH], F32)
-            nc.scalar.activation(res[:].rearrange("p nt j -> p (nt j)"), acc[:], ACT.Tanh)
-            nc.sync.dma_start(out_v[:, :, CH * c : CH * (c + 1)], res[:])
-
-        def finish_open(c, banks, store_tiles):
-            res = sb("res%d" % c, [P, 4, CH], F32)
-            accs = [bank(i) for i in banks]
-            for nt in range(4):
-                mm2(accs[nt][:, 0:CH], nt, c, 0)
-            for nt in range(4):
-                mm2(accs[nt][:, 0:CH], nt, c, 1)
-                nc.scalar.activation(res[:, nt, :], accs[nt][:, 0:CH], ACT.Tanh)
+                mm2(nt, group + 1, 1)
+                nc.scalar.activation(res[:, nt, :], acc[group, nt][:, 0:width], ACT.Tanh)
                 if (nt + 1) % store_tiles == 0:
                     rows = slice(nt + 1 - store_tiles, nt + 1)
-                    nc.sync.dma_start(out_v[:, rows, CH * c : CH * (c + 1)], res[:, rows, :])
+                    nc.sync.dma_start(out_v[:, rows, first : first + width], res[:, rows, :])
 
-        cast(0, 0, 0, 2)
-        cast(0, 0, 2, 2)
-        load_w1(1, 1, reuse="raw00")
-        quant_w(0, 0, 0, 2)
+        def chunk(c):
+            return slice(CH * c, CH * (c + 1))
+
+        cast(0, 0, 0)
+        cast(0, 0, 2)
+        quant_w(0, 0, 0)
         mm1(0, 0)
         mm1(1, 0)
-        for u in range(8):
-            nc.scalar.activation(gb[u][:], ones[:], ACT.Copy, scale=g[:, u // 4, u % 4 : u % 4 + 1])
+        vw.append(sb("vw1", [P, S], U32))
         nc.vector.tensor_copy(vw[1][:], tabw[1][:].bitcast(U32).indirect(offs_t[:]))
         w2w = sb("w2w", [P, 2, N // 2], I32, "tabw1")
         nc.sync.dma_start(w2w[:], w2_words.rearrange("a p c -> p a c").bitcast(I32))
-        late["w2"] = w2w[:].rearrange("p a c -> p (a c)").bitcast(U8)
-        cast(1, 0, 0, 2)
-        cast(1, 0, 2, 2)
-        quant_w(1, 0, 0, 2)
+        w2c = w2w[:].rearrange("p a c -> p (a c)").bitcast(U8)
+        cast_last(0, 0)
+        cast_last(0, 1)
+        cast_last(2, 0)
+        cast_last(2, 1)
+        quant_w(1, 0, 0)
         mm1(0, 1)
         mm1(1, 1)
+        quant_w(0, 0, 2, reuse="grp100")
+        quant_w(1, 0, 2)
         evac(0, shared=True)
-        quant_w(0, 0, 2, 2, reuse="grp100")
-        quant_w(1, 0, 2, 2)
         for u in (2, 3):
             mm1(u, 0)
             mm1(u, 1)
         evac(1)
         picks(0)
-        cast(0, 1, 0, 2, reuse="wc100")
-        cast(0, 1, 2, 2, reuse="wc102")
-        cast(1, 1, 0, 2, reuse="ws100")
+        cast(0, 1, 0, reuse="wc100")
         evac(2)
         picks(1)
-        quant_w(0, 1, 0, 2)
-        quant_w(0, 1, 2, 2)
-        quant_w(1, 1, 0, 2)
-        cast(1, 1, 2, 2, reuse="ws102")
+        quant_w(0, 1, 0)
+        cast(1, 1, 0, reuse="ws100")
         evac(3)
+        picks(2)
+        quant_w(1, 1, 0)
         for u in (4, 5):
             mm1(u, 0)
             mm1(u, 1)
-        picks(2)
-        quant_w(1, 1, 2, 2)
+        cast(0, 1, 2, reuse="wc102")
+        cast(1, 1, 2, reuse="ws102")
+        picks(3)
+        evac(4)
+        quant_w(0, 1, 2)
+        quant_w(1, 1, 2)
         for u in (6, 7):
             mm1(u, 0)
             mm1(u, 1)
-        picks(3)
-        recip(0, 2)
-        evac(4)
-        evac(5)
-        picks(4)
-        recip(2, 2)
-        evac(6)
-        evac(7)
-        picks(5)
-        picks(6)
-        picks(7)
-        recip(4, 2)
-        recip(6, 1)
-        recip(7, 1)
-        make_z(0, 0, reuse="gb7")
-        make_z(1, 0)
-        make_z(0, 1, reuse="h7")
-        quant_z(0, 0, 2)
-        finish(0)
-        make_z(1, 1)
-        make_z(0, 2, reuse="gb7")
-        quant_z(1, 0, 2)
-        finish(1)
-        make_z(1, 2)
-        make_z(0, 3, reuse="h7")
-        quant_z(2, 0, 2)
-        finish(2)
-        quant_z(3, 0, 1)
-        make_z(1, 3)
-        quant_z(3, 1, 1)
-        finish_open(3, [4, 5, 6, 7], 2)
+        for u in range(4, 8):
+            if u < 7:
+                evac(u + 1)
+            picks(u)
+            inv_root(u - 4)
+            second_factor(u - 4)
+        make_z(0, slice(0, HALF))
+        inv_root(4)
+        second_factor(4)
+        make_z(0, chunk(2))
+        inv_root(5)
+        second_factor(5)
+        quant_z(0, slice(0, HALF))
+        quant_z(0, chunk(2))
+        for c in range(3):
+            for nt in range(4):
+                mm2(nt, c, 0)
+        inv_root(6)
+        inv_root(7)
+        second_factor(6)
+        second_factor(7)
+        make_z(1, chunk(0))
+        make_z(1, chunk(1))
+        quant_z(1, chunk(0))
+        for nt in range(4):
+            mm2(nt, 0, 1)
+        make_z(1, chunk(2))
+        quant_z(1, chunk(1))
+        finish(0, 2)
+        late[0] = sb("late0", [P, CH, 4], BF16, "spare7")
+        late[1] = sb("late1", [P, CH, 4], BF16)
+        make_z(0, chunk(3))
+        quant_z(1, chunk(2))
+        finish(1, 4)
+        make_z(1, chunk(3))
+        quant_z(0, chunk(3))
+        for nt in range(4):
+            mm2(nt, 3, 0)
+        quant_z(1, chunk(3))
+        finish(2, 2)

@@ -19,7 +19,6 @@ ALU = mybir.AluOpType
 P = 128
 CH = 128
 HALF = 256
-SQUARED = 4
 
 
 def tile_list_pair_spread_positions_kernel(
@@ -43,7 +42,7 @@ def tile_list_pair_spread_positions_kernel(
         tabs = sb("tabs", [P, T // 4], I32)
         w2s = sb("w2s", [P, 2, N // 4], I32)
         g = sb("g", [P, 2, 4], F32)
-        hedge = sb("hedge", [P, HALF], F32)
+        h = [sb("h%d" % t, [P, 2 * S], F32) for t in range(3)]
         one = sb("one", [P, 1], F32, "tabw1")
         warm = sb("warm", [P, 1], F32, "raw10")
         zero = sb("zero", [P, 1], F32, "one2")
@@ -52,7 +51,8 @@ def tile_list_pair_spread_positions_kernel(
         nc.vector.memset(tabs[:], 0)
         nc.vector.memset(one[:], 1.0)
         nc.vector.memset(zero[:], 0.0)
-        nc.vector.memset(hedge[:], -1.5)
+        for t in range(3):
+            nc.vector.memset(h[t][:, S : 2 * S], 0.0)
         for q in range(4):
             nc.scalar.dma_start(tabs[32 * q : 32 * q + 8, :], tab_scales[:, 4 * q : 4 * q + 4, :].bitcast(I32))
         nc.scalar.activation(warm[:], one[:], ACT.Abs_reciprocal_sqrt, bias=zero[:])
@@ -89,8 +89,14 @@ def tile_list_pair_spread_positions_kernel(
         vw = [sb("vw0", [P, S], U32)]
         nc.vector.tensor_copy(vs[:], tabs[:].bitcast(U8).indirect(offs_t[:]))
         nc.vector.tensor_copy(vw[0][:], tabw[0][:].bitcast(U32).indirect(offs_t[:]))
-        load_w1(0, 1, reuse="tabs")
-        load_w1(1, 1, reuse="tabw0")
+
+        def load_half(a, half, reuse):
+            raw[a, 1, half] = sb("raw%d1%d" % (a, half), [P, 4, HALF], F32, reuse)
+            src = w1[512 * a : 512 * (a + 1), 512 + HALF * half : 512 + HALF * (half + 1)]
+            nc.sync.dma_start(raw[a, 1, half][:], src.rearrange("(p j) c -> p j c", j=4))
+
+        load_half(0, 0, "tabw0")
+        load_half(0, 1, "tabs")
         w2sb = w2s[:].rearrange("p a c -> p (a c)").bitcast(U8)
 
         grp, wc, ws = {}, {}, {}
@@ -109,6 +115,14 @@ def tile_list_pair_spread_positions_kernel(
                 grp[1, 0, t0] = sb("grp10%d" % t0, [P, 2, P, 4], BF16)
             dst = grp[1, 0, t0][:, :, 64 * half : 64 * (half + 1), :].rearrange("p t m j -> p m j t")
             nc.scalar.copy(dst, last[half][:].rearrange("p j (m t) -> p m j t", t=4)[:, :, :, t0 : t0 + 2])
+
+        def cast_half(a, half, reuse=""):
+            if half == 0:
+                grp[a, 1] = sb("grp%d1" % a, [P, 4, P, 4], BF16, reuse)
+                grp[a, 1, 0] = grp[a, 1][:, 0:2]
+                grp[a, 1, 2] = grp[a, 1][:, 2:4]
+            dst = grp[a, 1][:, :, 64 * half : 64 * (half + 1), :].rearrange("p t m j -> p m j t")
+            nc.scalar.copy(dst, raw[a, 1, half][:].rearrange("p j (m t) -> p m j t", t=4))
 
         def quant_w(a, b, t0, reuse=""):
             codes = sb("wc%d%d%d" % (a, b, t0), [P, 2 * P], U32, reuse)
@@ -140,56 +154,44 @@ def tile_list_pair_spread_positions_kernel(
                     stop=(a == 1),
                 )
 
-        h = [sb("h%d" % u, [P, S], F32) for u in range(8)]
-
         def evac(u, shared=False):
-            nc.scalar.copy(h[u][:, 0:512], hps[u, 0][:])
+            nc.scalar.copy(h[u % 3][:, 0:512], hps[u, 0][:])
             if shared:
-                nc.vector.tensor_copy(h[u][:, 512:1024], hps[u, 1][:])
+                nc.vector.tensor_copy(h[u % 3][:, 512:1024], hps[u, 1][:])
             else:
-                nc.scalar.copy(h[u][:, 512:1024], hps[u, 1][:])
+                nc.scalar.copy(h[u % 3][:, 512:1024], hps[u, 1][:])
 
         leg2 = [sb("leg2_%d" % b, [P, 4, NP], F32) for b in range(2)]
-        left = [sb("left%d" % b, [P, 4, NP], F32) for b in range(2)]
+        left, num, root = {}, {}, {}
+        left[1] = sb("left1", [P, 4, NP], F32)
         right = [sb("right%d" % b, [P, 4, NP], F32) for b in range(2)]
-        spare = [sb("spare%d" % u, [P, NP], F32) for u in range(8)]
-        num = [left[u // 4][:, u % 4, :] if u < SQUARED else spare[u][:] for u in range(8)]
-        root = [spare[u][:] if u < SQUARED else left[u // 4][:, u % 4, :] for u in range(8)]
-        tmp = ctx.enter_context(tc.tile_pool(name="tmp", bufs=2))
 
-        def picks(u):
+        def pick2(u):
             b, t = divmod(u, 4)
-            for half in range(2):
-                cols = slice(HALF * half, HALF * (half + 1))
-                picked = h[u][:].indirect(pos2_t[:, 16 * half : 16 * (half + 1)])
-                nc.vector.tensor_tensor(leg2[b][:, t, cols], picked, hedge[:], ALU.mult)
-            for half in range(2):
-                cols = slice(HALF * half, HALF * (half + 1))
-                picked = h[u][:].indirect(pos1_t[:, 16 * half : 16 * (half + 1)])
-                nc.vector.tensor_tensor(num[u][:, cols], picked, leg2[b][:, t, cols], ALU.add)
+            nc.vector.tensor_scalar(leg2[b][:, t, :], h[u % 3][:].indirect(pos2_t[:]), -1.5, 0.0, ALU.mult, ALU.add)
+
+        def pick1(u, reuse):
+            b, t = divmod(u, 4)
+            num[u] = sb("num%d" % u, [P, NP], F32, reuse)
+            nc.vector.tensor_tensor(num[u][:], h[u % 3][:].indirect(pos1_t[:]), leg2[b][:, t, :], ALU.add)
 
         def inv_root(u):
             b, t = divmod(u, 4)
-            mag = tmp.tile([P, NP], F32, name="mag")
+            mag = sb("mag%d" % u, [P, NP], F32)
+            root[u] = sb("root%d" % u, [P, NP], F32)[:] if b == 0 else left[1][:, t, :]
             nc.scalar.activation(mag[:], leg2[b][:, t, :], ACT.Abs)
             nc.scalar.activation(root[u], mag[:], ACT.Abs_reciprocal_sqrt, bias=1.0, scale=1.0 / 1.5)
 
-        def square_then_gain(u):
-            b, t = divmod(u, 4)
-            rec = tmp.tile([P, NP], F32, name="rec")
-            nc.scalar.activation(rec[:], root[u], ACT.Square)
-            nc.vector.tensor_scalar(right[b][:, t, :], rec[:], g[:, b, t : t + 1], None, ALU.mult)
+        def square(t):
+            nc.scalar.activation(right[0][:, t, :], root[t], ACT.Square)
 
-        def second_factor(u):
-            if u < SQUARED:
-                square_then_gain(u)
-            else:
-                gain_and_root(u)
+        def gain_num(t):
+            nc.vector.tensor_scalar(left[0][:, t, :], num[t][:], g[:, 0, t : t + 1], None, ALU.mult)
 
         def gain_and_root(u):
-            b, t = divmod(u, 4)
+            t = u - 4
             nc.vector.scalar_tensor_tensor(
-                right[b][:, t, :], num[u], g[:, b, t : t + 1], root[u], ALU.mult, ALU.mult
+                right[1][:, t, :], num[u][:], g[:, 1, t : t + 1], root[u], ALU.mult, ALU.mult
             )
 
         zb = [sb("zb%d" % b, [P, NP - CH, 4], BF16) for b in range(2)]
@@ -272,40 +274,62 @@ def tile_list_pair_spread_positions_kernel(
         for u in (2, 3):
             mm1(u, 0)
             mm1(u, 1)
+        load_half(1, 0, "grp000")
+        load_half(1, 1, "raw00")
         evac(1)
-        picks(0)
-        cast(0, 1, 0, reuse="wc100")
+        pick2(0)
+        pick2(1)
+        cast_half(0, 0, reuse="wc100")
+        pick1(0, "tabw0")
         evac(2)
-        picks(1)
+        pick2(2)
+        cast_half(0, 1)
+        pick1(1, "tabs")
         quant_w(0, 1, 0)
-        cast(1, 1, 0, reuse="ws100")
-        evac(3)
-        picks(2)
-        quant_w(1, 1, 0)
-        for u in (4, 5):
-            mm1(u, 0)
-            mm1(u, 1)
-        cast(0, 1, 2, reuse="wc102")
-        cast(1, 1, 2, reuse="ws102")
-        picks(3)
-        evac(4)
         quant_w(0, 1, 2)
-        quant_w(1, 1, 2)
-        for u in (6, 7):
-            mm1(u, 0)
-            mm1(u, 1)
         for u in range(4, 8):
-            if u < 7:
-                evac(u + 1)
-            picks(u)
-            inv_root(u - 4)
-            second_factor(u - 4)
+            mm1(u, 0)
+        evac(3)
+        pick2(3)
+        cast_half(1, 0, reuse="ws100")
+        pick1(2, "grp000")
+        cast_half(1, 1)
+        quant_w(1, 1, 0)
+        mm1(4, 1)
+        mm1(5, 1)
+        quant_w(1, 1, 2)
+        mm1(6, 1)
+        mm1(7, 1)
+        pick1(3, "raw00")
+        left[0] = sb("left0", [P, 4, NP], F32, "ws100")
+        evac(4)
+        pick2(4)
+        evac(5)
+        pick2(5)
+        inv_root(0)
+        pick1(4, "mag0")
+        evac(6)
+        square(0)
+        pick2(6)
+        inv_root(1)
+        pick1(5, "mag1")
+        evac(7)
+        square(1)
+        pick2(7)
+        inv_root(2)
+        pick1(6, "mag2")
+        square(2)
+        pick1(7, "root2")
+        inv_root(3)
+        square(3)
+        for t in range(4):
+            gain_num(t)
         make_z(0, slice(0, HALF))
         inv_root(4)
-        second_factor(4)
+        gain_and_root(4)
         make_z(0, chunk(2))
         inv_root(5)
-        second_factor(5)
+        gain_and_root(5)
         quant_z(0, slice(0, HALF))
         quant_z(0, chunk(2))
         for c in range(3):
@@ -313,8 +337,8 @@ def tile_list_pair_spread_positions_kernel(
                 mm2(nt, c, 0)
         inv_root(6)
         inv_root(7)
-        second_factor(6)
-        second_factor(7)
+        gain_and_root(6)
+        gain_and_root(7)
         make_z(1, chunk(0))
         make_z(1, chunk(1))
         quant_z(1, chunk(0))
@@ -323,7 +347,7 @@ def tile_list_pair_spread_positions_kernel(
         make_z(1, chunk(2))
         quant_z(1, chunk(1))
         finish(0, 2)
-        late[0] = sb("late0", [P, CH, 4], BF16, "spare7")
+        late[0] = sb("late0", [P, CH, 4], BF16, "root2")
         late[1] = sb("late1", [P, CH, 4], BF16)
         make_z(0, chunk(3))
         quant_z(1, chunk(2))

@@ -19,6 +19,7 @@ ALU = mybir.AluOpType
 P = 128
 CH = 128
 HALF = 256
+SQUARED = 5
 
 
 def tile_list_pair_spread_positions_kernel(
@@ -40,8 +41,6 @@ def tile_list_pair_spread_positions_kernel(
         pos2_t = keep.tile([P, NP // 16], U16, name="pos2_t")
         tabw = {}
         tabs = sb("tabs", [P, T // 4], I32)
-        w2s = sb("w2s", [P, 2, N // 4], I32)
-        g = sb("g", [P, 2, 4], F32)
         h = [sb("h%d" % t, [P, 2 * S], F32) for t in range(3)]
         one = sb("one", [P, 1], F32, "tabw1")
         warm = sb("warm", [P, 1], F32, "raw10")
@@ -77,13 +76,6 @@ def tile_list_pair_spread_positions_kernel(
             last.append(sb("last%d" % half, [P, 4, HALF], F32, "raw10" if half == 0 else "one2"))
             src = w1[512:1024, HALF * half : HALF * (half + 1)]
             nc.sync.dma_start(last[half][:], src.rearrange("(p j) c -> p j c", j=4))
-        nc.gpsimd.memset(w2s[:], 0)
-        nc.gpsimd.dma_start(g[:], gain.rearrange("(b p t) -> p b t", b=2, t=4))
-        for q in range(4):
-            nc.gpsimd.dma_start(
-                w2s[32 * q : 32 * q + 4, :, :],
-                w2_scales[:, 4 * q : 4 * q + 4, :].rearrange("a r n -> r a n").bitcast(I32),
-            )
 
         vs = sb("vs", [P, S], U8)
         vw = [sb("vw0", [P, S], U32)]
@@ -97,7 +89,6 @@ def tile_list_pair_spread_positions_kernel(
 
         load_half(0, 0, "tabw0")
         load_half(0, 1, "tabs")
-        w2sb = w2s[:].rearrange("p a c -> p (a c)").bitcast(U8)
 
         grp, wc, ws = {}, {}, {}
 
@@ -116,13 +107,17 @@ def tile_list_pair_spread_positions_kernel(
             dst = grp[1, 0, t0][:, :, 64 * half : 64 * (half + 1), :].rearrange("p t m j -> p m j t")
             nc.scalar.copy(dst, last[half][:].rearrange("p j (m t) -> p m j t", t=4)[:, :, :, t0 : t0 + 2])
 
-        def cast_half(a, half, reuse=""):
+        def cast_half(a, half, reuse="", on_vector=False):
             if half == 0:
                 grp[a, 1] = sb("grp%d1" % a, [P, 4, P, 4], BF16, reuse)
                 grp[a, 1, 0] = grp[a, 1][:, 0:2]
                 grp[a, 1, 2] = grp[a, 1][:, 2:4]
             dst = grp[a, 1][:, :, 64 * half : 64 * (half + 1), :].rearrange("p t m j -> p m j t")
-            nc.scalar.copy(dst, raw[a, 1, half][:].rearrange("p j (m t) -> p m j t", t=4))
+            src = raw[a, 1, half][:].rearrange("p j (m t) -> p m j t", t=4)
+            if on_vector:
+                nc.vector.tensor_copy(dst, src)
+            else:
+                nc.scalar.copy(dst, src)
 
         def quant_w(a, b, t0, reuse=""):
             codes = sb("wc%d%d%d" % (a, b, t0), [P, 2 * P], U32, reuse)
@@ -162,8 +157,8 @@ def tile_list_pair_spread_positions_kernel(
                 nc.scalar.copy(h[u % 3][:, 512:1024], hps[u, 1][:])
 
         leg2 = [sb("leg2_%d" % b, [P, 4, NP], F32) for b in range(2)]
-        left, num, root = {}, {}, {}
-        left[1] = sb("left1", [P, 4, NP], F32)
+        num, root, left = {}, {}, {}
+        left = [sb("left%d" % b, [P, 4, NP], F32) for b in range(2)]
         right = [sb("right%d" % b, [P, 4, NP], F32) for b in range(2)]
 
         def pick2(u):
@@ -174,19 +169,29 @@ def tile_list_pair_spread_positions_kernel(
             b, t = divmod(u, 4)
             num[u] = sb("num%d" % u, [P, NP], F32, reuse)
             nc.vector.tensor_tensor(num[u][:], h[u % 3][:].indirect(pos1_t[:]), leg2[b][:, t, :], ALU.add)
+            if u < SQUARED:
+                gain_num(u)
 
         def inv_root(u):
             b, t = divmod(u, 4)
             mag = sb("mag%d" % u, [P, NP], F32)
-            root[u] = sb("root%d" % u, [P, NP], F32)[:] if b == 0 else left[1][:, t, :]
+            root[u] = sb("root%d" % u, [P, NP], F32)[:] if u < SQUARED else left[1][:, t, :]
             nc.scalar.activation(mag[:], leg2[b][:, t, :], ACT.Abs)
             nc.scalar.activation(root[u], mag[:], ACT.Abs_reciprocal_sqrt, bias=1.0, scale=1.0 / 1.5)
 
-        def square(t):
-            nc.scalar.activation(right[0][:, t, :], root[t], ACT.Square)
+        def square(u):
+            b, t = divmod(u, 4)
+            nc.scalar.activation(right[b][:, t, :], root[u], ACT.Square)
 
-        def gain_num(t):
-            nc.vector.tensor_scalar(left[0][:, t, :], num[t][:], g[:, 0, t : t + 1], None, ALU.mult)
+        def gain_num(u):
+            b, t = divmod(u, 4)
+            nc.gpsimd.tensor_scalar(left[b][:, t, :], num[u][:], g[:, b, t : t + 1], 0.0, ALU.mult, ALU.add)
+
+        def second_factor(u):
+            if u < SQUARED:
+                square(u)
+            else:
+                gain_and_root(u)
 
         def gain_and_root(u):
             t = u - 4
@@ -276,23 +281,32 @@ def tile_list_pair_spread_positions_kernel(
             mm1(u, 1)
         load_half(1, 0, "grp000")
         load_half(1, 1, "raw00")
+        g = sb("g", [P, 2, 4], F32, "grp002")
+        nc.sync.dma_start(g[:], gain.rearrange("(b p t) -> p b t", b=2, t=4))
+        w2s = sb("w2s", [P, 2, N // 4], I32, "wc100")
+        nc.gpsimd.memset(w2s[:], 0)
+        for q in range(4):
+            nc.sync.dma_start(
+                w2s[32 * q : 32 * q + 4, :, :],
+                w2_scales[:, 4 * q : 4 * q + 4, :].rearrange("a r n -> r a n").bitcast(I32),
+            )
+        w2sb = w2s[:].rearrange("p a c -> p (a c)").bitcast(U8)
+        cast_half(0, 0, reuse="grp102", on_vector=True)
         evac(1)
         pick2(0)
         pick2(1)
-        cast_half(0, 0, reuse="wc100")
-        pick1(0, "tabw0")
-        evac(2)
-        pick2(2)
         cast_half(0, 1)
-        pick1(1, "tabs")
+        pick1(0, "tabs")
         quant_w(0, 1, 0)
         quant_w(0, 1, 2)
         for u in range(4, 8):
             mm1(u, 0)
+        evac(2)
+        pick2(2)
+        cast_half(1, 0, reuse="ws100")
+        pick1(1, "grp000")
         evac(3)
         pick2(3)
-        cast_half(1, 0, reuse="ws100")
-        pick1(2, "grp000")
         cast_half(1, 1)
         quant_w(1, 1, 0)
         mm1(4, 1)
@@ -300,36 +314,34 @@ def tile_list_pair_spread_positions_kernel(
         quant_w(1, 1, 2)
         mm1(6, 1)
         mm1(7, 1)
-        pick1(3, "raw00")
-        left[0] = sb("left0", [P, 4, NP], F32, "ws100")
+        pick1(2, "raw00")
         evac(4)
+        inv_root(0)
+        pick1(3, "mag0")
         pick2(4)
+        square(0)
         evac(5)
         pick2(5)
-        inv_root(0)
-        pick1(4, "mag0")
-        evac(6)
-        square(0)
-        pick2(6)
         inv_root(1)
-        pick1(5, "mag1")
-        evac(7)
+        pick1(4, "mag1")
+        evac(6)
         square(1)
-        pick2(7)
+        pick2(6)
         inv_root(2)
-        pick1(6, "mag2")
+        pick1(5, "mag2")
+        evac(7)
         square(2)
-        pick1(7, "root2")
+        pick2(7)
         inv_root(3)
+        pick1(6, "mag3")
         square(3)
-        for t in range(4):
-            gain_num(t)
+        pick1(7, "root3")
         make_z(0, slice(0, HALF))
         inv_root(4)
-        gain_and_root(4)
+        second_factor(4)
         make_z(0, chunk(2))
         inv_root(5)
-        gain_and_root(5)
+        second_factor(5)
         quant_z(0, slice(0, HALF))
         quant_z(0, chunk(2))
         for c in range(3):
@@ -337,8 +349,8 @@ def tile_list_pair_spread_positions_kernel(
                 mm2(nt, c, 0)
         inv_root(6)
         inv_root(7)
-        gain_and_root(6)
-        gain_and_root(7)
+        second_factor(6)
+        second_factor(7)
         make_z(1, chunk(0))
         make_z(1, chunk(1))
         quant_z(1, chunk(0))
@@ -347,7 +359,7 @@ def tile_list_pair_spread_positions_kernel(
         make_z(1, chunk(2))
         quant_z(1, chunk(1))
         finish(0, 2)
-        late[0] = sb("late0", [P, CH, 4], BF16, "root2")
+        late[0] = sb("late0", [P, CH, 4], BF16, "root3")
         late[1] = sb("late1", [P, CH, 4], BF16)
         make_z(0, chunk(3))
         quant_z(1, chunk(2))

@@ -19,7 +19,7 @@ ALU = mybir.AluOpType
 P = 128
 CH = 128
 HALF = 256
-SQUARED = 5
+SQUARED = 6
 
 
 def tile_list_pair_spread_positions_kernel(
@@ -107,27 +107,29 @@ def tile_list_pair_spread_positions_kernel(
             dst = grp[1, 0, t0][:, :, 64 * half : 64 * (half + 1), :].rearrange("p t m j -> p m j t")
             nc.scalar.copy(dst, last[half][:].rearrange("p j (m t) -> p m j t", t=4)[:, :, :, t0 : t0 + 2])
 
-        def cast_half(a, half, reuse="", on_vector=False):
+        def cast_half(a, half, reuse="", on_pool=False):
             if half == 0:
                 grp[a, 1] = sb("grp%d1" % a, [P, 4, P, 4], BF16, reuse)
                 grp[a, 1, 0] = grp[a, 1][:, 0:2]
                 grp[a, 1, 2] = grp[a, 1][:, 2:4]
             dst = grp[a, 1][:, :, 64 * half : 64 * (half + 1), :].rearrange("p t m j -> p m j t")
             src = raw[a, 1, half][:].rearrange("p j (m t) -> p m j t", t=4)
-            if on_vector:
-                nc.vector.tensor_copy(dst, src)
+            if on_pool:
+                order = "p m j t -> p m t j"
+                nc.gpsimd.tensor_scalar(dst.rearrange(order), src.rearrange(order), 1.0, 0.0, ALU.mult, ALU.add)
             else:
                 nc.scalar.copy(dst, src)
 
-        def quant_w(a, b, t0, reuse=""):
-            codes = sb("wc%d%d%d" % (a, b, t0), [P, 2 * P], U32, reuse)
-            scales = sb("ws%d%d%d" % (a, b, t0), [P, 2 * P], U8)
+        def quant_w(a, b, t0, nt=2, reuse=""):
+            codes = sb("wc%d%d%d" % (a, b, t0), [P, nt * P], U32, reuse)
+            scales = sb("ws%d%d%d" % (a, b, t0), [P, nt * P], U8)
+            source = grp[a, b, t0] if nt == 2 else grp[a, b]
             nc.vector.quantize_mx(
                 out=codes[:].bitcast(FP8X4),
                 scales=scales[:],
-                in_=grp[a, b, t0][:].rearrange("p t m j -> p (t m j)"),
+                in_=source[:].rearrange("p t m j -> p (t m j)"),
             )
-            for t in range(2):
+            for t in range(nt):
                 wc[a, b, t0 + t] = codes[:, P * t : P * (t + 1)]
                 ws[a, b, t0 + t] = scales[:, P * t : P * (t + 1)]
 
@@ -291,22 +293,18 @@ def tile_list_pair_spread_positions_kernel(
                 w2_scales[:, 4 * q : 4 * q + 4, :].rearrange("a r n -> r a n").bitcast(I32),
             )
         w2sb = w2s[:].rearrange("p a c -> p (a c)").bitcast(U8)
-        cast_half(0, 0, reuse="grp102", on_vector=True)
+        cast_half(0, 0, reuse="grp102", on_pool=True)
+        cast_half(0, 1, on_pool=True)
         evac(1)
         pick2(0)
         pick2(1)
-        cast_half(0, 1)
-        pick1(0, "tabs")
-        quant_w(0, 1, 0)
-        quant_w(0, 1, 2)
+        quant_w(0, 1, 0, 4)
         for u in range(4, 8):
             mm1(u, 0)
+        pick1(0, "tabs")
         evac(2)
         pick2(2)
         cast_half(1, 0, reuse="ws100")
-        pick1(1, "grp000")
-        evac(3)
-        pick2(3)
         cast_half(1, 1)
         quant_w(1, 1, 0)
         mm1(4, 1)
@@ -314,23 +312,19 @@ def tile_list_pair_spread_positions_kernel(
         quant_w(1, 1, 2)
         mm1(6, 1)
         mm1(7, 1)
-        pick1(2, "raw00")
-        evac(4)
+        pick1(1, "raw00")
+        evac(3)
+        pick2(3)
         inv_root(0)
-        pick1(3, "mag0")
-        pick2(4)
-        square(0)
-        evac(5)
-        pick2(5)
-        inv_root(1)
-        pick1(4, "mag1")
-        evac(6)
-        square(1)
-        pick2(6)
-        inv_root(2)
-        pick1(5, "mag2")
+        pick1(2, "mag0")
+        for u in range(4, 7):
+            evac(u)
+            pick2(u)
+            square(u - 4)
+            pick1(u - 1, "root%d" % (u - 4))
+            if u < 6:
+                inv_root(u - 3)
         evac(7)
-        square(2)
         pick2(7)
         inv_root(3)
         pick1(6, "mag3")

@@ -19,7 +19,7 @@ ALU = mybir.AluOpType
 P = 128
 CH = 128
 HALF = 256
-SQUARED = 6
+SQUARED = 4
 
 
 def tile_list_pair_spread_positions_kernel(

@@ -15,11 +15,12 @@ FP8X4 = mybir.dt.float8_e4m3fn_x4
 FP4X4 = mybir.dt.float4_e2m1fn_x4
 ACT = mybir.ActivationFunctionType
 ALU = mybir.AluOpType
+WIDTH = {F32: 4, I32: 4, U32: 4, BF16: 2, U8: 1}
 
 P = 128
 CH = 128
 HALF = 256
-SQUARED = 4
+WINDOWS = 4
 
 
 def tile_list_pair_spread_positions_kernel(
@@ -27,109 +28,100 @@ def tile_list_pair_spread_positions_kernel(
 ):
     nc = tc.nc
     with ExitStack() as ctx:
+        lists = ctx.enter_context(tc.tile_pool(name="lists", bufs=1))
         keep = ctx.enter_context(tc.tile_pool(name="keep", bufs=1))
         psum = ctx.enter_context(tc.psum_pool(name="psum", bufs=1))
+        where = {"end": 0}
 
-        def sb(name, shape, dtype, tag=""):
-            return keep.tile(shape, dtype, name=name, tag=tag or name, align_bytes=64)
+        def sb(name, shape, dtype, over="", at=0):
+            if over:
+                where[name] = where[over] + at
+            else:
+                size = WIDTH[dtype]
+                for extent in shape[1:]:
+                    size = size * extent
+                where[name] = where["end"]
+                where["end"] = where["end"] + (size + 63) // 64 * 64
+            return keep.tile(shape, dtype, name=name, tag=name, align_bytes=64, offset=where[name])
+
+        def room(name, size):
+            where[name] = where["end"]
+            where["end"] = where["end"] + size
 
         def bank(i):
             return psum.tile([P, 512], F32, name="bank%d" % i)
 
-        offs_t = keep.tile([P, S // 16], U16, name="offs_t")
-        pos1_t = keep.tile([P, NP // 16], U16, name="pos1_t")
-        pos2_t = keep.tile([P, NP // 16], U16, name="pos2_t")
-        tabw = {}
+        offs_t = lists.tile([P, S // 16], U16, name="offs_t")
+        pos1_t = lists.tile([P, NP // 16], U16, name="pos1_t")
+        pos2_t = lists.tile([P, NP // 16], U16, name="pos2_t")
+
         tabs = sb("tabs", [P, T // 4], I32)
-        h = [sb("h%d" % t, [P, 2 * S], F32) for t in range(3)]
-        one = sb("one", [P, 1], F32, "tabw1")
-        warm = sb("warm", [P, 1], F32, "raw10")
-        zero = sb("zero", [P, 1], F32, "one2")
-        raw = {}
+        h = [sb("h%d" % i, [P, 2 * S], F32) for i in range(WINDOWS)]
+        room("second", 8 * T)
+        one = sb("one", [P, 1], F32, "second")
+        warm = sb("warm", [P, 1], F32, "second", 4 * T)
+        zero = sb("zero", [P, 1], F32, "second", 6 * T)
 
         nc.vector.memset(tabs[:], 0)
         nc.vector.memset(one[:], 1.0)
         nc.vector.memset(zero[:], 0.0)
-        for t in range(3):
-            nc.vector.memset(h[t][:, S : 2 * S], 0.0)
+        for i in range(WINDOWS):
+            nc.gpsimd.memset(h[i][:, S : 2 * S], 0.0)
         for q in range(4):
             nc.scalar.dma_start(tabs[32 * q : 32 * q + 8, :], tab_scales[:, 4 * q : 4 * q + 4, :].bitcast(I32))
         nc.scalar.activation(warm[:], one[:], ACT.Abs_reciprocal_sqrt, bias=zero[:])
 
-        def load_tab(a):
-            tabw[a] = sb("tabw%d" % a, [P, T], I32)
+        tabw, raw = {}, {}
+
+        def load_tab(a, over="", at=0):
+            tabw[a] = sb("tabw%d" % a, [P, T], I32, over, at)
             nc.sync.dma_start(tabw[a][:], tab_words[a].rearrange("p t i -> p (t i)").bitcast(I32))
 
-        def load_w1(a, b, reuse=""):
-            raw[a, b] = sb("raw%d%d" % (a, b), [P, 4, 512], F32, reuse)
-            src = w1[512 * a : 512 * (a + 1), 512 * b : 512 * (b + 1)]
-            nc.sync.dma_start(raw[a, b][:], src.rearrange("(p j) c -> p j c", j=4))
+        def load_w1(a, first, width, over="", at=0):
+            raw[a, first] = sb("raw%d_%d" % (a, first), [P, 4, width], F32, over, at)
+            src = w1[512 * a : 512 * (a + 1), first : first + width]
+            nc.sync.dma_start(raw[a, first][:], src.rearrange("(p j) c -> p j c", j=4))
 
         nc.sync.dma_start(offs_t[:], offs)
         load_tab(0)
-        load_w1(0, 0)
+        load_w1(0, 0, 512)
         nc.sync.dma_start(pos2_t[:], pos2)
         nc.sync.dma_start(pos1_t[:], pos1)
-        load_tab(1)
-        last = []
-        for half in range(2):
-            last.append(sb("last%d" % half, [P, 4, HALF], F32, "raw10" if half == 0 else "one2"))
-            src = w1[512:1024, HALF * half : HALF * (half + 1)]
-            nc.sync.dma_start(last[half][:], src.rearrange("(p j) c -> p j c", j=4))
+        load_tab(1, "second")
+        load_w1(1, 0, HALF, "second", 4 * T)
+        load_w1(1, HALF, HALF, "second", 6 * T)
 
         vs = sb("vs", [P, S], U8)
-        vw = [sb("vw0", [P, S], U32)]
+        vw = [sb("vw%d" % a, [P, S], U32) for a in range(2)]
         nc.vector.tensor_copy(vs[:], tabs[:].bitcast(U8).indirect(offs_t[:]))
         nc.vector.tensor_copy(vw[0][:], tabw[0][:].bitcast(U32).indirect(offs_t[:]))
-
-        def load_half(a, half, reuse):
-            raw[a, 1, half] = sb("raw%d1%d" % (a, half), [P, 4, HALF], F32, reuse)
-            src = w1[512 * a : 512 * (a + 1), 512 + HALF * half : 512 + HALF * (half + 1)]
-            nc.sync.dma_start(raw[a, 1, half][:], src.rearrange("(p j) c -> p j c", j=4))
-
-        load_half(0, 0, "tabw0")
-        load_half(0, 1, "tabs")
+        load_w1(0, 512, 512, "tabw0")
 
         grp, wc, ws = {}, {}, {}
 
-        def cast(a, b, t0, on_vector=False, reuse=""):
-            grp[a, b, t0] = sb("grp%d%d%d" % (a, b, t0), [P, 2, P, 4], BF16, reuse)
-            dst = grp[a, b, t0][:].rearrange("p t m j -> p m j t")
-            src = raw[a, b][:].rearrange("p j (m t) -> p m j t", t=4)[:, :, :, t0 : t0 + 2]
-            if on_vector:
-                nc.vector.tensor_copy(dst, src)
-            else:
-                nc.scalar.copy(dst, src)
-
-        def cast_last(t0, half):
-            if half == 0:
-                grp[1, 0, t0] = sb("grp10%d" % t0, [P, 2, P, 4], BF16)
-            dst = grp[1, 0, t0][:, :, 64 * half : 64 * (half + 1), :].rearrange("p t m j -> p m j t")
-            nc.scalar.copy(dst, last[half][:].rearrange("p j (m t) -> p m j t", t=4)[:, :, :, t0 : t0 + 2])
-
-        def cast_half(a, half, reuse="", on_pool=False):
-            if half == 0:
-                grp[a, 1] = sb("grp%d1" % a, [P, 4, P, 4], BF16, reuse)
-                grp[a, 1, 0] = grp[a, 1][:, 0:2]
-                grp[a, 1, 2] = grp[a, 1][:, 2:4]
-            dst = grp[a, 1][:, :, 64 * half : 64 * (half + 1), :].rearrange("p t m j -> p m j t")
-            src = raw[a, 1, half][:].rearrange("p j (m t) -> p m j t", t=4)
-            if on_pool:
+        def cast(engine, a, b, t0, first, width, base):
+            lo = (first - 512 * b) // 4
+            dst = grp[a, b, t0][:, :, lo : lo + width // 4, :].rearrange("p t m j -> p m j t")
+            src = raw[a, base][:, :, first - base : first - base + width]
+            src = src.rearrange("p j (m t) -> p m j t", t=4)[:, :, :, t0 : t0 + 2]
+            if engine == "pool":
                 order = "p m j t -> p m t j"
                 nc.gpsimd.tensor_scalar(dst.rearrange(order), src.rearrange(order), 1.0, 0.0, ALU.mult, ALU.add)
             else:
                 nc.scalar.copy(dst, src)
 
-        def quant_w(a, b, t0, nt=2, reuse=""):
-            codes = sb("wc%d%d%d" % (a, b, t0), [P, nt * P], U32, reuse)
-            scales = sb("ws%d%d%d" % (a, b, t0), [P, nt * P], U8)
-            source = grp[a, b, t0] if nt == 2 else grp[a, b]
+        def group_tile(a, b, t0, over="", at=0):
+            grp[a, b, t0] = sb("grp%d%d%d" % (a, b, t0), [P, 2, P, 4], BF16, over, at)
+
+        def quant_w(a, b, t0, over="", at=0):
+            codes = sb("wc%d%d%d" % (a, b, t0), [P, 2 * P], U32, over, at)
+            scales = sb("ws%d%d%d" % (a, b, t0), [P, 2 * P], U8)
             nc.vector.quantize_mx(
                 out=codes[:].bitcast(FP8X4),
                 scales=scales[:],
-                in_=source[:].rearrange("p t m j -> p (t m j)"),
+                in_=grp[a, b, t0][:].rearrange("p t m j -> p (t m j)"),
             )
-            for t in range(nt):
+            for t in range(2):
                 wc[a, b, t0 + t] = codes[:, P * t : P * (t + 1)]
                 ws[a, b, t0 + t] = scales[:, P * t : P * (t + 1)]
 
@@ -152,215 +144,243 @@ def tile_list_pair_spread_positions_kernel(
                 )
 
         def evac(u, shared=False):
-            nc.scalar.copy(h[u % 3][:, 0:512], hps[u, 0][:])
+            nc.scalar.copy(h[u % WINDOWS][:, 0:512], hps[u, 0][:])
             if shared:
-                nc.vector.tensor_copy(h[u % 3][:, 512:1024], hps[u, 1][:])
+                nc.vector.tensor_copy(h[u % WINDOWS][:, 512:1024], hps[u, 1][:])
             else:
-                nc.scalar.copy(h[u % 3][:, 512:1024], hps[u, 1][:])
+                nc.scalar.copy(h[u % WINDOWS][:, 512:1024], hps[u, 1][:])
 
-        leg2 = [sb("leg2_%d" % b, [P, 4, NP], F32) for b in range(2)]
-        num, root, left = {}, {}, {}
+        leg2 = {}
         left = [sb("left%d" % b, [P, 4, NP], F32) for b in range(2)]
         right = [sb("right%d" % b, [P, 4, NP], F32) for b in range(2)]
+        num, mag, root, inv = {}, {}, {}, {}
+
+        legs = [sb("legs%d" % i, [P, 2, NP], F32) for i in range(4)]
 
         def pick2(u):
+            leg2[u] = legs[u // 2][:, u % 2, :]
+            nc.vector.tensor_scalar(leg2[u], h[u % WINDOWS][:].indirect(pos2_t[:]), -1.5, 0.0, ALU.mult, ALU.add)
+
+        def pick1(u, over="", at=0):
+            num[u] = sb("num%d" % u, [P, NP], F32, over, at)
+            nc.vector.tensor_tensor(num[u][:], h[u % WINDOWS][:].indirect(pos1_t[:]), leg2[u], ALU.add)
+
+        def pick1_direct(u):
+            nc.vector.tensor_tensor(left[1][:, u - 4, :], h[u % WINDOWS][:].indirect(pos1_t[:]), leg2[u], ALU.add)
+
+        def magnitude_in_left(u):
+            nc.scalar.activation(left[1][:, u - 4, :], leg2[u], ACT.Abs)
+
+        def inv_root_from_left(u):
+            root[u] = sb("root%d" % u, [P, NP], F32)
+            nc.scalar.activation(root[u][:], left[1][:, u - 4, :], ACT.Abs_reciprocal_sqrt, bias=1.0, scale=1.0 / 1.5)
+
+        def square_apart(u):
+            inv[u] = sb("inv%d" % u, [P, NP], F32)
+            nc.scalar.activation(inv[u][:], root[u][:], ACT.Square)
+
+        def gain_inv(u):
+            nc.scalar.activation(right[1][:, u - 4, :], inv[u][:], ACT.Copy, scale=g[:, 1, u - 4 : u - 3])
+
+        def magnitude(u, count, over="", at=0):
+            tile = sb("mag%d" % u, [P, count, NP], F32, over, at)
+            nc.scalar.activation(tile[:], legs[u // 2][:, u % 2 : u % 2 + count, :], ACT.Abs)
+            for i in range(count):
+                mag[u + i] = (tile, i)
+
+        def inv_root(u, count, over="", at=0):
+            tile, i = mag[u]
+            root[u] = sb("root%d" % u, [P, count, NP], F32, over, at)
+            nc.scalar.activation(root[u][:], tile[:, i : i + count, :], ACT.Abs_reciprocal_sqrt, bias=1.0, scale=1.0 / 1.5)
+
+        def square(u, count):
             b, t = divmod(u, 4)
-            nc.vector.tensor_scalar(leg2[b][:, t, :], h[u % 3][:].indirect(pos2_t[:]), -1.5, 0.0, ALU.mult, ALU.add)
+            nc.scalar.activation(right[b][:, t : t + count, :], root[u][:], ACT.Square)
 
-        def pick1(u, reuse):
+        def gain_num(u, engine):
             b, t = divmod(u, 4)
-            num[u] = sb("num%d" % u, [P, NP], F32, reuse)
-            nc.vector.tensor_tensor(num[u][:], h[u % 3][:].indirect(pos1_t[:]), leg2[b][:, t, :], ALU.add)
-            if u < SQUARED:
-                gain_num(u)
+            engine.tensor_scalar(left[b][:, t, :], num[u][:], g[:, b, t : t + 1], 0.0, ALU.mult, ALU.add)
 
-        def inv_root(u):
-            b, t = divmod(u, 4)
-            mag = sb("mag%d" % u, [P, NP], F32)
-            root[u] = sb("root%d" % u, [P, NP], F32)[:] if u < SQUARED else left[1][:, t, :]
-            nc.scalar.activation(mag[:], leg2[b][:, t, :], ACT.Abs)
-            nc.scalar.activation(root[u], mag[:], ACT.Abs_reciprocal_sqrt, bias=1.0, scale=1.0 / 1.5)
-
-        def square(u):
-            b, t = divmod(u, 4)
-            nc.scalar.activation(right[b][:, t, :], root[u], ACT.Square)
-
-        def gain_num(u):
-            b, t = divmod(u, 4)
-            nc.gpsimd.tensor_scalar(left[b][:, t, :], num[u][:], g[:, b, t : t + 1], 0.0, ALU.mult, ALU.add)
-
-        def second_factor(u):
-            if u < SQUARED:
-                square(u)
-            else:
-                gain_and_root(u)
-
-        def gain_and_root(u):
-            t = u - 4
-            nc.vector.scalar_tensor_tensor(
-                right[1][:, t, :], num[u][:], g[:, 1, t : t + 1], root[u], ALU.mult, ALU.mult
-            )
-
-        zb = [sb("zb%d" % b, [P, NP - CH, 4], BF16) for b in range(2)]
-        late = {}
-
-        def z_tile(b, cols):
-            return late[b][:] if cols.start == NP - CH else zb[b][:, cols, :]
-
-        zc = [sb("zc%d" % b, [P, NP], U32) for b in range(2)]
+        zb = {}
+        zc = {1: sb("zc1", [P, NP], U32)}
         zs = [sb("zs%d" % b, [P, NP], U8) for b in range(2)]
 
-        def make_z(b, cols):
+        def make_z(b, cols, over="", at=0):
+            zb[b, cols.start] = sb("zb%d_%d" % (b, cols.start), [P, cols.stop - cols.start, 4], BF16, over, at)
             nc.vector.tensor_tensor(
-                z_tile(b, cols).rearrange("p (c i) t -> p c t i", i=2),
+                zb[b, cols.start][:].rearrange("p (c i) t -> p c t i", i=2),
                 left[b][:, :, cols].rearrange("p t (c i) -> p c t i", i=2),
                 right[b][:, :, cols].rearrange("p t (c i) -> p c t i", i=2),
                 ALU.mult,
             )
 
         def quant_z(b, cols):
+            first = max(start for group, start in zb if group == b and start <= cols.start)
+            source = zb[b, first][:, cols.start - first : cols.stop - first, :]
             nc.vector.quantize_mx(
                 out=zc[b][:, cols].bitcast(FP8X4),
                 scales=zs[b][:, cols],
-                in_=z_tile(b, cols).rearrange("p c t -> p (c t)"),
+                in_=source.rearrange("p c t -> p (c t)"),
             )
 
         acc = {}
 
-        def mm2(nt, c, b):
-            group, part = max(c - 1, 0), c % 2 if c < 2 else 0
-            if b == 0 and part == 0:
-                acc[group, nt] = bank(4 * (group % 2) + nt)
-            cols = slice(CH * c, CH * (c + 1))
-            nc.tensor.matmul_mx(
-                out=acc[group, nt][:, CH * part : CH * (part + 1)],
-                lhsT=w2c[:, 2 * N * b + 2 * P * nt : 2 * N * b + 2 * P * (nt + 1)].bitcast(FP4X4),
-                lhsT_scale=w2sb[:, N * b + P * nt : N * b + P * (nt + 1)],
-                rhs=zc[b][:, cols].bitcast(FP8X4),
-                rhs_scale=zs[b][:, cols],
-                start=(b == 0 and part == 0),
-                stop=(b == 1 and c > 0),
-            )
+        def mm2(c, b):
+            last = c == 3
+            for nt in range(4):
+                if b == 0 and (last or nt == 0):
+                    acc[c, nt] = bank(3 + nt if last else c)
+                place = acc[c, nt][:, 0:CH] if last else acc[c, 0][:, CH * nt : CH * (nt + 1)]
+                cols = slice(CH * c, CH * (c + 1))
+                nc.tensor.matmul_mx(
+                    out=place,
+                    lhsT=w2c[:, 2 * N * b + 2 * P * nt : 2 * N * b + 2 * P * (nt + 1)].bitcast(FP4X4),
+                    lhsT_scale=w2sb[:, N * b + P * nt : N * b + P * (nt + 1)],
+                    rhs=zc[b][:, cols].bitcast(FP8X4),
+                    rhs_scale=zs[b][:, cols],
+                    start=(b == 0 and (last or nt == 0)),
+                    stop=(b == 1 and (last or nt == 3)),
+                )
 
         out_v = out.rearrange("(nt p) j -> p nt j", p=P)
 
-        def finish(group, store_tiles):
-            width = HALF if group == 0 else CH
-            first = 0 if group == 0 else CH * (group + 1)
-            res = sb("res%d" % group, [P, 4, width], F32)
-            for nt in range(4):
-                mm2(nt, group + 1, 1)
-                nc.scalar.activation(res[:, nt, :], acc[group, nt][:, 0:width], ACT.Tanh)
-                if (nt + 1) % store_tiles == 0:
-                    rows = slice(nt + 1 - store_tiles, nt + 1)
-                    nc.sync.dma_start(out_v[:, rows, first : first + width], res[:, rows, :])
+        def finish(c):
+            res = sb("res%d" % c, [P, 4, CH], F32)
+            cols = slice(CH * c, CH * (c + 1))
+            if c < 3:
+                nc.scalar.activation(res[:].rearrange("p n j -> p (n j)"), acc[c, 0][:], ACT.Tanh)
+                nc.sync.dma_start(out_v[:, :, cols], res[:])
+            else:
+                for nt in range(4):
+                    nc.scalar.activation(res[:, nt, :], acc[c, nt][:, 0:CH], ACT.Tanh)
+                    if nt % 2 == 1:
+                        nc.sync.dma_start(out_v[:, nt - 1 : nt + 1, cols], res[:, nt - 1 : nt + 1, :])
 
         def chunk(c):
             return slice(CH * c, CH * (c + 1))
 
-        cast(0, 0, 0)
-        cast(0, 0, 2)
+        for t0 in (0, 2):
+            group_tile(0, 0, t0)
+            cast("act", 0, 0, t0, 0, 512, 0)
         quant_w(0, 0, 0)
         mm1(0, 0)
         mm1(1, 0)
-        vw.append(sb("vw1", [P, S], U32))
         nc.vector.tensor_copy(vw[1][:], tabw[1][:].bitcast(U32).indirect(offs_t[:]))
+        load_w1(1, 512, 512, "raw0_0")
         w2w = sb("w2w", [P, 2, N // 2], I32, "tabw1")
         nc.sync.dma_start(w2w[:], w2_words.rearrange("a p c -> p a c").bitcast(I32))
         w2c = w2w[:].rearrange("p a c -> p (a c)").bitcast(U8)
-        cast_last(0, 0)
-        cast_last(0, 1)
-        cast_last(2, 0)
-        cast_last(2, 1)
+        g = sb("g", [P, 2, 4], F32, "tabw1", 4096)
+        nc.sync.dma_start(g[:], gain.rearrange("(b p t) -> p b t", b=2, t=4))
+        w2s = sb("w2s", [P, 2, N // 4], I32, "tabs")
+        nc.gpsimd.memset(w2s[:], 0)
+        for t0 in (0, 2):
+            group_tile(1, 0, t0)
+            for first in (0, HALF):
+                cast("act", 1, 0, t0, first, HALF, first)
         quant_w(1, 0, 0)
         mm1(0, 1)
         mm1(1, 1)
-        quant_w(0, 0, 2, reuse="grp100")
-        quant_w(1, 0, 2)
+        quant_w(0, 0, 2, "grp100")
+        room("third", 4096)
+        quant_w(1, 0, 2, "third")
         evac(0, shared=True)
         for u in (2, 3):
             mm1(u, 0)
             mm1(u, 1)
-        load_half(1, 0, "grp000")
-        load_half(1, 1, "raw00")
-        g = sb("g", [P, 2, 4], F32, "grp002")
-        nc.sync.dma_start(g[:], gain.rearrange("(b p t) -> p b t", b=2, t=4))
-        w2s = sb("w2s", [P, 2, N // 4], I32, "wc100")
-        nc.gpsimd.memset(w2s[:], 0)
         for q in range(4):
             nc.sync.dma_start(
                 w2s[32 * q : 32 * q + 4, :, :],
                 w2_scales[:, 4 * q : 4 * q + 4, :].rearrange("a r n -> r a n").bitcast(I32),
             )
         w2sb = w2s[:].rearrange("p a c -> p (a c)").bitcast(U8)
-        cast_half(0, 0, reuse="grp102", on_pool=True)
-        cast_half(0, 1, on_pool=True)
-        evac(1)
-        pick2(0)
-        pick2(1)
-        quant_w(0, 1, 0, 4)
-        for u in range(4, 8):
-            mm1(u, 0)
-        pick1(0, "tabs")
-        evac(2)
-        pick2(2)
-        cast_half(1, 0, reuse="ws100")
-        cast_half(1, 1)
-        quant_w(1, 1, 0)
-        mm1(4, 1)
-        mm1(5, 1)
-        quant_w(1, 1, 2)
-        mm1(6, 1)
-        mm1(7, 1)
-        pick1(1, "raw00")
-        evac(3)
-        pick2(3)
-        inv_root(0)
-        pick1(2, "mag0")
-        for u in range(4, 7):
+
+        group_tile(0, 1, 0, "grp102")
+        group_tile(0, 1, 2)
+        group_tile(1, 1, 0)
+        group_tile(1, 1, 2)
+        cast("pool", 0, 1, 0, 512, 512, 512)
+        cast("pool", 0, 1, 2, 512, 512, 512)
+        cast("pool", 1, 1, 0, 512, 512, 512)
+        cast("pool", 1, 1, 2, 512, 512, 512)
+        for u in range(1, 4):
             evac(u)
+        for u in range(4):
             pick2(u)
-            square(u - 4)
-            pick1(u - 1, "root%d" % (u - 4))
-            if u < 6:
-                inv_root(u - 3)
+        quant_w(0, 1, 0, "raw1_512")
+        quant_w(1, 1, 0, "raw1_512", 4096)
+        mm1(4, 0)
+        mm1(4, 1)
+        mm1(5, 0)
+        mm1(5, 1)
+        quant_w(0, 1, 2, "raw1_512", 1024)
+        quant_w(1, 1, 2)
+        mm1(6, 0)
+        mm1(6, 1)
+        mm1(7, 0)
+        mm1(7, 1)
+        pick1(0, "grp010")
+        pick1(1, "raw1_512", 2048)
+        pick1(2, "grp110")
+        magnitude(0, 2, "third")
+        magnitude(2, 2, "raw0_512")
+        inv_root(0, 2)
+        inv_root(2, 1)
+        inv_root(3, 1)
+        evac(4)
+        pick2(4)
+        gain_num(2, nc.gpsimd)
+        square(0, 2)
+        gain_num(0, nc.vector)
+        gain_num(1, nc.vector)
+        pick1(3, "root0")
+        evac(5)
+        pick2(5)
+        gain_num(3, nc.gpsimd)
+        square(2, 1)
+        pick1(4, "root2")
+        evac(6)
+        pick2(6)
+        gain_num(4, nc.gpsimd)
+        square(3, 1)
+        magnitude(4, 2)
         evac(7)
+        pick1(5, "root3")
         pick2(7)
-        inv_root(3)
-        pick1(6, "mag3")
-        square(3)
-        pick1(7, "root3")
-        make_z(0, slice(0, HALF))
-        inv_root(4)
-        second_factor(4)
-        make_z(0, chunk(2))
-        inv_root(5)
-        second_factor(5)
+        gain_num(5, nc.gpsimd)
+        inv_root(4, 2)
+        magnitude_in_left(6)
+        square(4, 2)
+        inv_root_from_left(6)
+        magnitude_in_left(7)
+        square_apart(6)
+        inv_root_from_left(7)
+        gain_inv(6)
+        square_apart(7)
+        gain_inv(7)
+        make_z(0, slice(0, 3 * CH), "mag4")
+        pick1_direct(6)
+        pick1_direct(7)
+        zc[0] = sb("zc0", [P, NP], U32, "inv6")
         quant_z(0, slice(0, HALF))
+        mm2(0, 0)
+        mm2(1, 0)
         quant_z(0, chunk(2))
-        for c in range(3):
-            for nt in range(4):
-                mm2(nt, c, 0)
-        inv_root(6)
-        inv_root(7)
-        second_factor(6)
-        second_factor(7)
+        mm2(2, 0)
+
+        def close(c):
+            quant_z(1, chunk(c))
+            mm2(c, 1)
+            finish(c)
+
         make_z(1, chunk(0))
         make_z(1, chunk(1))
-        quant_z(1, chunk(0))
-        for nt in range(4):
-            mm2(nt, 0, 1)
+        close(0)
         make_z(1, chunk(2))
-        quant_z(1, chunk(1))
-        finish(0, 2)
-        late[0] = sb("late0", [P, CH, 4], BF16, "root3")
-        late[1] = sb("late1", [P, CH, 4], BF16)
-        make_z(0, chunk(3))
-        quant_z(1, chunk(2))
-        finish(1, 4)
+        close(1)
+        make_z(0, chunk(3), "zb1_0")
+        close(2)
         make_z(1, chunk(3))
         quant_z(0, chunk(3))
-        for nt in range(4):
-            mm2(nt, 3, 0)
-        quant_z(1, chunk(3))
-        finish(2, 2)
+        mm2(3, 0)
+        close(3)

@@ -66,7 +66,7 @@ def tile_list_pair_spread_positions_kernel(
         nc.vector.memset(one[:], 1.0)
         nc.vector.memset(zero[:], 0.0)
         for i in range(WINDOWS):
-            nc.gpsimd.memset(h[i][:, S : 2 * S], 0.0)
+            nc.vector.memset(h[i][:, S : 2 * S], 0.0)
         for q in range(4):
             nc.scalar.dma_start(tabs[32 * q : 32 * q + 8, :], tab_scales[:, 4 * q : 4 * q + 4, :].bitcast(I32))
         nc.scalar.activation(warm[:], one[:], ACT.Abs_reciprocal_sqrt, bias=zero[:])
@@ -99,19 +99,25 @@ def tile_list_pair_spread_positions_kernel(
 
         grp, wc, ws = {}, {}, {}
 
-        def cast(engine, a, b, t0, first, width, base):
+        def cast(a, b, t0, first, width, base):
             lo = (first - 512 * b) // 4
             dst = grp[a, b, t0][:, :, lo : lo + width // 4, :].rearrange("p t m j -> p m j t")
             src = raw[a, base][:, :, first - base : first - base + width]
             src = src.rearrange("p j (m t) -> p m j t", t=4)[:, :, :, t0 : t0 + 2]
+            nc.scalar.copy(dst, src)
+
+        def cast_half(engine, a, half):
+            dst = wide[a][:, :, 64 * half : 64 * (half + 1), :]
+            src = raw[a, 512][:, :, HALF * half : HALF * (half + 1)]
             if engine == "pool":
-                order = "p m j t -> p m t j"
-                nc.gpsimd.tensor_scalar(dst.rearrange(order), src.rearrange(order), 1.0, 0.0, ALU.mult, ALU.add)
+                dst = dst.rearrange("p t m j -> p m t j")
+                src = src.rearrange("p j (m t) -> p m t j", t=4)
+                nc.gpsimd.tensor_scalar(dst, src, 1.0, 0.0, ALU.mult, ALU.add)
             else:
-                nc.scalar.copy(dst, src)
+                nc.scalar.copy(dst.rearrange("p t m j -> p m j t"), src.rearrange("p j (m t) -> p m j t", t=4))
 
         def group_tile(a, b, t0, over="", at=0):
-            grp[a, b, t0] = sb("grp%d%d%d" % (a, b, t0), [P, 2, P, 4], BF16, over, at)
+            grp[a, b, t0] = sb("grp%d%d%d" % (a, b, t0), [P, 2, P, 4], BF16, over, at)[:]
 
         def quant_w(a, b, t0, over="", at=0):
             codes = sb("wc%d%d%d" % (a, b, t0), [P, 2 * P], U32, over, at)
@@ -119,7 +125,7 @@ def tile_list_pair_spread_positions_kernel(
             nc.vector.quantize_mx(
                 out=codes[:].bitcast(FP8X4),
                 scales=scales[:],
-                in_=grp[a, b, t0][:].rearrange("p t m j -> p (t m j)"),
+                in_=grp[a, b, t0].rearrange("p t m j -> p (t m j)"),
             )
             for t in range(2):
                 wc[a, b, t0 + t] = codes[:, P * t : P * (t + 1)]
@@ -261,7 +267,7 @@ def tile_list_pair_spread_positions_kernel(
 
         for t0 in (0, 2):
             group_tile(0, 0, t0)
-            cast("act", 0, 0, t0, 0, 512, 0)
+            cast(0, 0, t0, 0, 512, 0)
         quant_w(0, 0, 0)
         mm1(0, 0)
         mm1(1, 0)
@@ -274,10 +280,11 @@ def tile_list_pair_spread_positions_kernel(
         nc.sync.dma_start(g[:], gain.rearrange("(b p t) -> p b t", b=2, t=4))
         w2s = sb("w2s", [P, 2, N // 4], I32, "tabs")
         nc.gpsimd.memset(w2s[:], 0)
+        room("late0", 4096)
         for t0 in (0, 2):
-            group_tile(1, 0, t0)
+            group_tile(1, 0, t0, "late0" if t0 else "")
             for first in (0, HALF):
-                cast("act", 1, 0, t0, first, HALF, first)
+                cast(1, 0, t0, first, HALF, first)
         quant_w(1, 0, 0)
         mm1(0, 1)
         mm1(1, 1)
@@ -295,20 +302,20 @@ def tile_list_pair_spread_positions_kernel(
             )
         w2sb = w2s[:].rearrange("p a c -> p (a c)").bitcast(U8)
 
-        group_tile(0, 1, 0, "grp102")
-        group_tile(0, 1, 2)
-        group_tile(1, 1, 0)
-        group_tile(1, 1, 2)
-        cast("pool", 0, 1, 0, 512, 512, 512)
-        cast("pool", 0, 1, 2, 512, 512, 512)
-        cast("pool", 1, 1, 0, 512, 512, 512)
-        cast("pool", 1, 1, 2, 512, 512, 512)
+        wide = [sb("wide0", [P, 4, P, 4], BF16, "late0"), sb("wide1", [P, 4, P, 4], BF16, "third")]
+        for a in range(2):
+            for t0 in (0, 2):
+                grp[a, 1, t0] = wide[a][:, t0 : t0 + 2]
+        cast_half("pool", 0, 0)
+        cast_half("pool", 0, 1)
+        cast_half("pool", 1, 0)
         for u in range(1, 4):
             evac(u)
         for u in range(4):
             pick2(u)
+        cast_half("act", 1, 1)
         quant_w(0, 1, 0, "raw1_512")
-        quant_w(1, 1, 0, "raw1_512", 4096)
+        quant_w(1, 1, 0)
         mm1(4, 0)
         mm1(4, 1)
         mm1(5, 0)
@@ -319,10 +326,10 @@ def tile_list_pair_spread_positions_kernel(
         mm1(6, 1)
         mm1(7, 0)
         mm1(7, 1)
-        pick1(0, "grp010")
-        pick1(1, "raw1_512", 2048)
-        pick1(2, "grp110")
-        magnitude(0, 2, "third")
+        pick1(0, "raw1_512", 2048)
+        pick1(1, "wide0")
+        pick1(2, "wide0", 2048)
+        magnitude(0, 2, "raw1_512", 4096)
         magnitude(2, 2, "raw0_512")
         inv_root(0, 2)
         inv_root(2, 1)

@@ -56,20 +56,22 @@ def tile_list_pair_spread_positions_kernel(
         pos2_t = lists.tile([P, NP // 16], U16, name="pos2_t")
 
         tabs = sb("tabs", [P, T // 4], I32)
-        h = [sb("h%d" % i, [P, 2 * S], F32) for i in range(WINDOWS)]
         room("second", 8 * T)
-        one = sb("one", [P, 1], F32, "second")
-        warm = sb("warm", [P, 1], F32, "second", 4 * T)
-        zero = sb("zero", [P, 1], F32, "second", 6 * T)
+        h = {i: sb("h%d" % i, [P, 2 * S], F32) for i in (2, 3, 0, 1)}
+        one = sb("one", [P, 32], F32, "second", 4 * T - 64)
+        zero = sb("zero", [P, 32], F32, "h2", -64)
+        warm = sb("warm", [P, 1], F32, "h3")
 
         nc.vector.memset(tabs[:], 0)
         nc.vector.memset(one[:], 1.0)
         nc.vector.memset(zero[:], 0.0)
-        for i in range(WINDOWS):
+        for i in range(2):
             nc.vector.memset(h[i][:, S : 2 * S], 0.0)
         for q in range(4):
             nc.scalar.dma_start(tabs[32 * q : 32 * q + 8, :], tab_scales[:, 4 * q : 4 * q + 4, :].bitcast(I32))
-        nc.scalar.activation(warm[:], one[:], ACT.Abs_reciprocal_sqrt, bias=zero[:])
+        nc.scalar.activation(warm[:], one[:, 0:1], ACT.Abs_reciprocal_sqrt, bias=zero[:, 0:1])
+        for i in range(2, WINDOWS):
+            nc.gpsimd.memset(h[i][:, S : 2 * S], 0.0)
 
         tabw, raw = {}, {}
 
@@ -83,8 +85,10 @@ def tile_list_pair_spread_positions_kernel(
             nc.sync.dma_start(raw[a, first][:], src.rearrange("(p j) c -> p j c", j=4))
 
         nc.sync.dma_start(offs_t[:], offs)
-        load_tab(0)
-        load_w1(0, 0, 512)
+        room("first", 4 * T + 1024)
+        load_tab(0, "first")
+        room("early", 3 * 4096)
+        load_w1(0, 0, 512, "early", 4096 - 64)
         nc.sync.dma_start(pos2_t[:], pos2)
         nc.sync.dma_start(pos1_t[:], pos1)
         load_tab(1, "second")
@@ -92,23 +96,17 @@ def tile_list_pair_spread_positions_kernel(
         load_w1(1, HALF, HALF, "second", 6 * T)
 
         vs = sb("vs", [P, S], U8)
-        vw = [sb("vw%d" % a, [P, S], U32) for a in range(2)]
+        vw = [sb("vw0", [P, S], U32)]
         nc.vector.tensor_copy(vs[:], tabs[:].bitcast(U8).indirect(offs_t[:]))
         nc.vector.tensor_copy(vw[0][:], tabw[0][:].bitcast(U32).indirect(offs_t[:]))
-        load_w1(0, 512, 512, "tabw0")
+        load_w1(0, 512, 512, "first", 1024)
 
-        grp, wc, ws = {}, {}, {}
+        wide, wc, ws = {}, {}, {}
 
-        def cast(a, b, t0, first, width, base):
-            lo = (first - 512 * b) // 4
-            dst = grp[a, b, t0][:, :, lo : lo + width // 4, :].rearrange("p t m j -> p m j t")
-            src = raw[a, base][:, :, first - base : first - base + width]
-            src = src.rearrange("p j (m t) -> p m j t", t=4)[:, :, :, t0 : t0 + 2]
-            nc.scalar.copy(dst, src)
-
-        def cast_half(engine, a, half):
-            dst = wide[a][:, :, 64 * half : 64 * (half + 1), :]
-            src = raw[a, 512][:, :, HALF * half : HALF * (half + 1)]
+        def cast(engine, a, b, base, first, count):
+            dst = wide[a, b][:, :, first : first + count, :]
+            lo = 512 * b + 4 * first - base
+            src = raw[a, base][:, :, lo : lo + 4 * count]
             if engine == "pool":
                 dst = dst.rearrange("p t m j -> p m t j")
                 src = src.rearrange("p j (m t) -> p m t j", t=4)
@@ -116,8 +114,8 @@ def tile_list_pair_spread_positions_kernel(
             else:
                 nc.scalar.copy(dst.rearrange("p t m j -> p m j t"), src.rearrange("p j (m t) -> p m j t", t=4))
 
-        def group_tile(a, b, t0, over="", at=0):
-            grp[a, b, t0] = sb("grp%d%d%d" % (a, b, t0), [P, 2, P, 4], BF16, over, at)[:]
+        def wide_tile(a, b, over="", at=0):
+            wide[a, b] = sb("wide%d%d" % (a, b), [P, 4, P, 4], BF16, over, at)
 
         def quant_w(a, b, t0, over="", at=0):
             codes = sb("wc%d%d%d" % (a, b, t0), [P, 2 * P], U32, over, at)
@@ -125,7 +123,7 @@ def tile_list_pair_spread_positions_kernel(
             nc.vector.quantize_mx(
                 out=codes[:].bitcast(FP8X4),
                 scales=scales[:],
-                in_=grp[a, b, t0].rearrange("p t m j -> p (t m j)"),
+                in_=wide[a, b][:, t0 : t0 + 2].rearrange("p t m j -> p (t m j)"),
             )
             for t in range(2):
                 wc[a, b, t0 + t] = codes[:, P * t : P * (t + 1)]
@@ -265,32 +263,32 @@ def tile_list_pair_spread_positions_kernel(
         def chunk(c):
             return slice(CH * c, CH * (c + 1))
 
-        for t0 in (0, 2):
-            group_tile(0, 0, t0)
-            cast(0, 0, t0, 0, 512, 0)
+        wide_tile(0, 0)
+        cast("act", 0, 0, 0, 0, 64)
+        cast("pool", 0, 0, 0, 64, 64)
         quant_w(0, 0, 0)
         mm1(0, 0)
         mm1(1, 0)
+        vw.append(sb("vw1", [P, S], U32, "early"))
         nc.vector.tensor_copy(vw[1][:], tabw[1][:].bitcast(U32).indirect(offs_t[:]))
-        load_w1(1, 512, 512, "raw0_0")
+        load_w1(1, 512, 512, "early", 4096)
         w2w = sb("w2w", [P, 2, N // 2], I32, "tabw1")
         nc.sync.dma_start(w2w[:], w2_words.rearrange("a p c -> p a c").bitcast(I32))
         w2c = w2w[:].rearrange("p a c -> p (a c)").bitcast(U8)
         g = sb("g", [P, 2, 4], F32, "tabw1", 4096)
         nc.sync.dma_start(g[:], gain.rearrange("(b p t) -> p b t", b=2, t=4))
-        w2s = sb("w2s", [P, 2, N // 4], I32, "tabs")
+        w2s = sb("w2s", [P, 2, N // 4], I32, "first")
         nc.gpsimd.memset(w2s[:], 0)
-        room("late0", 4096)
-        for t0 in (0, 2):
-            group_tile(1, 0, t0, "late0" if t0 else "")
-            for first in (0, HALF):
-                cast(1, 0, t0, first, HALF, first)
+        wide_tile(1, 0)
+        cast("act", 1, 0, 0, 0, 64)
+        cast("act", 1, 0, HALF, 64, 32)
+        cast("pool", 1, 0, HALF, 96, 32)
         quant_w(1, 0, 0)
         mm1(0, 1)
         mm1(1, 1)
-        quant_w(0, 0, 2, "grp100")
-        room("third", 4096)
-        quant_w(1, 0, 2, "third")
+        quant_w(0, 0, 2, "raw1_256")
+        room("third", 8192)
+        quant_w(1, 0, 2, "third", 4096 - 512)
         evac(0, shared=True)
         for u in (2, 3):
             mm1(u, 0)
@@ -302,18 +300,17 @@ def tile_list_pair_spread_positions_kernel(
             )
         w2sb = w2s[:].rearrange("p a c -> p (a c)").bitcast(U8)
 
-        wide = [sb("wide0", [P, 4, P, 4], BF16, "late0"), sb("wide1", [P, 4, P, 4], BF16, "third")]
-        for a in range(2):
-            for t0 in (0, 2):
-                grp[a, 1, t0] = wide[a][:, t0 : t0 + 2]
-        cast_half("pool", 0, 0)
-        cast_half("pool", 0, 1)
-        cast_half("pool", 1, 0)
+        wide_tile(0, 1, "wide10")
+        wide_tile(1, 1, "third", 4096)
+        cast("pool", 0, 1, 512, 0, 64)
+        cast("pool", 0, 1, 512, 64, 64)
+        cast("pool", 1, 1, 512, 0, 64)
+        cast("pool", 1, 1, 512, 64, 32)
         for u in range(1, 4):
             evac(u)
         for u in range(4):
             pick2(u)
-        cast_half("act", 1, 1)
+        cast("act", 1, 1, 512, 96, 32)
         quant_w(0, 1, 0, "raw1_512")
         quant_w(1, 1, 0)
         mm1(4, 0)
@@ -327,9 +324,9 @@ def tile_list_pair_spread_positions_kernel(
         mm1(7, 0)
         mm1(7, 1)
         pick1(0, "raw1_512", 2048)
-        pick1(1, "wide0")
-        pick1(2, "wide0", 2048)
-        magnitude(0, 2, "raw1_512", 4096)
+        pick1(1, "wide01")
+        pick1(2, "wide01", 2048)
+        magnitude(0, 2, "third")
         magnitude(2, 2, "raw0_512")
         inv_root(0, 2)
         inv_root(2, 1)

@@ -55,22 +55,20 @@ def tile_list_pair_spread_positions_kernel(
         pos1_t = lists.tile([P, NP // 16], U16, name="pos1_t")
         pos2_t = lists.tile([P, NP // 16], U16, name="pos2_t")
 
-        tabs = sb("tabs", [P, T // 4], I32)
-        room("second", 8 * T)
-        h = {i: sb("h%d" % i, [P, 2 * S], F32) for i in (2, 3, 0, 1)}
-        one = sb("one", [P, 32], F32, "second", 4 * T - 64)
-        zero = sb("zero", [P, 32], F32, "h2", -64)
-        warm = sb("warm", [P, 1], F32, "h3")
+        room("early", 1024 + 3 * 4096)
+        tabs = sb("tabs", [P, T // 4], I32, "early")
+        h = [sb("h%d" % i, [P, 2 * S], F32) for i in range(WINDOWS)]
+        one = sb("one", [P, 32], F32, "h1", -64)
+        zero = sb("zero", [P, 32], F32, "h3", -64)
+        warm = sb("warm", [P, 1], F32)
 
-        nc.vector.memset(tabs[:], 0)
+        nc.gpsimd.memset(tabs[:], 0)
         nc.vector.memset(one[:], 1.0)
         nc.vector.memset(zero[:], 0.0)
-        for i in range(2):
-            nc.vector.memset(h[i][:, S : 2 * S], 0.0)
         for q in range(4):
-            nc.scalar.dma_start(tabs[32 * q : 32 * q + 8, :], tab_scales[:, 4 * q : 4 * q + 4, :].bitcast(I32))
+            nc.gpsimd.dma_start(tabs[32 * q : 32 * q + 8, :], tab_scales[:, 4 * q : 4 * q + 4, :].bitcast(I32))
         nc.scalar.activation(warm[:], one[:, 0:1], ACT.Abs_reciprocal_sqrt, bias=zero[:, 0:1])
-        for i in range(2, WINDOWS):
+        for i in range(WINDOWS):
             nc.gpsimd.memset(h[i][:, S : 2 * S], 0.0)
 
         tabw, raw = {}, {}
@@ -87,13 +85,12 @@ def tile_list_pair_spread_positions_kernel(
         nc.sync.dma_start(offs_t[:], offs)
         room("first", 4 * T + 1024)
         load_tab(0, "first")
-        room("early", 3 * 4096)
-        load_w1(0, 0, 512, "early", 4096 - 64)
+        load_w1(0, 0, 512, "early", 1024 + 4096 - 64)
         nc.sync.dma_start(pos2_t[:], pos2)
         nc.sync.dma_start(pos1_t[:], pos1)
-        load_tab(1, "second")
-        load_w1(1, 0, HALF, "second", 4 * T)
-        load_w1(1, HALF, HALF, "second", 6 * T)
+        load_tab(1)
+        load_w1(1, 0, HALF)
+        load_w1(1, HALF, HALF)
 
         vs = sb("vs", [P, S], U8)
         vw = [sb("vw0", [P, S], U32)]
@@ -266,12 +263,12 @@ def tile_list_pair_spread_positions_kernel(
         wide_tile(0, 0)
         cast("act", 0, 0, 0, 0, 64)
         cast("pool", 0, 0, 0, 64, 64)
-        quant_w(0, 0, 0)
+        quant_w(0, 0, 0, "early")
         mm1(0, 0)
         mm1(1, 0)
-        vw.append(sb("vw1", [P, S], U32, "early"))
+        vw.append(sb("vw1", [P, S], U32, "early", 1024))
         nc.vector.tensor_copy(vw[1][:], tabw[1][:].bitcast(U32).indirect(offs_t[:]))
-        load_w1(1, 512, 512, "early", 4096)
+        load_w1(1, 512, 512, "early", 1024 + 4096)
         w2w = sb("w2w", [P, 2, N // 2], I32, "tabw1")
         nc.sync.dma_start(w2w[:], w2_words.rearrange("a p c -> p a c").bitcast(I32))
         w2c = w2w[:].rearrange("p a c -> p (a c)").bitcast(U8)

@@ -58,17 +58,20 @@ def tile_list_pair_spread_positions_kernel(
         room("early", 1024 + 3 * 4096)
         tabs = sb("tabs", [P, T // 4], I32, "early")
         h = [sb("h%d" % i, [P, 2 * S], F32) for i in range(WINDOWS)]
-        one = sb("one", [P, 32], F32, "h1", -64)
+        one = sb("one", [P, 1], F32)
         zero = sb("zero", [P, 32], F32, "h3", -64)
         warm = sb("warm", [P, 1], F32)
 
         nc.gpsimd.memset(tabs[:], 0)
         nc.vector.memset(one[:], 1.0)
-        nc.vector.memset(zero[:], 0.0)
+        nc.vector.memset(zero[:, 0:1], 0.0)
         for q in range(4):
             nc.gpsimd.dma_start(tabs[32 * q : 32 * q + 8, :], tab_scales[:, 4 * q : 4 * q + 4, :].bitcast(I32))
         nc.scalar.activation(warm[:], one[:, 0:1], ACT.Abs_reciprocal_sqrt, bias=zero[:, 0:1])
-        for i in range(WINDOWS):
+        for i in range(2):
+            nc.vector.memset(h[i][:, S : 2 * S - 1], 0.0)
+            nc.vector.memset(h[i][:, 2 * S - 1 : 2 * S], 0.0)
+        for i in range(2, WINDOWS):
             nc.gpsimd.memset(h[i][:, S : 2 * S], 0.0)
 
         tabw, raw = {}, {}
@@ -114,15 +117,15 @@ def tile_list_pair_spread_positions_kernel(
         def wide_tile(a, b, over="", at=0):
             wide[a, b] = sb("wide%d%d" % (a, b), [P, 4, P, 4], BF16, over, at)
 
-        def quant_w(a, b, t0, over="", at=0):
-            codes = sb("wc%d%d%d" % (a, b, t0), [P, 2 * P], U32, over, at)
-            scales = sb("ws%d%d%d" % (a, b, t0), [P, 2 * P], U8)
+        def quant_w(a, b, t0, over="", at=0, count=2):
+            codes = sb("wc%d%d%d" % (a, b, t0), [P, count * P], U32, over, at)
+            scales = sb("ws%d%d%d" % (a, b, t0), [P, count * P], U8)
             nc.vector.quantize_mx(
                 out=codes[:].bitcast(FP8X4),
                 scales=scales[:],
-                in_=wide[a, b][:, t0 : t0 + 2].rearrange("p t m j -> p (t m j)"),
+                in_=wide[a, b][:, t0 : t0 + count].rearrange("p t m j -> p (t m j)"),
             )
-            for t in range(2):
+            for t in range(count):
                 wc[a, b, t0 + t] = codes[:, P * t : P * (t + 1)]
                 ws[a, b, t0 + t] = scales[:, P * t : P * (t + 1)]
 
@@ -280,8 +283,9 @@ def tile_list_pair_spread_positions_kernel(
         cast("act", 1, 0, 0, 0, 64)
         cast("act", 1, 0, HALF, 64, 32)
         cast("pool", 1, 0, HALF, 96, 32)
-        quant_w(1, 0, 0)
+        quant_w(1, 0, 0, count=1)
         mm1(0, 1)
+        quant_w(1, 0, 1, count=1)
         mm1(1, 1)
         quant_w(0, 0, 2, "raw1_256")
         room("third", 8192)

@@ -20,7 +20,7 @@ WIDTH = {F32: 4, I32: 4, U32: 4, BF16: 2, U8: 1}
 P = 128
 CH = 128
 HALF = 256
-WINDOWS = 4
+WINDOWS = 6
 
 
 def tile_list_pair_spread_positions_kernel(
@@ -55,29 +55,25 @@ def tile_list_pair_spread_positions_kernel(
         pos1_t = lists.tile([P, NP // 16], U16, name="pos1_t")
         pos2_t = lists.tile([P, NP // 16], U16, name="pos2_t")
 
-        room("early", 1024 + 3 * 4096)
-        tabs = sb("tabs", [P, T // 4], I32, "early")
+        room("first", 4 * 4 * 512)
+        rows = sb("rows", [P, T // 4], I32, "first")
+        planes = sb("planes", [P, 2 * S // 4], I32)
         h = [sb("h%d" % i, [P, 2 * S], F32) for i in range(WINDOWS)]
         one = sb("one", [P, 1], F32)
-        zero = sb("zero", [P, 32], F32, "h3", -64)
         warm = sb("warm", [P, 1], F32)
 
-        nc.gpsimd.memset(tabs[:], 0)
         nc.vector.memset(one[:], 1.0)
-        nc.vector.memset(zero[:, 0:1], 0.0)
-        for q in range(4):
-            nc.gpsimd.dma_start(tabs[32 * q : 32 * q + 8, :], tab_scales[:, 4 * q : 4 * q + 4, :].bitcast(I32))
-        nc.scalar.activation(warm[:], one[:, 0:1], ACT.Abs_reciprocal_sqrt, bias=zero[:, 0:1])
-        for i in range(2):
-            nc.vector.memset(h[i][:, S : 2 * S - 1], 0.0)
-            nc.vector.memset(h[i][:, 2 * S - 1 : 2 * S], 0.0)
-        for i in range(2, WINDOWS):
+        nc.gpsimd.memset(rows[32:64, :], 0)
+        nc.gpsimd.memset(rows[64:128, :], 0)
+        nc.vector.memset(planes[:], 0)
+        nc.scalar.activation(warm[:], one[:, 0:1], ACT.Abs_reciprocal_sqrt, bias=1.0)
+        for i in range(WINDOWS):
             nc.gpsimd.memset(h[i][:, S : 2 * S], 0.0)
 
         tabw, raw = {}, {}
 
-        def load_tab(a, over="", at=0):
-            tabw[a] = sb("tabw%d" % a, [P, T], I32, over, at)
+        def load_tab(a, over=""):
+            tabw[a] = sb("tabw%d" % a, [P, T], I32, over)
             nc.sync.dma_start(tabw[a][:], tab_words[a].rearrange("p t i -> p (t i)").bitcast(I32))
 
         def load_w1(a, first, width, over="", at=0):
@@ -86,36 +82,52 @@ def tile_list_pair_spread_positions_kernel(
             nc.sync.dma_start(raw[a, first][:], src.rearrange("(p j) c -> p j c", j=4))
 
         nc.sync.dma_start(offs_t[:], offs)
-        room("first", 4 * T + 1024)
-        load_tab(0, "first")
-        load_w1(0, 0, 512, "early", 1024 + 4096 - 64)
+        nc.sync.dma_start(rows[0:32, :], tab_scales.rearrange("a q t -> (a q) t").bitcast(I32))
+        load_tab(0)
+        load_w1(0, 0, 512)
         nc.sync.dma_start(pos2_t[:], pos2)
         nc.sync.dma_start(pos1_t[:], pos1)
-        load_tab(1)
-        load_w1(1, 0, HALF)
-        load_w1(1, HALF, HALF)
 
-        vs = sb("vs", [P, S], U8)
-        vw = [sb("vw0", [P, S], U32)]
-        nc.vector.tensor_copy(vs[:], tabs[:].bitcast(U8).indirect(offs_t[:]))
+        picked = sb("picked", [P, S // 4], I32)
+        vw = [sb("vw%d" % a, [P, S], U32) for a in range(2)]
+        nc.vector.tensor_copy(picked[:].bitcast(U8), rows[:].bitcast(U8).indirect(offs_t[:]))
         nc.vector.tensor_copy(vw[0][:], tabw[0][:].bitcast(U32).indirect(offs_t[:]))
-        load_w1(0, 512, 512, "first", 1024)
+
+        def place_rows(a):
+            for q in range(4):
+                nc.sync.dma_start(
+                    planes[32 * q : 32 * q + 4, S // 4 * a : S // 4 * (a + 1)],
+                    picked[16 * a + 4 * q : 16 * a + 4 * q + 4, :],
+                )
+
+        vs = planes[:].bitcast(U8)
+        place_rows(0)
+        load_tab(1, "first")
+        place_rows(1)
+        load_w1(1, 0, HALF, "tabw0")
+        load_w1(1, HALF, HALF, "tabw0", 4096)
+        load_w1(0, 512, 512, "raw0_0")
 
         wide, wc, ws = {}, {}, {}
 
-        def cast(engine, a, b, base, first, count):
-            dst = wide[a, b][:, :, first : first + count, :]
+        def cast(engine, a, b, base, first, count, slots=slice(0, 4)):
+            dst = wide[a, b][:, slots, first : first + count, :]
             lo = 512 * b + 4 * first - base
-            src = raw[a, base][:, :, lo : lo + 4 * count]
+            src = raw[a, base][:, :, lo : lo + 4 * count].rearrange("p j (m t) -> p j m t", t=4)[:, :, :, slots]
             if engine == "pool":
                 dst = dst.rearrange("p t m j -> p m t j")
-                src = src.rearrange("p j (m t) -> p m t j", t=4)
+                src = src.rearrange("p j m t -> p m t j")
                 nc.gpsimd.tensor_scalar(dst, src, 1.0, 0.0, ALU.mult, ALU.add)
+                return
+            dst = dst.rearrange("p t m j -> p m j t")
+            src = src.rearrange("p j m t -> p m j t")
+            if engine == "act":
+                nc.scalar.copy(dst, src)
             else:
-                nc.scalar.copy(dst.rearrange("p t m j -> p m j t"), src.rearrange("p j (m t) -> p m j t", t=4))
+                nc.vector.tensor_copy(dst, src)
 
-        def wide_tile(a, b, over="", at=0):
-            wide[a, b] = sb("wide%d%d" % (a, b), [P, 4, P, 4], BF16, over, at)
+        def wide_tile(a, b, over=""):
+            wide[a, b] = sb("wide%d%d" % (a, b), [P, 4, P, 4], BF16, over)
 
         def quant_w(a, b, t0, over="", at=0, count=2):
             codes = sb("wc%d%d%d" % (a, b, t0), [P, count * P], U32, over, at)
@@ -136,81 +148,164 @@ def tile_list_pair_spread_positions_kernel(
             for half in range(2):
                 if a == 0:
                     hps[u, half] = bank(2 * t + half)
-                span = slice(512 * half, 512 * (half + 1))
                 nc.tensor.matmul_mx(
                     out=hps[u, half][:],
                     lhsT=wc[a, b, t].bitcast(FP8X4),
                     lhsT_scale=ws[a, b, t],
-                    rhs=vw[a][:, span].bitcast(FP8X4),
-                    rhs_scale=vs[4 * a :, span],
+                    rhs=vw[a][:, 512 * half : 512 * (half + 1)].bitcast(FP8X4),
+                    rhs_scale=vs[:, S * a + 512 * half : S * a + 512 * (half + 1)],
                     start=(a == 0),
                     stop=(a == 1),
                 )
 
         def evac(u, shared=False):
-            nc.scalar.copy(h[u % WINDOWS][:, 0:512], hps[u, 0][:])
             if shared:
-                nc.vector.tensor_copy(h[u % WINDOWS][:, 512:1024], hps[u, 1][:])
+                nc.vector.tensor_copy(h[u % WINDOWS][:, 0:512], hps[u, 0][:])
             else:
-                nc.scalar.copy(h[u % WINDOWS][:, 512:1024], hps[u, 1][:])
+                nc.scalar.copy(h[u % WINDOWS][:, 0:512], hps[u, 0][:])
+            nc.scalar.copy(h[u % WINDOWS][:, 512:1024], hps[u, 1][:])
 
-        leg2 = {}
-        left = [sb("left%d" % b, [P, 4, NP], F32) for b in range(2)]
-        right = [sb("right%d" % b, [P, 4, NP], F32) for b in range(2)]
-        num, mag, root, inv = {}, {}, {}, {}
+        room("factors", 8192)
+        legs = {0: sb("legs0", [P, 2, NP], F32), 1: sb("legs1", [P, 2, NP], F32, "factors")}
+        legs[2] = sb("legs2", [P, 2, NP], F32)
+        legs[3] = sb("legs3", [P, 2, NP], F32)
+        left, right, num = {}, {}, {}
 
-        legs = [sb("legs%d" % i, [P, 2, NP], F32) for i in range(4)]
+        def second_leg(u):
+            nc.vector.tensor_scalar(
+                legs[u // 2][:, u % 2, :], h[u % WINDOWS][:].indirect(pos2_t[:]), -1.5, 0.0, ALU.mult, ALU.add
+            )
 
-        def pick2(u):
-            leg2[u] = legs[u // 2][:, u % 2, :]
-            nc.vector.tensor_scalar(leg2[u], h[u % WINDOWS][:].indirect(pos2_t[:]), -1.5, 0.0, ALU.mult, ALU.add)
+        def first_leg(u, dst):
+            nc.vector.tensor_tensor(dst, h[u % WINDOWS][:].indirect(pos1_t[:]), legs[u // 2][:, u % 2, :], ALU.add)
 
-        def pick1(u, over="", at=0):
-            num[u] = sb("num%d" % u, [P, NP], F32, over, at)
-            nc.vector.tensor_tensor(num[u][:], h[u % WINDOWS][:].indirect(pos1_t[:]), leg2[u], ALU.add)
+        def magnitude(pair, dst):
+            nc.scalar.activation(dst, legs[pair][:], ACT.Abs)
 
-        def pick1_direct(u):
-            nc.vector.tensor_tensor(left[1][:, u - 4, :], h[u % WINDOWS][:].indirect(pos1_t[:]), leg2[u], ALU.add)
+        def inv_root(dst, src):
+            nc.scalar.activation(dst, src, ACT.Abs_reciprocal_sqrt, bias=1.0, scale=1.0 / 1.5)
 
-        def magnitude_in_left(u):
-            nc.scalar.activation(left[1][:, u - 4, :], leg2[u], ACT.Abs)
+        def pair_tile(name, over="", at=0):
+            return sb(name, [P, 2, NP], F32, over, at)
 
-        def inv_root_from_left(u):
-            root[u] = sb("root%d" % u, [P, NP], F32)
-            nc.scalar.activation(root[u][:], left[1][:, u - 4, :], ACT.Abs_reciprocal_sqrt, bias=1.0, scale=1.0 / 1.5)
+        wide_tile(0, 0)
+        low, high = slice(0, 2), slice(2, 4)
+        cast("dve", 0, 0, 0, 0, 128, low)
+        cast("act", 0, 0, 0, 0, 128, high)
+        quant_w(0, 0, 0)
+        mm1(0, 0)
+        mm1(1, 0)
+        quant_w(0, 0, 2)
+        mm1(2, 0)
+        mm1(3, 0)
+        nc.vector.tensor_copy(vw[1][:], tabw[1][:].bitcast(U32).indirect(offs_t[:]))
+        load_w1(1, 512, 512, "first")
+        wide_tile(1, 0)
+        cast("act", 1, 0, 0, 0, 64, low)
+        cast("act", 1, 0, 0, 0, 64, high)
+        cast("dve", 1, 0, HALF, 64, 64, low)
+        cast("act", 1, 0, HALF, 64, 64, high)
+        quant_w(1, 0, 0, count=1)
+        mm1(0, 1)
+        quant_w(1, 0, 1, count=1)
+        mm1(1, 1)
+        room("third", 4096)
+        quant_w(1, 0, 2, "third")
+        evac(0, shared=True)
+        mm1(2, 1)
+        mm1(3, 1)
 
-        def square_apart(u):
-            inv[u] = sb("inv%d" % u, [P, NP], F32)
-            nc.scalar.activation(inv[u][:], root[u][:], ACT.Square)
+        w2w = sb("w2w", [P, 2, N // 2], I32, "wide00")
+        nc.sync.dma_start(w2w[:], w2_words.rearrange("a p c -> p a c").bitcast(I32))
+        w2c = w2w[:].rearrange("p a c -> p (a c)").bitcast(U8)
+        g = sb("g", [P, 2, 4], F32, "wide00", 2048)
+        nc.sync.dma_start(g[:], gain.rearrange("(b p t) -> p b t", b=2, t=4))
+        w2s = sb("w2s", [P, 2, N // 4], I32, "wide10")
+        nc.vector.memset(w2s[:], 0)
+        for q in range(4):
+            nc.sync.dma_start(
+                w2s[32 * q : 32 * q + 4, :, :],
+                w2_scales[:, 4 * q : 4 * q + 4, :].rearrange("a r n -> r a n").bitcast(I32),
+            )
+        w2sb = w2s[:].rearrange("p a c -> p (a c)").bitcast(U8)
 
-        def gain_inv(u):
-            nc.scalar.activation(right[1][:, u - 4, :], inv[u][:], ACT.Copy, scale=g[:, 1, u - 4 : u - 3])
+        wide_tile(0, 1)
+        room("late", 8192)
+        wide_tile(1, 1, "late")
+        cast("pool", 0, 1, 512, 0, 64)
+        cast("pool", 0, 1, 512, 64, 64)
+        cast("pool", 1, 1, 512, 0, 64)
+        cast("pool", 1, 1, 512, 64, 32)
+        for u in range(1, 4):
+            evac(u)
+        for u in range(4):
+            second_leg(u)
+        cast("dve", 1, 1, 512, 96, 32)
+        quant_w(0, 1, 0, "first")
+        quant_w(1, 1, 0)
+        mm1(4, 0)
+        mm1(4, 1)
+        mm1(5, 0)
+        mm1(5, 1)
+        quant_w(0, 1, 2, "first", 1024)
+        quant_w(1, 1, 2)
+        mm1(6, 0)
+        mm1(6, 1)
+        mm1(7, 0)
+        mm1(7, 1)
+        right[0] = sb("right0", [P, 4, NP], F32, "late")
+        num[0] = sb("num0", [P, NP], F32, "first", 2048)[:]
+        num[1] = sb("num1", [P, NP], F32, "wide01")[:]
+        num[2], num[3] = right[0][:, 2, :], right[0][:, 3, :]
+        for u in range(4):
+            first_leg(u, num[u])
 
-        def magnitude(u, count, over="", at=0):
-            tile = sb("mag%d" % u, [P, count, NP], F32, over, at)
-            nc.scalar.activation(tile[:], legs[u // 2][:, u % 2 : u % 2 + count, :], ACT.Abs)
-            for i in range(count):
-                mag[u + i] = (tile, i)
+        mag01, mag23 = pair_tile("mag01", "third"), pair_tile("mag23")
+        left[1] = sb("left1", [P, 4, NP], F32)
+        magnitude(0, mag01[:])
+        magnitude(1, mag23[:])
+        inv_root(right[0][:, 0:2, :], mag01[:])
+        inv_root(left[1][:, 2:4, :], mag23[:])
+        nc.scalar.activation(right[0][:, 1, :], right[0][:, 1, :], ACT.Square)
+        for u in range(4, 8):
+            evac(u)
+        for u in range(4, 8):
+            second_leg(u)
 
-        def inv_root(u, count, over="", at=0):
-            tile, i = mag[u]
-            root[u] = sb("root%d" % u, [P, count, NP], F32, over, at)
-            nc.scalar.activation(root[u][:], tile[:, i : i + count, :], ACT.Abs_reciprocal_sqrt, bias=1.0, scale=1.0 / 1.5)
+        left[0] = sb("left0", [P, 4, NP], F32, "factors")
+        for t in (2, 3, 1):
+            nc.gpsimd.tensor_scalar(left[0][:, t, :], num[t], g[:, 0, t : t + 1], 0.0, ALU.mult, ALU.add)
+        nc.gpsimd.tensor_scalar(left[0][:, 0, :], num[0], g[:, 0, 0:1], 0.0, ALU.mult, ALU.add)
+        nc.gpsimd.tensor_tensor(left[0][:, 0, :], left[0][:, 0, :], right[0][:, 0, :], ALU.mult)
 
-        def square(u, count):
-            b, t = divmod(u, 4)
-            nc.scalar.activation(right[b][:, t : t + count, :], root[u][:], ACT.Square)
+        right[1] = sb("right1", [P, 4, NP], F32)
+        inv45, inv67 = pair_tile("inv45"), pair_tile("inv67")
+        mag67, root67 = pair_tile("mag67", "mag23"), pair_tile("root67")
+        root45 = pair_tile("root45", "third")
+        nc.scalar.activation(right[0][:, 2:4, :], left[1][:, 2:4, :], ACT.Square)
+        magnitude(2, left[1][:, 0:2, :])
+        inv_root(root45[:], left[1][:, 0:2, :])
+        magnitude(3, mag67[:])
+        nc.scalar.activation(inv45[:], root45[:], ACT.Square)
+        inv_root(root67[:], mag67[:])
 
-        def gain_num(u, engine):
-            b, t = divmod(u, 4)
-            engine.tensor_scalar(left[b][:, t, :], num[u][:], g[:, b, t : t + 1], 0.0, ALU.mult, ALU.add)
+        def gain_inv(t, src):
+            nc.scalar.activation(right[1][:, t, :], src, ACT.Copy, scale=g[:, 1, t : t + 1])
+
+        gain_inv(0, inv45[:, 0, :])
+        nc.scalar.activation(inv67[:], root67[:], ACT.Square)
+        gain_inv(1, inv45[:, 1, :])
+        gain_inv(2, inv67[:, 0, :])
+        gain_inv(3, inv67[:, 1, :])
+        for u in range(4, 8):
+            first_leg(u, left[1][:, u - 4, :])
 
         zb = {}
-        zc = {1: sb("zc1", [P, NP], U32)}
+        zc = [sb("zc%d" % b, [P, NP], U32) for b in range(2)]
         zs = [sb("zs%d" % b, [P, NP], U8) for b in range(2)]
 
-        def make_z(b, cols, over="", at=0):
-            zb[b, cols.start] = sb("zb%d_%d" % (b, cols.start), [P, cols.stop - cols.start, 4], BF16, over, at)
+        def make_z(b, cols):
+            zb[b, cols.start] = sb("zb%d_%d" % (b, cols.start), [P, cols.stop - cols.start, 4], BF16)
             nc.vector.tensor_tensor(
                 zb[b, cols.start][:].rearrange("p (c i) t -> p c t i", i=2),
                 left[b][:, :, cols].rearrange("p t (c i) -> p c t i", i=2),
@@ -219,12 +314,10 @@ def tile_list_pair_spread_positions_kernel(
             )
 
         def quant_z(b, cols):
-            first = max(start for group, start in zb if group == b and start <= cols.start)
-            source = zb[b, first][:, cols.start - first : cols.stop - first, :]
             nc.vector.quantize_mx(
                 out=zc[b][:, cols].bitcast(FP8X4),
                 scales=zs[b][:, cols],
-                in_=source.rearrange("p c t -> p (c t)"),
+                in_=zb[b, cols.start][:].rearrange("p c t -> p (c t)"),
             )
 
         acc = {}
@@ -263,129 +356,19 @@ def tile_list_pair_spread_positions_kernel(
         def chunk(c):
             return slice(CH * c, CH * (c + 1))
 
-        wide_tile(0, 0)
-        cast("act", 0, 0, 0, 0, 64)
-        cast("pool", 0, 0, 0, 64, 64)
-        quant_w(0, 0, 0, "early")
-        mm1(0, 0)
-        mm1(1, 0)
-        vw.append(sb("vw1", [P, S], U32, "early", 1024))
-        nc.vector.tensor_copy(vw[1][:], tabw[1][:].bitcast(U32).indirect(offs_t[:]))
-        load_w1(1, 512, 512, "early", 1024 + 4096)
-        w2w = sb("w2w", [P, 2, N // 2], I32, "tabw1")
-        nc.sync.dma_start(w2w[:], w2_words.rearrange("a p c -> p a c").bitcast(I32))
-        w2c = w2w[:].rearrange("p a c -> p (a c)").bitcast(U8)
-        g = sb("g", [P, 2, 4], F32, "tabw1", 4096)
-        nc.sync.dma_start(g[:], gain.rearrange("(b p t) -> p b t", b=2, t=4))
-        w2s = sb("w2s", [P, 2, N // 4], I32, "first")
-        nc.gpsimd.memset(w2s[:], 0)
-        wide_tile(1, 0)
-        cast("act", 1, 0, 0, 0, 64)
-        cast("act", 1, 0, HALF, 64, 32)
-        cast("pool", 1, 0, HALF, 96, 32)
-        quant_w(1, 0, 0, count=1)
-        mm1(0, 1)
-        quant_w(1, 0, 1, count=1)
-        mm1(1, 1)
-        quant_w(0, 0, 2, "raw1_256")
-        room("third", 8192)
-        quant_w(1, 0, 2, "third", 4096 - 512)
-        evac(0, shared=True)
-        for u in (2, 3):
-            mm1(u, 0)
-            mm1(u, 1)
-        for q in range(4):
-            nc.sync.dma_start(
-                w2s[32 * q : 32 * q + 4, :, :],
-                w2_scales[:, 4 * q : 4 * q + 4, :].rearrange("a r n -> r a n").bitcast(I32),
-            )
-        w2sb = w2s[:].rearrange("p a c -> p (a c)").bitcast(U8)
-
-        wide_tile(0, 1, "wide10")
-        wide_tile(1, 1, "third", 4096)
-        cast("pool", 0, 1, 512, 0, 64)
-        cast("pool", 0, 1, 512, 64, 64)
-        cast("pool", 1, 1, 512, 0, 64)
-        cast("pool", 1, 1, 512, 64, 32)
-        for u in range(1, 4):
-            evac(u)
-        for u in range(4):
-            pick2(u)
-        cast("act", 1, 1, 512, 96, 32)
-        quant_w(0, 1, 0, "raw1_512")
-        quant_w(1, 1, 0)
-        mm1(4, 0)
-        mm1(4, 1)
-        mm1(5, 0)
-        mm1(5, 1)
-        quant_w(0, 1, 2, "raw1_512", 1024)
-        quant_w(1, 1, 2)
-        mm1(6, 0)
-        mm1(6, 1)
-        mm1(7, 0)
-        mm1(7, 1)
-        pick1(0, "raw1_512", 2048)
-        pick1(1, "wide01")
-        pick1(2, "wide01", 2048)
-        magnitude(0, 2, "third")
-        magnitude(2, 2, "raw0_512")
-        inv_root(0, 2)
-        inv_root(2, 1)
-        inv_root(3, 1)
-        evac(4)
-        pick2(4)
-        gain_num(2, nc.gpsimd)
-        square(0, 2)
-        gain_num(0, nc.vector)
-        gain_num(1, nc.vector)
-        pick1(3, "root0")
-        evac(5)
-        pick2(5)
-        gain_num(3, nc.gpsimd)
-        square(2, 1)
-        pick1(4, "root2")
-        evac(6)
-        pick2(6)
-        gain_num(4, nc.gpsimd)
-        square(3, 1)
-        magnitude(4, 2)
-        evac(7)
-        pick1(5, "root3")
-        pick2(7)
-        gain_num(5, nc.gpsimd)
-        inv_root(4, 2)
-        magnitude_in_left(6)
-        square(4, 2)
-        inv_root_from_left(6)
-        magnitude_in_left(7)
-        square_apart(6)
-        inv_root_from_left(7)
-        gain_inv(6)
-        square_apart(7)
-        gain_inv(7)
-        make_z(0, slice(0, 3 * CH), "mag4")
-        pick1_direct(6)
-        pick1_direct(7)
-        zc[0] = sb("zc0", [P, NP], U32, "inv6")
-        quant_z(0, slice(0, HALF))
-        mm2(0, 0)
-        mm2(1, 0)
-        quant_z(0, chunk(2))
-        mm2(2, 0)
-
         def close(c):
             quant_z(1, chunk(c))
             mm2(c, 1)
             finish(c)
 
+        for half in range(2):
+            make_z(0, slice(HALF * half, HALF * (half + 1)))
+        for half in range(2):
+            quant_z(0, slice(HALF * half, HALF * (half + 1)))
+            mm2(2 * half, 0)
+            mm2(2 * half + 1, 0)
         make_z(1, chunk(0))
-        make_z(1, chunk(1))
-        close(0)
-        make_z(1, chunk(2))
-        close(1)
-        make_z(0, chunk(3), "zb1_0")
-        close(2)
-        make_z(1, chunk(3))
-        quant_z(0, chunk(3))
-        mm2(3, 0)
+        for c in range(1, 4):
+            make_z(1, chunk(c))
+            close(c - 1)
         close(3)

@@ -215,10 +215,10 @@ def tile_list_pair_spread_positions_kernel(
         mm1(2, 1)
         mm1(3, 1)
 
-        w2w = sb("w2w", [P, 2, N // 2], I32, "wide00")
+        w2w = sb("w2w", [P, 2, N // 2], I32, "wide10", 1024)
         nc.sync.dma_start(w2w[:], w2_words.rearrange("a p c -> p a c").bitcast(I32))
         w2c = w2w[:].rearrange("p a c -> p (a c)").bitcast(U8)
-        g = sb("g", [P, 2, 4], F32, "wide00", 2048)
+        g = sb("g", [P, 2, 4], F32, "wide10", 3072)
         nc.sync.dma_start(g[:], gain.rearrange("(b p t) -> p b t", b=2, t=4))
         w2s = sb("w2s", [P, 2, N // 4], I32, "wide10")
         nc.vector.memset(w2s[:], 0)
@@ -325,9 +325,11 @@ def tile_list_pair_spread_positions_kernel(
         def mm2(c, b):
             last = c == 3
             for nt in range(4):
-                if b == 0 and (last or nt == 0):
-                    acc[c, nt] = bank(3 + nt if last else c)
-                place = acc[c, nt][:, 0:CH] if last else acc[c, 0][:, CH * nt : CH * (nt + 1)]
+                head = nt - nt % 2 if last else 0
+                tail = head + 1 if last else 3
+                if b == 0 and nt == head:
+                    acc[c, nt] = bank(c + nt // 2)
+                place = acc[c, head][:, CH * (nt - head) : CH * (nt - head + 1)]
                 cols = slice(CH * c, CH * (c + 1))
                 nc.tensor.matmul_mx(
                     out=place,
@@ -335,8 +337,8 @@ def tile_list_pair_spread_positions_kernel(
                     lhsT_scale=w2sb[:, N * b + P * nt : N * b + P * (nt + 1)],
                     rhs=zc[b][:, cols].bitcast(FP8X4),
                     rhs_scale=zs[b][:, cols],
-                    start=(b == 0 and (last or nt == 0)),
-                    stop=(b == 1 and (last or nt == 3)),
+                    start=(b == 0 and nt == head),
+                    stop=(b == 1 and nt == tail),
                 )
 
         out_v = out.rearrange("(nt p) j -> p nt j", p=P)
@@ -348,10 +350,10 @@ def tile_list_pair_spread_positions_kernel(
                 nc.scalar.activation(res[:].rearrange("p n j -> p (n j)"), acc[c, 0][:], ACT.Tanh)
                 nc.sync.dma_start(out_v[:, :, cols], res[:])
             else:
-                for nt in range(4):
-                    nc.scalar.activation(res[:, nt, :], acc[c, nt][:, 0:CH], ACT.Tanh)
-                    if nt % 2 == 1:
-                        nc.sync.dma_start(out_v[:, nt - 1 : nt + 1, cols], res[:, nt - 1 : nt + 1, :])
+                for nt in (0, 2):
+                    pair = res[:, nt : nt + 2, :]
+                    nc.scalar.activation(pair.rearrange("p n j -> p (n j)"), acc[c, nt][:, 0 : 2 * CH], ACT.Tanh)
+                    nc.sync.dma_start(out_v[:, nt : nt + 2, cols], pair)
 
         def chunk(c):
             return slice(CH * c, CH * (c + 1))

@@ -21,6 +21,7 @@ P = 128
 CH = 128
 HALF = 256
 WINDOWS = 6
+FLOOR = 2.0**-100
 
 
 def tile_list_pair_spread_positions_kernel(
@@ -158,6 +159,11 @@ def tile_list_pair_spread_positions_kernel(
                     stop=(a == 1),
                 )
 
+        def evac_signed(u):
+            for half in range(2):
+                dst = h[u % WINDOWS][:, 512 * half : 512 * (half + 1)]
+                nc.scalar.activation(dst, hps[u, half][:], ACT.Copy, scale=sign[:, u - 4 : u - 3])
+
         def evac(u, shared=False):
             if shared:
                 nc.vector.tensor_copy(h[u % WINDOWS][:, 0:512], hps[u, 0][:])
@@ -265,10 +271,18 @@ def tile_list_pair_spread_positions_kernel(
         magnitude(0, mag01[:])
         magnitude(1, mag23[:])
         inv_root(right[0][:, 0:2, :], mag01[:])
+        sign = sb("sign", [P, 4], F32, "third")
+        amount = sb("amount", [P, 4], F32, "third", 64)
+        floored = sb("floored", [P, 4], F32)
+        shrink = sb("shrink", [P, 4], F32)
+        nc.scalar.activation(amount[:], g[:, 1, :], ACT.Abs)
+        nc.scalar.activation(sign[:], g[:, 1, :], ACT.Sign)
+        nc.scalar.activation(floored[:], amount[:], ACT.Identity, bias=FLOOR)
+        nc.vector.reciprocal(shrink[:], floored[:])
         inv_root(left[1][:, 2:4, :], mag23[:])
         nc.scalar.activation(right[0][:, 1, :], right[0][:, 1, :], ACT.Square)
         for u in range(4, 8):
-            evac(u)
+            evac_signed(u)
         for u in range(4, 8):
             second_leg(u)
 
@@ -279,45 +293,47 @@ def tile_list_pair_spread_positions_kernel(
         nc.gpsimd.tensor_tensor(left[0][:, 0, :], left[0][:, 0, :], right[0][:, 0, :], ALU.mult)
 
         right[1] = sb("right1", [P, 4, NP], F32)
-        inv45, inv67 = pair_tile("inv45"), pair_tile("inv67")
-        mag67, root67 = pair_tile("mag67", "mag23"), pair_tile("root67")
-        root45 = pair_tile("root45", "third")
+        mag67 = pair_tile("mag67", "mag23")
+
+        def gained_root(t, src):
+            c = shrink[:, t : t + 1]
+            nc.scalar.activation(right[1][:, t, :], src, ACT.Abs_reciprocal_sqrt, bias=c, scale=c)
+
         nc.scalar.activation(right[0][:, 2:4, :], left[1][:, 2:4, :], ACT.Square)
-        magnitude(2, left[1][:, 0:2, :])
-        inv_root(root45[:], left[1][:, 0:2, :])
-        magnitude(3, mag67[:])
-        nc.scalar.activation(inv45[:], root45[:], ACT.Square)
-        inv_root(root67[:], mag67[:])
-
-        def gain_inv(t, src):
-            nc.scalar.activation(right[1][:, t, :], src, ACT.Copy, scale=g[:, 1, t : t + 1])
-
-        gain_inv(0, inv45[:, 0, :])
-        nc.scalar.activation(inv67[:], root67[:], ACT.Square)
-        gain_inv(1, inv45[:, 1, :])
-        gain_inv(2, inv67[:, 0, :])
-        gain_inv(3, inv67[:, 1, :])
+        nc.scalar.activation(left[1][:, 0:2, :], legs[2][:], ACT.Abs, scale=1.0 / 1.5)
+        gained_root(0, left[1][:, 0, :])
+        gained_root(1, left[1][:, 1, :])
+        nc.scalar.activation(mag67[:], legs[3][:], ACT.Abs, scale=1.0 / 1.5)
+        nc.scalar.activation(right[1][:, 0:2, :], right[1][:, 0:2, :], ACT.Square)
+        gained_root(2, mag67[:, 0, :])
+        gained_root(3, mag67[:, 1, :])
+        nc.scalar.activation(right[1][:, 2, :], right[1][:, 2, :], ACT.Square)
+        nc.scalar.activation(right[1][:, 3, :], right[1][:, 3, :], ACT.Square)
         for u in range(4, 8):
             first_leg(u, left[1][:, u - 4, :])
 
-        zb = {}
-        zc = [sb("zc%d" % b, [P, NP], U32) for b in range(2)]
-        zs = [sb("zs%d" % b, [P, NP], U8) for b in range(2)]
+        zb, zc, zs = {}, {}, {}
 
-        def make_z(b, cols):
-            zb[b, cols.start] = sb("zb%d_%d" % (b, cols.start), [P, cols.stop - cols.start, 4], BF16)
+        def chunk(c):
+            return slice(CH * c, CH * (c + 1))
+
+        def make_z(b, first, count, over="", at=0):
+            cols = slice(CH * first, CH * (first + count))
+            tile = sb("zb%d_%d" % (b, first), [P, count * CH, 4], BF16, over, at)
             nc.vector.tensor_tensor(
-                zb[b, cols.start][:].rearrange("p (c i) t -> p c t i", i=2),
+                tile[:].rearrange("p (c i) t -> p c t i", i=2),
                 left[b][:, :, cols].rearrange("p t (c i) -> p c t i", i=2),
                 right[b][:, :, cols].rearrange("p t (c i) -> p c t i", i=2),
                 ALU.mult,
             )
+            for c in range(count):
+                zb[b, first + c] = tile[:, chunk(c), :]
 
-        def quant_z(b, cols):
+        def quant_z(b, c, over="", at=0):
+            zc[b, c] = sb("zc%d_%d" % (b, c), [P, CH], U32, over, at)
+            zs[b, c] = sb("zs%d_%d" % (b, c), [P, CH], U8)
             nc.vector.quantize_mx(
-                out=zc[b][:, cols].bitcast(FP8X4),
-                scales=zs[b][:, cols],
-                in_=zb[b, cols.start][:].rearrange("p c t -> p (c t)"),
+                out=zc[b, c][:].bitcast(FP8X4), scales=zs[b, c][:], in_=zb[b, c].rearrange("p c t -> p (c t)")
             )
 
         acc = {}
@@ -329,14 +345,12 @@ def tile_list_pair_spread_positions_kernel(
                 tail = head + 1 if last else 3
                 if b == 0 and nt == head:
                     acc[c, nt] = bank(c + nt // 2)
-                place = acc[c, head][:, CH * (nt - head) : CH * (nt - head + 1)]
-                cols = slice(CH * c, CH * (c + 1))
                 nc.tensor.matmul_mx(
-                    out=place,
+                    out=acc[c, head][:, CH * (nt - head) : CH * (nt - head + 1)],
                     lhsT=w2c[:, 2 * N * b + 2 * P * nt : 2 * N * b + 2 * P * (nt + 1)].bitcast(FP4X4),
                     lhsT_scale=w2sb[:, N * b + P * nt : N * b + P * (nt + 1)],
-                    rhs=zc[b][:, cols].bitcast(FP8X4),
-                    rhs_scale=zs[b][:, cols],
+                    rhs=zc[b, c][:].bitcast(FP8X4),
+                    rhs_scale=zs[b, c][:],
                     start=(b == 0 and nt == head),
                     stop=(b == 1 and nt == tail),
                 )
@@ -345,32 +359,35 @@ def tile_list_pair_spread_positions_kernel(
 
         def finish(c):
             res = sb("res%d" % c, [P, 4, CH], F32)
-            cols = slice(CH * c, CH * (c + 1))
             if c < 3:
                 nc.scalar.activation(res[:].rearrange("p n j -> p (n j)"), acc[c, 0][:], ACT.Tanh)
-                nc.sync.dma_start(out_v[:, :, cols], res[:])
+                nc.sync.dma_start(out_v[:, :, chunk(c)], res[:])
             else:
                 for nt in (0, 2):
                     pair = res[:, nt : nt + 2, :]
                     nc.scalar.activation(pair.rearrange("p n j -> p (n j)"), acc[c, nt][:, 0 : 2 * CH], ACT.Tanh)
-                    nc.sync.dma_start(out_v[:, nt : nt + 2, cols], pair)
+                    nc.sync.dma_start(out_v[:, nt : nt + 2, chunk(c)], pair)
 
-        def chunk(c):
-            return slice(CH * c, CH * (c + 1))
+        def open_chunk(c, over="", at=0):
+            quant_z(0, c, over, at)
+            mm2(c, 0)
 
-        def close(c):
-            quant_z(1, chunk(c))
+        def close_chunk(c):
+            quant_z(1, c)
             mm2(c, 1)
             finish(c)
 
-        for half in range(2):
-            make_z(0, slice(HALF * half, HALF * (half + 1)))
-        for half in range(2):
-            quant_z(0, slice(HALF * half, HALF * (half + 1)))
-            mm2(2 * half, 0)
-            mm2(2 * half + 1, 0)
-        make_z(1, chunk(0))
-        for c in range(1, 4):
-            make_z(1, chunk(c))
-            close(c - 1)
-        close(3)
+        make_z(0, 0, 2, "legs3")
+        make_z(0, 2, 1, "legs3", 2048)
+        for c in range(3):
+            open_chunk(c)
+        make_z(1, 0, 1)
+        make_z(1, 1, 1)
+        close_chunk(0)
+        make_z(1, 2, 1)
+        close_chunk(1)
+        make_z(0, 3, 1, "zb1_0")
+        close_chunk(2)
+        make_z(1, 3, 1, "zb1_1")
+        open_chunk(3)
+        close_chunk(3)

@@ -240,13 +240,12 @@ def tile_list_pair_spread_positions_kernel(
         wide_tile(1, 1, "late")
         cast("pool", 0, 1, 512, 0, 64)
         cast("pool", 0, 1, 512, 64, 64)
-        cast("pool", 1, 1, 512, 0, 64)
-        cast("pool", 1, 1, 512, 64, 32)
         for u in range(1, 4):
             evac(u)
+        cast("act", 1, 1, 512, 0, 128, slice(2, 4))
         for u in range(4):
             second_leg(u)
-        cast("dve", 1, 1, 512, 96, 32)
+        cast("dve", 1, 1, 512, 0, 128, slice(0, 2))
         quant_w(0, 1, 0, "first")
         quant_w(1, 1, 0)
         mm1(4, 0)
@@ -279,10 +278,10 @@ def tile_list_pair_spread_positions_kernel(
         nc.scalar.activation(sign[:], g[:, 1, :], ACT.Sign)
         nc.scalar.activation(floored[:], amount[:], ACT.Identity, bias=FLOOR)
         nc.vector.reciprocal(shrink[:], floored[:])
-        inv_root(left[1][:, 2:4, :], mag23[:])
-        nc.scalar.activation(right[0][:, 1, :], right[0][:, 1, :], ACT.Square)
         for u in range(4, 8):
             evac_signed(u)
+        inv_root(left[1][:, 2:4, :], mag23[:])
+        nc.scalar.activation(right[0][:, 1, :], right[0][:, 1, :], ACT.Square)
         for u in range(4, 8):
             second_leg(u)
 

@@ -59,7 +59,7 @@ def tile_list_pair_spread_positions_kernel(
         room("first", 4 * 4 * 512)
         rows = sb("rows", [P, T // 4], I32, "first")
         planes = sb("planes", [P, 2 * S // 4], I32)
-        h = [sb("h%d" % i, [P, 2 * S], F32) for i in range(WINDOWS)]
+        h = [sb("h%d" % i, [P, 2 * S], F32) for i in range(4)]
         one = sb("one", [P, 1], F32)
         warm = sb("warm", [P, 1], F32)
 
@@ -68,23 +68,27 @@ def tile_list_pair_spread_positions_kernel(
         nc.gpsimd.memset(rows[64:128, :], 0)
         nc.vector.memset(planes[:], 0)
         nc.scalar.activation(warm[:], one[:, 0:1], ACT.Abs_reciprocal_sqrt, bias=1.0)
-        for i in range(WINDOWS):
+        for i in range(4):
             nc.gpsimd.memset(h[i][:, S : 2 * S], 0.0)
 
         tabw, raw = {}, {}
 
-        def load_tab(a, over=""):
-            tabw[a] = sb("tabw%d" % a, [P, T], I32, over)
+        def load_tab(a, over="", at=0):
+            tabw[a] = sb("tabw%d" % a, [P, T], I32, over, at)
             nc.sync.dma_start(tabw[a][:], tab_words[a].rearrange("p t i -> p (t i)").bitcast(I32))
 
-        def load_w1(a, first, width, over="", at=0):
-            raw[a, first] = sb("raw%d_%d" % (a, first), [P, 4, width], F32, over, at)
+        def load_w1(a, first, width, over="", into=None):
+            if into is None:
+                raw[a, first] = sb("raw%d_%d" % (a, first), [P, 4, width], F32, over)[:]
+            else:
+                raw[a, first] = into.rearrange("p (j c) -> p j c", j=4)
             src = w1[512 * a : 512 * (a + 1), first : first + width]
-            nc.sync.dma_start(raw[a, first][:], src.rearrange("(p j) c -> p j c", j=4))
+            nc.sync.dma_start(raw[a, first], src.rearrange("(p j) c -> p j c", j=4))
 
         nc.sync.dma_start(offs_t[:], offs)
         nc.sync.dma_start(rows[0:32, :], tab_scales.rearrange("a q t -> (a q) t").bitcast(I32))
-        load_tab(0)
+        room("pair", 2 * 8192)
+        load_tab(0, "pair", 4096)
         load_w1(0, 0, 512)
         nc.sync.dma_start(pos2_t[:], pos2)
         nc.sync.dma_start(pos1_t[:], pos1)
@@ -105,8 +109,9 @@ def tile_list_pair_spread_positions_kernel(
         place_rows(0)
         load_tab(1, "first")
         place_rows(1)
-        load_w1(1, 0, HALF, "tabw0")
-        load_w1(1, HALF, HALF, "tabw0", 4096)
+        for i in range(2):
+            h.append(sb("h%d" % (4 + i), [P, 2 * S], F32, "pair", 8192 * i))
+            load_w1(1, HALF * i, HALF, into=h[4 + i][:, S : 2 * S])
         load_w1(0, 512, 512, "raw0_0")
 
         wide, wc, ws = {}, {}, {}
@@ -226,14 +231,7 @@ def tile_list_pair_spread_positions_kernel(
         w2c = w2w[:].rearrange("p a c -> p (a c)").bitcast(U8)
         g = sb("g", [P, 2, 4], F32, "wide10", 3072)
         nc.sync.dma_start(g[:], gain.rearrange("(b p t) -> p b t", b=2, t=4))
-        w2s = sb("w2s", [P, 2, N // 4], I32, "wide10")
-        nc.vector.memset(w2s[:], 0)
-        for q in range(4):
-            nc.sync.dma_start(
-                w2s[32 * q : 32 * q + 4, :, :],
-                w2_scales[:, 4 * q : 4 * q + 4, :].rearrange("a r n -> r a n").bitcast(I32),
-            )
-        w2sb = w2s[:].rearrange("p a c -> p (a c)").bitcast(U8)
+        w2s = planes[:, 0 : N // 2].rearrange("p (a c) -> p a c", a=2)
 
         wide_tile(0, 1)
         room("late", 8192)
@@ -258,6 +256,12 @@ def tile_list_pair_spread_positions_kernel(
         mm1(6, 1)
         mm1(7, 0)
         mm1(7, 1)
+        for q in range(4):
+            nc.sync.dma_start(
+                w2s[32 * q : 32 * q + 4, :, :],
+                w2_scales[:, 4 * q : 4 * q + 4, :].rearrange("a r n -> r a n").bitcast(I32),
+            )
+        w2sb = vs[:, 0 : 2 * N]
         right[0] = sb("right0", [P, 4, NP], F32, "late")
         num[0] = sb("num0", [P, NP], F32, "first", 2048)[:]
         num[1] = sb("num1", [P, NP], F32, "wide01")[:]

@@ -238,12 +238,13 @@ def tile_list_pair_spread_positions_kernel(
         wide_tile(1, 1, "late")
         cast("pool", 0, 1, 512, 0, 64)
         cast("pool", 0, 1, 512, 64, 64)
+        cast("pool", 1, 1, 512, 0, 64)
+        cast("pool", 1, 1, 512, 64, 32)
         for u in range(1, 4):
             evac(u)
-        cast("act", 1, 1, 512, 0, 128, slice(2, 4))
         for u in range(4):
             second_leg(u)
-        cast("dve", 1, 1, 512, 0, 128, slice(0, 2))
+        cast("dve", 1, 1, 512, 96, 32)
         quant_w(0, 1, 0, "first")
         quant_w(1, 1, 0)
         mm1(4, 0)

@@ -89,9 +89,18 @@ def tile_list_pair_spread_positions_kernel(
         nc.sync.dma_start(rows[0:32, :], tab_scales.rearrange("a q t -> (a q) t").bitcast(I32))
         room("pair", 2 * 8192)
         load_tab(0, "pair", 4096)
-        load_w1(0, 0, 512)
+        g = sb("g", [P, 8], F32)
+        sign = sb("sign", [P, 8], F32)
+        amount = sb("amount", [P, 8], F32)
+        floored = sb("floored", [P, 8], F32)
+        shrink = sb("shrink", [P, 8], F32)
         nc.sync.dma_start(pos2_t[:], pos2)
+        load_w1(0, 0, 512)
+        nc.sync.dma_start(g[:].rearrange("p (b t) -> p b t", b=2), gain.rearrange("(b p t) -> p b t", b=2, t=4))
         nc.sync.dma_start(pos1_t[:], pos1)
+        nc.scalar.activation(amount[:], g[:], ACT.Abs)
+        nc.scalar.activation(sign[:], g[:], ACT.Sign)
+        nc.scalar.activation(floored[:], amount[:], ACT.Identity, bias=FLOOR)
 
         picked = sb("picked", [P, S // 4], I32)
         vw = [sb("vw%d" % a, [P, S], U32) for a in range(2)]
@@ -164,23 +173,18 @@ def tile_list_pair_spread_positions_kernel(
                     stop=(a == 1),
                 )
 
-        def evac_signed(u):
+        def evac(u, shared=False):
             for half in range(2):
                 dst = h[u % WINDOWS][:, 512 * half : 512 * (half + 1)]
-                nc.scalar.activation(dst, hps[u, half][:], ACT.Copy, scale=sign[:, u - 4 : u - 3])
+                if shared and half == 0:
+                    nc.vector.tensor_scalar(dst, hps[u, half][:], sign[:, u : u + 1], None, ALU.mult)
+                else:
+                    nc.scalar.activation(dst, hps[u, half][:], ACT.Copy, scale=sign[:, u : u + 1])
 
-        def evac(u, shared=False):
-            if shared:
-                nc.vector.tensor_copy(h[u % WINDOWS][:, 0:512], hps[u, 0][:])
-            else:
-                nc.scalar.copy(h[u % WINDOWS][:, 0:512], hps[u, 0][:])
-            nc.scalar.copy(h[u % WINDOWS][:, 512:1024], hps[u, 1][:])
-
-        room("factors", 8192)
-        legs = {0: sb("legs0", [P, 2, NP], F32), 1: sb("legs1", [P, 2, NP], F32, "factors")}
+        legs = {0: sb("legs0", [P, 2, NP], F32), 1: sb("legs1", [P, 2, NP], F32)}
         legs[2] = sb("legs2", [P, 2, NP], F32)
         legs[3] = sb("legs3", [P, 2, NP], F32)
-        left, right, num = {}, {}, {}
+        left, right = {}, {}
 
         def second_leg(u):
             nc.vector.tensor_scalar(
@@ -190,11 +194,15 @@ def tile_list_pair_spread_positions_kernel(
         def first_leg(u, dst):
             nc.vector.tensor_tensor(dst, h[u % WINDOWS][:].indirect(pos1_t[:]), legs[u // 2][:, u % 2, :], ALU.add)
 
-        def magnitude(pair, dst):
-            nc.scalar.activation(dst, legs[pair][:], ACT.Abs)
+        def magnitude(dst, src):
+            nc.scalar.activation(dst, src, ACT.Abs, scale=1.0 / 1.5)
 
-        def inv_root(dst, src):
-            nc.scalar.activation(dst, src, ACT.Abs_reciprocal_sqrt, bias=1.0, scale=1.0 / 1.5)
+        def inv_root(u, src):
+            c = shrink[:, u : u + 1]
+            nc.scalar.activation(right[u // 4][:, u % 4, :], src, ACT.Abs_reciprocal_sqrt, bias=c, scale=c)
+
+        def square(dst):
+            nc.scalar.activation(dst, dst, ACT.Square)
 
         def pair_tile(name, over="", at=0):
             return sb(name, [P, 2, NP], F32, over, at)
@@ -210,6 +218,7 @@ def tile_list_pair_spread_positions_kernel(
         mm1(2, 0)
         mm1(3, 0)
         nc.vector.tensor_copy(vw[1][:], tabw[1][:].bitcast(U32).indirect(offs_t[:]))
+        nc.vector.reciprocal(shrink[:], floored[:])
         load_w1(1, 512, 512, "first")
         wide_tile(1, 0)
         cast("act", 1, 0, 0, 0, 64, low)
@@ -229,8 +238,6 @@ def tile_list_pair_spread_positions_kernel(
         w2w = sb("w2w", [P, 2, N // 2], I32, "wide10", 1024)
         nc.sync.dma_start(w2w[:], w2_words.rearrange("a p c -> p a c").bitcast(I32))
         w2c = w2w[:].rearrange("p a c -> p (a c)").bitcast(U8)
-        g = sb("g", [P, 2, 4], F32, "wide10", 3072)
-        nc.sync.dma_start(g[:], gain.rearrange("(b p t) -> p b t", b=2, t=4))
         w2s = planes[:, 0 : N // 2].rearrange("p (a c) -> p a c", a=2)
 
         wide_tile(0, 1)
@@ -238,13 +245,11 @@ def tile_list_pair_spread_positions_kernel(
         wide_tile(1, 1, "late")
         cast("pool", 0, 1, 512, 0, 64)
         cast("pool", 0, 1, 512, 64, 64)
-        cast("pool", 1, 1, 512, 0, 64)
-        cast("pool", 1, 1, 512, 64, 32)
         for u in range(1, 4):
             evac(u)
         for u in range(4):
             second_leg(u)
-        cast("dve", 1, 1, 512, 96, 32)
+        cast("dve", 1, 1, 512, 0, 128)
         quant_w(0, 1, 0, "first")
         quant_w(1, 1, 0)
         mm1(4, 0)
@@ -263,56 +268,50 @@ def tile_list_pair_spread_positions_kernel(
                 w2_scales[:, 4 * q : 4 * q + 4, :].rearrange("a r n -> r a n").bitcast(I32),
             )
         w2sb = vs[:, 0 : 2 * N]
-        right[0] = sb("right0", [P, 4, NP], F32, "late")
-        num[0] = sb("num0", [P, NP], F32, "first", 2048)[:]
-        num[1] = sb("num1", [P, NP], F32, "wide01")[:]
-        num[2], num[3] = right[0][:, 2, :], right[0][:, 3, :]
+        left[0] = sb("left0", [P, 4, NP], F32, "late")
         for u in range(4):
-            first_leg(u, num[u])
+            first_leg(u, left[0][:, u, :])
 
-        mag01, mag23 = pair_tile("mag01", "third"), pair_tile("mag23")
-        left[1] = sb("left1", [P, 4, NP], F32)
-        magnitude(0, mag01[:])
-        magnitude(1, mag23[:])
-        inv_root(right[0][:, 0:2, :], mag01[:])
-        sign = sb("sign", [P, 4], F32, "third")
-        amount = sb("amount", [P, 4], F32, "third", 64)
-        floored = sb("floored", [P, 4], F32)
-        shrink = sb("shrink", [P, 4], F32)
-        nc.scalar.activation(amount[:], g[:, 1, :], ACT.Abs)
-        nc.scalar.activation(sign[:], g[:, 1, :], ACT.Sign)
-        nc.scalar.activation(floored[:], amount[:], ACT.Identity, bias=FLOOR)
-        nc.vector.reciprocal(shrink[:], floored[:])
-        for u in range(4, 8):
-            evac_signed(u)
-        inv_root(left[1][:, 2:4, :], mag23[:])
-        nc.scalar.activation(right[0][:, 1, :], right[0][:, 1, :], ACT.Square)
-        for u in range(4, 8):
-            second_leg(u)
-
-        left[0] = sb("left0", [P, 4, NP], F32, "factors")
-        for t in (2, 3, 1):
-            nc.gpsimd.tensor_scalar(left[0][:, t, :], num[t], g[:, 0, t : t + 1], 0.0, ALU.mult, ALU.add)
-        nc.gpsimd.tensor_scalar(left[0][:, 0, :], num[0], g[:, 0, 0:1], 0.0, ALU.mult, ALU.add)
-        nc.gpsimd.tensor_tensor(left[0][:, 0, :], left[0][:, 0, :], right[0][:, 0, :], ALU.mult)
-
+        right[0] = sb("right0", [P, 4, NP], F32)
         right[1] = sb("right1", [P, 4, NP], F32)
+        left[1] = sb("left1", [P, 4, NP], F32)
+        mag01, mag23 = pair_tile("mag01", "third"), pair_tile("mag23")
+        magnitude(mag01[:], legs[0][:])
+        magnitude(mag23[:], legs[1][:])
+        for u in range(4):
+            inv_root(u, (mag01, mag23)[u // 2][:, u % 2, :])
+        square(right[0][:, :, 0:CH])
+        square(right[0][:, :, CH : 3 * CH])
+        zpool = sb("zpool", [P, 3 * CH, 4], BF16)
+        for c in range(3):
+            cols = slice(CH * c, CH * (c + 1))
+            nc.gpsimd.tensor_tensor(
+                zpool[:, cols, :].rearrange("p (c i) t -> p c t i", i=2),
+                left[0][:, :, cols].rearrange("p t (c i) -> p c t i", i=2),
+                right[0][:, :, cols].rearrange("p t (c i) -> p c t i", i=2),
+                ALU.mult,
+            )
+        mag4 = left[1][:, :, 0:CH]
+        mag5 = sb("mag5", [P, NP], F32, "mag01")
         mag67 = pair_tile("mag67", "mag23")
-
-        def gained_root(t, src):
-            c = shrink[:, t : t + 1]
-            nc.scalar.activation(right[1][:, t, :], src, ACT.Abs_reciprocal_sqrt, bias=c, scale=c)
-
-        nc.scalar.activation(right[0][:, 2:4, :], left[1][:, 2:4, :], ACT.Square)
-        nc.scalar.activation(left[1][:, 0:2, :], legs[2][:], ACT.Abs, scale=1.0 / 1.5)
-        gained_root(0, left[1][:, 0, :])
-        gained_root(1, left[1][:, 1, :])
-        nc.scalar.activation(mag67[:], legs[3][:], ACT.Abs, scale=1.0 / 1.5)
-        nc.scalar.activation(right[1][:, 0:2, :], right[1][:, 0:2, :], ACT.Square)
-        gained_root(2, mag67[:, 0, :])
-        gained_root(3, mag67[:, 1, :])
-        nc.scalar.activation(right[1][:, 2, :], right[1][:, 2, :], ACT.Square)
-        nc.scalar.activation(right[1][:, 3, :], right[1][:, 3, :], ACT.Square)
+        for u in range(4, 7):
+            evac(u)
+            second_leg(u)
+        magnitude(mag4, legs[2][:, 0, :].rearrange("p (t c) -> p t c", t=4))
+        evac(7)
+        second_leg(7)
+        c4 = shrink[:, 4:5]
+        root4 = right[1][:, 0, :].rearrange("p (t c) -> p t c", t=4)
+        nc.scalar.activation(root4, mag4, ACT.Abs_reciprocal_sqrt, bias=c4, scale=c4)
+        magnitude(mag5[:], legs[2][:, 1, :])
+        square(right[0][:, :, 3 * CH : NP])
+        inv_root(5, mag5[:])
+        magnitude(mag67[:], legs[3][:])
+        square(right[1][:, 0:2, :])
+        inv_root(6, mag67[:, 0, :])
+        inv_root(7, mag67[:, 1, :])
+        for cols in (slice(0, HALF), slice(HALF, NP)):
+            square(right[1][:, 2:4, cols])
         for u in range(4, 8):
             first_leg(u, left[1][:, u - 4, :])
 
@@ -381,10 +380,9 @@ def tile_list_pair_spread_positions_kernel(
             mm2(c, 1)
             finish(c)
 
-        make_z(0, 0, 2, "legs3")
-        make_z(0, 2, 1, "legs3", 2048)
         for c in range(3):
-            open_chunk(c)
+            zb[0, c] = zpool[:, chunk(c), :]
+            open_chunk(c, "legs3", 512 * c)
         make_z(1, 0, 1)
         make_z(1, 1, 1)
         close_chunk(0)

@@ -89,18 +89,12 @@ def tile_list_pair_spread_positions_kernel(
         nc.sync.dma_start(rows[0:32, :], tab_scales.rearrange("a q t -> (a q) t").bitcast(I32))
         room("pair", 2 * 8192)
         load_tab(0, "pair", 4096)
-        g = sb("g", [P, 8], F32)
         sign = sb("sign", [P, 8], F32)
         amount = sb("amount", [P, 8], F32)
         floored = sb("floored", [P, 8], F32)
-        shrink = sb("shrink", [P, 8], F32)
-        nc.sync.dma_start(pos2_t[:], pos2)
         load_w1(0, 0, 512)
-        nc.sync.dma_start(g[:].rearrange("p (b t) -> p b t", b=2), gain.rearrange("(b p t) -> p b t", b=2, t=4))
+        nc.sync.dma_start(pos2_t[:], pos2)
         nc.sync.dma_start(pos1_t[:], pos1)
-        nc.scalar.activation(amount[:], g[:], ACT.Abs)
-        nc.scalar.activation(sign[:], g[:], ACT.Sign)
-        nc.scalar.activation(floored[:], amount[:], ACT.Identity, bias=FLOOR)
 
         picked = sb("picked", [P, S // 4], I32)
         vw = [sb("vw%d" % a, [P, S], U32) for a in range(2)]
@@ -121,6 +115,8 @@ def tile_list_pair_spread_positions_kernel(
         for i in range(2):
             h.append(sb("h%d" % (4 + i), [P, 2 * S], F32, "pair", 8192 * i))
             load_w1(1, HALF * i, HALF, into=h[4 + i][:, S : 2 * S])
+        g = h[5][:, 0:8]
+        nc.sync.dma_start(g.rearrange("p (b t) -> p b t", b=2), gain.rearrange("(b p t) -> p b t", b=2, t=4))
         load_w1(0, 512, 512, "raw0_0")
 
         wide, wc, ws = {}, {}, {}
@@ -218,7 +214,6 @@ def tile_list_pair_spread_positions_kernel(
         mm1(2, 0)
         mm1(3, 0)
         nc.vector.tensor_copy(vw[1][:], tabw[1][:].bitcast(U32).indirect(offs_t[:]))
-        nc.vector.reciprocal(shrink[:], floored[:])
         load_w1(1, 512, 512, "first")
         wide_tile(1, 0)
         cast("act", 1, 0, 0, 0, 64, low)
@@ -231,7 +226,10 @@ def tile_list_pair_spread_positions_kernel(
         mm1(1, 1)
         room("third", 4096)
         quant_w(1, 0, 2, "third")
+        nc.scalar.activation(sign[:], g, ACT.Sign)
+        nc.scalar.activation(amount[:], g, ACT.Abs)
         evac(0, shared=True)
+        nc.scalar.activation(floored[:], amount[:], ACT.Identity, bias=FLOOR)
         mm1(2, 1)
         mm1(3, 1)
 
@@ -250,6 +248,8 @@ def tile_list_pair_spread_positions_kernel(
         for u in range(4):
             second_leg(u)
         cast("dve", 1, 1, 512, 0, 128)
+        shrink = sb("shrink", [P, 8], F32, "raw0_0")
+        nc.vector.reciprocal(shrink[:], floored[:])
         quant_w(0, 1, 0, "first")
         quant_w(1, 1, 0)
         mm1(4, 0)
@@ -304,14 +304,13 @@ def tile_list_pair_spread_positions_kernel(
         root4 = right[1][:, 0, :].rearrange("p (t c) -> p t c", t=4)
         nc.scalar.activation(root4, mag4, ACT.Abs_reciprocal_sqrt, bias=c4, scale=c4)
         magnitude(mag5[:], legs[2][:, 1, :])
-        square(right[0][:, :, 3 * CH : NP])
-        inv_root(5, mag5[:])
         magnitude(mag67[:], legs[3][:])
-        square(right[1][:, 0:2, :])
+        inv_root(5, mag5[:])
         inv_root(6, mag67[:, 0, :])
         inv_root(7, mag67[:, 1, :])
-        for cols in (slice(0, HALF), slice(HALF, NP)):
-            square(right[1][:, 2:4, cols])
+        square(right[0][:, :, 3 * CH : NP])
+        for c in range(4):
+            square(right[1][:, :, CH * c : CH * (c + 1)])
         for u in range(4, 8):
             first_leg(u, left[1][:, u - 4, :])
 

@@ -243,11 +243,12 @@ def tile_list_pair_spread_positions_kernel(
         wide_tile(1, 1, "late")
         cast("pool", 0, 1, 512, 0, 64)
         cast("pool", 0, 1, 512, 64, 64)
+        cast("pool", 1, 1, 512, 0, 32)
         for u in range(1, 4):
             evac(u)
         for u in range(4):
             second_leg(u)
-        cast("dve", 1, 1, 512, 0, 128)
+        cast("dve", 1, 1, 512, 32, 96)
         shrink = sb("shrink", [P, 8], F32, "raw0_0")
         nc.vector.reciprocal(shrink[:], floored[:])
         quant_w(0, 1, 0, "first")
@@ -280,17 +281,11 @@ def tile_list_pair_spread_positions_kernel(
         magnitude(mag23[:], legs[1][:])
         for u in range(4):
             inv_root(u, (mag01, mag23)[u // 2][:, u % 2, :])
-        square(right[0][:, :, 0:CH])
-        square(right[0][:, :, CH : 3 * CH])
+        cols = slice(0, 3 * CH)
+        woven = sb("woven", [P, 3 * CH, 4], F32)
+        nc.scalar.activation(woven[:], right[0][:, :, cols].rearrange("p t j -> p j t"), ACT.Square)
         zpool = sb("zpool", [P, 3 * CH, 4], BF16)
-        for c in range(3):
-            cols = slice(CH * c, CH * (c + 1))
-            nc.gpsimd.tensor_tensor(
-                zpool[:, cols, :].rearrange("p (c i) t -> p c t i", i=2),
-                left[0][:, :, cols].rearrange("p t (c i) -> p c t i", i=2),
-                right[0][:, :, cols].rearrange("p t (c i) -> p c t i", i=2),
-                ALU.mult,
-            )
+        nc.gpsimd.tensor_tensor(zpool[:], left[0][:, :, cols].rearrange("p t j -> p j t"), woven[:], ALU.mult)
         mag4 = left[1][:, :, 0:CH]
         mag5 = sb("mag5", [P, NP], F32, "mag01")
         mag67 = pair_tile("mag67", "mag23")

@@ -275,7 +275,6 @@ def tile_list_pair_spread_positions_kernel(
 
         right[0] = sb("right0", [P, 4, NP], F32)
         right[1] = sb("right1", [P, 4, NP], F32)
-        left[1] = sb("left1", [P, 4, NP], F32)
         mag01, mag23 = pair_tile("mag01", "third"), pair_tile("mag23")
         magnitude(mag01[:], legs[0][:])
         magnitude(mag23[:], legs[1][:])
@@ -286,24 +285,17 @@ def tile_list_pair_spread_positions_kernel(
         nc.scalar.activation(woven[:], right[0][:, :, cols].rearrange("p t j -> p j t"), ACT.Square)
         zpool = sb("zpool", [P, 3 * CH, 4], BF16)
         nc.gpsimd.tensor_tensor(zpool[:], left[0][:, :, cols].rearrange("p t j -> p j t"), woven[:], ALU.mult)
-        mag4 = left[1][:, :, 0:CH]
-        mag5 = sb("mag5", [P, NP], F32, "mag01")
-        mag67 = pair_tile("mag67", "mag23")
-        for u in range(4, 7):
+        for u in range(4, 8):
             evac(u)
             second_leg(u)
-        magnitude(mag4, legs[2][:, 0, :].rearrange("p (t c) -> p t c", t=4))
-        evac(7)
-        second_leg(7)
-        c4 = shrink[:, 4:5]
-        root4 = right[1][:, 0, :].rearrange("p (t c) -> p t c", t=4)
-        nc.scalar.activation(root4, mag4, ACT.Abs_reciprocal_sqrt, bias=c4, scale=c4)
-        magnitude(mag5[:], legs[2][:, 1, :])
+        rest = sb("rest", [P, 4, CH], F32)
+        nc.scalar.activation(rest[:], right[0][:, :, 3 * CH : NP], ACT.Square)
+        left[1] = sb("left1", [P, 4, NP], F32, "right0")
+        mag45, mag67 = pair_tile("mag45", "mag01"), pair_tile("mag67", "mag23")
+        magnitude(mag45[:], legs[2][:])
         magnitude(mag67[:], legs[3][:])
-        inv_root(5, mag5[:])
-        inv_root(6, mag67[:, 0, :])
-        inv_root(7, mag67[:, 1, :])
-        square(right[0][:, :, 3 * CH : NP])
+        for u in range(4, 8):
+            inv_root(u, (mag45, mag67)[u // 6][:, u % 2, :])
         for c in range(4):
             square(right[1][:, :, CH * c : CH * (c + 1)])
         for u in range(4, 8):
@@ -316,11 +308,12 @@ def tile_list_pair_spread_positions_kernel(
 
         def make_z(b, first, count, over="", at=0):
             cols = slice(CH * first, CH * (first + count))
+            factor = rest[:] if b == 0 else right[1][:, :, cols]
             tile = sb("zb%d_%d" % (b, first), [P, count * CH, 4], BF16, over, at)
             nc.vector.tensor_tensor(
                 tile[:].rearrange("p (c i) t -> p c t i", i=2),
                 left[b][:, :, cols].rearrange("p t (c i) -> p c t i", i=2),
-                right[b][:, :, cols].rearrange("p t (c i) -> p c t i", i=2),
+                factor.rearrange("p t (c i) -> p c t i", i=2),
                 ALU.mult,
             )
             for c in range(count):

from contextlib import ExitStack

import concourse.mybir as mybir

K, T, S, NP, H, N = 1024, 2048, 1024, 512, 1024, 512
FLOPS = 2 * K * H * S + 2 * H * N * NP

F32 = mybir.dt.float32
BF16 = mybir.dt.bfloat16
I32 = mybir.dt.int32
U32 = mybir.dt.uint32
U16 = mybir.dt.uint16
U8 = mybir.dt.uint8
FP8X4 = mybir.dt.float8_e4m3fn_x4
FP4X4 = mybir.dt.float4_e2m1fn_x4
ACT = mybir.ActivationFunctionType
ALU = mybir.AluOpType
WIDTH = {F32: 4, I32: 4, U32: 4, BF16: 2, U8: 1}

P = 128
CH = 128
HALF = 256
WINDOWS = 6
FLOOR = 2.0**-100


def tile_list_pair_spread_positions_kernel(
    tc, tab_words, tab_scales, offs, pos1, pos2, w1, gain, w2_words, w2_scales, out
):
    nc = tc.nc
    with ExitStack() as ctx:
        lists = ctx.enter_context(tc.tile_pool(name="lists", bufs=1))
        keep = ctx.enter_context(tc.tile_pool(name="keep", bufs=1))
        psum = ctx.enter_context(tc.psum_pool(name="psum", bufs=1))
        where = {"end": 0}

        def sb(name, shape, dtype, over="", at=0):
            if over:
                where[name] = where[over] + at
            else:
                size = WIDTH[dtype]
                for extent in shape[1:]:
                    size = size * extent
                where[name] = where["end"]
                where["end"] = where["end"] + (size + 63) // 64 * 64
            return keep.tile(shape, dtype, name=name, tag=name, align_bytes=64, offset=where[name])

        def room(name, size):
            where[name] = where["end"]
            where["end"] = where["end"] + size

        def bank(i):
            return psum.tile([P, 512], F32, name="bank%d" % i)

        offs_t = lists.tile([P, S // 16], U16, name="offs_t")
        pos1_t = lists.tile([P, NP // 16], U16, name="pos1_t")
        pos2_t = lists.tile([P, NP // 16], U16, name="pos2_t")

        room("first", 4 * 4 * 512)
        rows = sb("rows", [P, T // 4], I32, "first")
        planes = sb("planes", [P, 2 * S // 4], I32)
        h = [sb("h%d" % i, [P, 2 * S], F32) for i in range(4)]
        one = sb("one", [P, 1], F32)
        warm = sb("warm", [P, 1], F32)

        nc.vector.memset(one[:], 1.0)
        nc.gpsimd.memset(rows[32:64, :], 0)
        nc.gpsimd.memset(rows[64:128, :], 0)
        nc.vector.memset(planes[:], 0)
        nc.scalar.activation(warm[:], one[:, 0:1], ACT.Abs_reciprocal_sqrt, bias=1.0)
        for i in range(4):
            nc.gpsimd.memset(h[i][:, S : 2 * S], 0.0)

        tabw, raw = {}, {}

        def load_tab(a, over="", at=0):
            tabw[a] = sb("tabw%d" % a, [P, T], I32, over, at)
            nc.sync.dma_start(tabw[a][:], tab_words[a].rearrange("p t i -> p (t i)").bitcast(I32))

        def load_w1(a, first, width, over="", into=None):
            if into is None:
                raw[a, first] = sb("raw%d_%d" % (a, first), [P, 4, width], F32, over)[:]
            else:
                raw[a, first] = into.rearrange("p (j c) -> p j c", j=4)
            src = w1[512 * a : 512 * (a + 1), first : first + width]
            nc.sync.dma_start(raw[a, first], src.rearrange("(p j) c -> p j c", j=4))

        nc.sync.dma_start(offs_t[:], offs)
        nc.sync.dma_start(rows[0:32, :], tab_scales.rearrange("a q t -> (a q) t").bitcast(I32))
        room("pair", 2 * 8192)
        load_tab(0, "pair", 4096)
        sign = sb("sign", [P, 8], F32)
        amount = sb("amount", [P, 8], F32)
        floored = sb("floored", [P, 8], F32)
        load_w1(0, 0, 512)
        nc.sync.dma_start(pos2_t[:], pos2)
        nc.sync.dma_start(pos1_t[:], pos1)

        picked = sb("picked", [P, S // 4], I32)
        vw = [sb("vw%d" % a, [P, S], U32) for a in range(2)]
        nc.vector.tensor_copy(picked[:].bitcast(U8), rows[:].bitcast(U8).indirect(offs_t[:]))
        nc.vector.tensor_copy(vw[0][:], tabw[0][:].bitcast(U32).indirect(offs_t[:]))

        def place_rows(a):
            for q in range(4):
                nc.sync.dma_start(
                    planes[32 * q : 32 * q + 4, S // 4 * a : S // 4 * (a + 1)],
                    picked[16 * a + 4 * q : 16 * a + 4 * q + 4, :],
                )

        vs = planes[:].bitcast(U8)
        place_rows(0)
        load_tab(1, "first")
        place_rows(1)
        for i in range(2):
            h.append(sb("h%d" % (4 + i), [P, 2 * S], F32, "pair", 8192 * i))
            load_w1(1, HALF * i, HALF, into=h[4 + i][:, S : 2 * S])
        g = h[5][:, 0:8]
        nc.sync.dma_start(g.rearrange("p (b t) -> p b t", b=2), gain.rearrange("(b p t) -> p b t", b=2, t=4))
        load_w1(0, 512, 512, "raw0_0")

        wide, wc, ws = {}, {}, {}

        def cast(engine, a, b, base, first, count, slots=slice(0, 4)):
            dst = wide[a, b][:, slots, first : first + count, :]
            lo = 512 * b + 4 * first - base
            src = raw[a, base][:, :, lo : lo + 4 * count].rearrange("p j (m t) -> p j m t", t=4)[:, :, :, slots]
            if engine == "pool":
                dst = dst.rearrange("p t m j -> p m t j")
                src = src.rearrange("p j m t -> p m t j")
                nc.gpsimd.tensor_scalar(dst, src, 1.0, 0.0, ALU.mult, ALU.add)
                return
            dst = dst.rearrange("p t m j -> p m j t")
            src = src.rearrange("p j m t -> p m j t")
            if engine == "act":
                nc.scalar.copy(dst, src)
            else:
                nc.vector.tensor_copy(dst, src)

        def wide_tile(a, b, over=""):
            wide[a, b] = sb("wide%d%d" % (a, b), [P, 4, P, 4], BF16, over)

        def quant_w(a, b, t0, over="", at=0, count=2):
            codes = sb("wc%d%d%d" % (a, b, t0), [P, count * P], U32, over, at)
            scales = sb("ws%d%d%d" % (a, b, t0), [P, count * P], U8)
            nc.vector.quantize_mx(
                out=codes[:].bitcast(FP8X4),
                scales=scales[:],
                in_=wide[a, b][:, t0 : t0 + count].rearrange("p t m j -> p (t m j)"),
            )
            for t in range(count):
                wc[a, b, t0 + t] = codes[:, P * t : P * (t + 1)]
                ws[a, b, t0 + t] = scales[:, P * t : P * (t + 1)]

        hps = {}

        def mm1(u, a):
            b, t = divmod(u, 4)
            for half in range(2):
                if a == 0:
                    hps[u, half] = bank(2 * t + half)
                nc.tensor.matmul_mx(
                    out=hps[u, half][:],
                    lhsT=wc[a, b, t].bitcast(FP8X4),
                    lhsT_scale=ws[a, b, t],
                    rhs=vw[a][:, 512 * half : 512 * (half + 1)].bitcast(FP8X4),
                    rhs_scale=vs[:, S * a + 512 * half : S * a + 512 * (half + 1)],
                    start=(a == 0),
                    stop=(a == 1),
                )

        def evac(u, shared=False):
            for half in range(2):
                dst = h[u % WINDOWS][:, 512 * half : 512 * (half + 1)]
                if shared and half == 0:
                    nc.vector.tensor_scalar(dst, hps[u, half][:], sign[:, u : u + 1], None, ALU.mult)
                else:
                    nc.scalar.activation(dst, hps[u, half][:], ACT.Copy, scale=sign[:, u : u + 1])

        legs = {0: sb("legs0", [P, 2, NP], F32), 1: sb("legs1", [P, 2, NP], F32)}
        legs[2] = sb("legs2", [P, 2, NP], F32)
        legs[3] = sb("legs3", [P, 2, NP], F32)
        left, right = {}, {}

        def second_leg(u):
            nc.vector.tensor_scalar(
                legs[u // 2][:, u % 2, :], h[u % WINDOWS][:].indirect(pos2_t[:]), -1.5, 0.0, ALU.mult, ALU.add
            )

        def first_leg(u, dst):
            nc.vector.tensor_tensor(dst, h[u % WINDOWS][:].indirect(pos1_t[:]), legs[u // 2][:, u % 2, :], ALU.add)

        def magnitude(dst, src):
            nc.scalar.activation(dst, src, ACT.Abs, scale=1.0 / 1.5)

        def inv_root(u, src):
            c = shrink[:, u : u + 1]
            nc.scalar.activation(right[u // 4][:, u % 4, :], src, ACT.Abs_reciprocal_sqrt, bias=c, scale=c)

        def square(dst):
            nc.scalar.activation(dst, dst, ACT.Square)

        def pair_tile(name, over="", at=0):
            return sb(name, [P, 2, NP], F32, over, at)

        wide_tile(0, 0)
        low, high = slice(0, 2), slice(2, 4)
        cast("dve", 0, 0, 0, 0, 128, low)
        cast("act", 0, 0, 0, 0, 128, high)
        quant_w(0, 0, 0)
        mm1(0, 0)
        mm1(1, 0)
        quant_w(0, 0, 2)
        mm1(2, 0)
        mm1(3, 0)
        nc.vector.tensor_copy(vw[1][:], tabw[1][:].bitcast(U32).indirect(offs_t[:]))
        load_w1(1, 512, 512, "first")
        wide_tile(1, 0)
        cast("act", 1, 0, 0, 0, 64, low)
        cast("act", 1, 0, 0, 0, 64, high)
        cast("dve", 1, 0, HALF, 64, 64, low)
        cast("act", 1, 0, HALF, 64, 64, high)
        quant_w(1, 0, 0, count=1)
        mm1(0, 1)
        quant_w(1, 0, 1, count=1)
        mm1(1, 1)
        room("third", 4096)
        quant_w(1, 0, 2, "third")
        nc.scalar.activation(sign[:], g, ACT.Sign)
        nc.scalar.activation(amount[:], g, ACT.Abs)
        evac(0, shared=True)
        nc.scalar.activation(floored[:], amount[:], ACT.Identity, bias=FLOOR)
        mm1(2, 1)
        mm1(3, 1)

        w2w = sb("w2w", [P, 2, N // 2], I32, "wide10", 1024)
        nc.sync.dma_start(w2w[:], w2_words.rearrange("a p c -> p a c").bitcast(I32))
        w2c = w2w[:].rearrange("p a c -> p (a c)").bitcast(U8)
        w2s = planes[:, 0 : N // 2].rearrange("p (a c) -> p a c", a=2)

        wide_tile(0, 1)
        room("late", 8192)
        wide_tile(1, 1, "late")
        cast("pool", 0, 1, 512, 0, 64)
        cast("pool", 0, 1, 512, 64, 64)
        cast("pool", 1, 1, 512, 0, 32)
        for u in range(1, 4):
            evac(u)
        for u in range(4):
            second_leg(u)
        cast("dve", 1, 1, 512, 32, 96)
        shrink = sb("shrink", [P, 8], F32, "raw0_0")
        nc.vector.reciprocal(shrink[:], floored[:])
        quant_w(0, 1, 0, "first")
        quant_w(1, 1, 0)
        mm1(4, 0)
        mm1(4, 1)
        mm1(5, 0)
        mm1(5, 1)
        quant_w(0, 1, 2, "first", 1024)
        quant_w(1, 1, 2)
        mm1(6, 0)
        mm1(6, 1)
        mm1(7, 0)
        mm1(7, 1)
        for q in range(4):
            nc.sync.dma_start(
                w2s[32 * q : 32 * q + 4, :, :],
                w2_scales[:, 4 * q : 4 * q + 4, :].rearrange("a r n -> r a n").bitcast(I32),
            )
        w2sb = vs[:, 0 : 2 * N]
        left[0] = sb("left0", [P, 4, NP], F32, "late")
        for u in range(4):
            first_leg(u, left[0][:, u, :])

        right[0] = sb("right0", [P, 4, NP], F32)
        right[1] = sb("right1", [P, 4, NP], F32)
        mag01, mag23 = pair_tile("mag01", "third"), pair_tile("mag23")
        magnitude(mag01[:], legs[0][:])
        magnitude(mag23[:], legs[1][:])
        for u in range(4):
            inv_root(u, (mag01, mag23)[u // 2][:, u % 2, :])
        cols = slice(0, 3 * CH)
        woven = sb("woven", [P, 3 * CH, 4], F32)
        nc.scalar.activation(woven[:], right[0][:, :, cols].rearrange("p t j -> p j t"), ACT.Square)
        zpool = sb("zpool", [P, 3 * CH, 4], BF16)
        nc.gpsimd.tensor_tensor(zpool[:], left[0][:, :, cols].rearrange("p t j -> p j t"), woven[:], ALU.mult)
        for u in range(4, 8):
            evac(u)
            second_leg(u)
        rest = sb("rest", [P, 4, CH], F32)
        nc.scalar.activation(rest[:], right[0][:, :, 3 * CH : NP], ACT.Square)
        left[1] = sb("left1", [P, 4, NP], F32, "right0")
        mag45, mag67 = pair_tile("mag45", "mag01"), pair_tile("mag67", "mag23")
        magnitude(mag45[:], legs[2][:])
        magnitude(mag67[:], legs[3][:])
        for u in range(4, 8):
            inv_root(u, (mag45, mag67)[u // 6][:, u % 2, :])
        for c in range(4):
            square(right[1][:, :, CH * c : CH * (c + 1)])
        for u in range(4, 8):
            first_leg(u, left[1][:, u - 4, :])

        zb, zc, zs = {}, {}, {}

        def chunk(c):
            return slice(CH * c, CH * (c + 1))

        def make_z(b, first, count, over="", at=0):
            cols = slice(CH * first, CH * (first + count))
            factor = rest[:] if b == 0 else right[1][:, :, cols]
            tile = sb("zb%d_%d" % (b, first), [P, count * CH, 4], BF16, over, at)
            nc.vector.tensor_tensor(
                tile[:].rearrange("p (c i) t -> p c t i", i=2),
                left[b][:, :, cols].rearrange("p t (c i) -> p c t i", i=2),
                factor.rearrange("p t (c i) -> p c t i", i=2),
                ALU.mult,
            )
            for c in range(count):
                zb[b, first + c] = tile[:, chunk(c), :]

        def quant_z(b, c, over="", at=0):
            zc[b, c] = sb("zc%d_%d" % (b, c), [P, CH], U32, over, at)
            zs[b, c] = sb("zs%d_%d" % (b, c), [P, CH], U8)
            nc.vector.quantize_mx(
                out=zc[b, c][:].bitcast(FP8X4), scales=zs[b, c][:], in_=zb[b, c].rearrange("p c t -> p (c t)")
            )

        acc = {}

        def mm2(c, b):
            last = c == 3
            for nt in range(4):
                head = nt - nt % 2 if last else 0
                tail = head + 1 if last else 3
                if b == 0 and nt == head:
                    acc[c, nt] = bank(c + nt // 2)
                nc.tensor.matmul_mx(
                    out=acc[c, head][:, CH * (nt - head) : CH * (nt - head + 1)],
                    lhsT=w2c[:, 2 * N * b + 2 * P * nt : 2 * N * b + 2 * P * (nt + 1)].bitcast(FP4X4),
                    lhsT_scale=w2sb[:, N * b + P * nt : N * b + P * (nt + 1)],
                    rhs=zc[b, c][:].bitcast(FP8X4),
                    rhs_scale=zs[b, c][:],
                    start=(b == 0 and nt == head),
                    stop=(b == 1 and nt == tail),
                )

        out_v = out.rearrange("(nt p) j -> p nt j", p=P)

        def finish(c):
            res = sb("res%d" % c, [P, 4, CH], F32)
            if c < 3:
                nc.scalar.activation(res[:].rearrange("p n j -> p (n j)"), acc[c, 0][:], ACT.Tanh)
                nc.sync.dma_start(out_v[:, :, chunk(c)], res[:])
            else:
                for nt in (0, 2):
                    pair = res[:, nt : nt + 2, :]
                    nc.scalar.activation(pair.rearrange("p n j -> p (n j)"), acc[c, nt][:, 0 : 2 * CH], ACT.Tanh)
                    nc.sync.dma_start(out_v[:, nt : nt + 2, chunk(c)], pair)

        def open_chunk(c, over="", at=0):
            quant_z(0, c, over, at)
            mm2(c, 0)

        def close_chunk(c):
            quant_z(1, c)
            mm2(c, 1)
            finish(c)

        for c in range(3):
            zb[0, c] = zpool[:, chunk(c), :]
            open_chunk(c, "legs3", 512 * c)
        make_z(1, 0, 1)
        make_z(1, 1, 1)
        close_chunk(0)
        make_z(1, 2, 1)
        close_chunk(1)
        make_z(0, 3, 1, "zb1_0")
        close_chunk(2)
        make_z(1, 3, 1, "zb1_1")
        open_chunk(3)
        close_chunk(3)
